import numpy as np
import ml_dtypes


def mxq(x, axis, fmt="e4m3"):
    dtype, down = {"e4m3": (ml_dtypes.float8_e4m3fn, 7), "e5m2": (ml_dtypes.float8_e5m2, 14)}[fmt]
    v = np.moveaxis(np.asarray(x, np.float32).astype(ml_dtypes.bfloat16).astype(np.float64), axis, -1)
    blocks = v.reshape(v.shape[:-1] + (-1, 32))
    amax = np.abs(blocks).max(-1, keepdims=True)
    byte = np.maximum(np.where(amax > 0, np.frexp(amax)[1] - 1 + 127, 0) - down, 1)
    scale = np.exp2(byte - 127.0)
    codes = (blocks / scale).astype(np.float32).astype(dtype).astype(np.float64)
    return np.moveaxis((codes * scale).reshape(v.shape), -1, axis)


WIDE = False


def mx_kscale(k):
    if not WIDE:
        return np.ones(k)
    levels = np.array([24, -24, 12, -12, 0])
    if k % 512:
        return np.exp2(np.random.permutation(np.resize(levels, k // 32))).repeat(32)
    a = np.empty((k // 512, 16))
    for p in range(k // 512):
        a[p, :8] = np.random.permutation(np.resize(levels, 8))
        for g in range(8):
            far = levels[np.abs(levels - a[p, g]) >= 10]
            a[p, g + 8] = far[np.random.randint(len(far))]
    return np.exp2(a.ravel()).repeat(32)


def f64(x):
    return np.asarray(x).astype(np.float64)


def striped(idx):
    return np.tile(idx.reshape(-1, 16).T, (8, 1)).astype(np.uint16)


def unstriped(offs):
    return offs[:16].T.reshape(-1).astype(np.int64)


E2M1 = np.array([0.0, 0.5, 1.0, 1.5, 2.0, 3.0, 4.0, 6.0, -0.0, -0.5, -1.0, -1.5, -2.0, -3.0, -4.0, -6.0])


def pack_weight(w, fmt):
    k, n = w.shape
    w = f64(np.asarray(w, np.float32).astype(ml_dtypes.bfloat16)).reshape(k // 32, 32, n)
    amax = np.abs(w).max(1)
    if fmt == "e4m3":
        byte = np.frexp(amax)[1] - 1 + 127 - 7
    else:
        mant, ex = np.frexp(amax / 6.0)
        byte = np.where(mant > 0.5, ex, ex - 1) + 127
    byte = np.clip(np.where(amax > 0, byte, 1), 1, 254)
    scaled = (w * np.exp2(127.0 - byte)[:, None, :]).reshape(k, n).astype(np.float32)
    by_word = np.ascontiguousarray(scaled.reshape(k // 512, 128, 4, n).transpose(0, 1, 3, 2))
    if fmt == "e4m3":
        words = by_word.astype(ml_dtypes.float8_e4m3fn).view(np.uint8)
    else:
        c = by_word.astype(ml_dtypes.float4_e2m1fn).view(np.uint8) & 0xF
        words = (c[..., 0::2] | (c[..., 1::2] << 4)).reshape(k // 512, 128, 2 * n)
    return np.ascontiguousarray(words), np.ascontiguousarray(byte.astype(np.uint8).reshape(k // 512, 16, n))


def unpack_weight(words, scales, fmt):
    g, _, n = scales.shape
    words = np.ascontiguousarray(words).reshape(g, 128, n, -1)
    if fmt == "e4m3":
        vals = words.view(ml_dtypes.float8_e4m3fn).astype(np.float64)
    else:
        nib = np.empty((g, 128, n, 4), np.uint8)
        nib[..., 0::2] = words & 0xF
        nib[..., 1::2] = words >> 4
        vals = E2M1[nib]
    vals = vals * np.repeat(np.exp2(scales.astype(np.float64) - 127.0), 8, axis=1)[..., None]
    return vals.transpose(0, 1, 3, 2).reshape(g * 512, n)


def pack_table4(v):
    words, scales = pack_weight(v, "e2m1")
    g, t = words.shape[0] // 2, v.shape[1]
    return np.ascontiguousarray(words.reshape(g, 2, 128, t, 2).transpose(0, 2, 3, 1, 4).reshape(g, 128, t, 4)), scales


def unpack_table4(words, scales):
    g, _, t, _ = words.shape
    return unpack_weight(words.reshape(g, 128, t, 2, 2).transpose(0, 3, 1, 2, 4).reshape(2 * g, 128, 2 * t), scales, "e2m1")


def silu(f):
    return f / (1.0 + np.exp(-np.maximum(f, -700.0)))


K, R, N, T, J = 1024, 1024, 256, 4096, 1024


def setup_inputs():
    n = np.random.standard_normal
    s = mx_kscale(K)[:, None]
    u = mx_kscale(R)[:, None]
    wd = n((R, N)) / np.sqrt(R) / u
    wd4 = pack_weight(wd, "e2m1")
    wdrest = wd - unpack_weight(*wd4, "e2m1")
    p_tab = pack_table4(n((K, T)) * s)
    p_wu = pack_weight(n((K, R)) / np.sqrt(K) / s * u.T, "e4m3")
    p_wd8 = pack_weight(wdrest, "e4m3")
    return {
        "tab_words": p_tab[0],
        "tab_scales": p_tab[1],
        "wg": (n((K, R)) / np.sqrt(K) / s).astype(np.float32),
        "wu_words": p_wu[0],
        "wu_scales": p_wu[1],
        "wd4_words": wd4[0],
        "wd4_scales": wd4[1],
        "wd8_words": p_wd8[0],
        "wd8_scales": p_wd8[1],
        "rT": (n((N, T))).astype(np.float32),
        "offs": striped(np.random.permutation(T)[:J]),
    }


def reference(tab_words, tab_scales, wg, wu_words, wu_scales, wd4_words, wd4_scales, wd8_words, wd8_scales, rT, offs):
    idx = unstriped(offs)
    tab_ = unpack_table4(tab_words, tab_scales)[:, idx]
    wg_ = mxq(f64(wg), 0, "e4m3")
    wu_ = unpack_weight(wu_words, wu_scales, "e4m3")
    ga = wg_.T @ tab_
    ub = wu_.T @ tab_
    h = silu(ga) * ub
    h_ = mxq(h, 0, "e4m3")
    wd4_ = unpack_weight(wd4_words, wd4_scales, "e2m1")
    wd8_ = unpack_weight(wd8_words, wd8_scales, "e4m3")
    y = wd4_.T @ h_ + wd8_.T @ h_
    return y + f64(rT)[:, idx]

@@ -1,0 +1,310 @@
+from contextlib import ExitStack
+
+import concourse.mybir as mybir
+
+K, R, N, T, J = 1024, 1024, 256, 4096, 1024
+FLOPS = 2 * (2 * K * R * J + 2 * R * N * J)
+
+F32 = mybir.dt.float32
+BF16 = mybir.dt.bfloat16
+I32 = mybir.dt.int32
+U32 = mybir.dt.uint32
+U16 = mybir.dt.uint16
+U8 = mybir.dt.uint8
+FP8X4 = mybir.dt.float8_e4m3fn_x4
+FP4X4 = mybir.dt.float4_e2m1fn_x4
+SILU = mybir.ActivationFunctionType.Silu
+MULT = mybir.AluOpType.mult
+ADD = mybir.AluOpType.add
+
+P = 128
+PACK = 4
+PASS = P * PACK
+CH = 128
+CHUNKS = J // CH
+HALF = J // 2
+
+
+def tile_list_gmlpt_silu_res_resL_kernel(
+    tc, tab_words, tab_scales, wg, wu_words, wu_scales, wd4_words, wd4_scales, wd8_words, wd8_scales, rT, offs, out
+):
+    nc = tc.nc
+    with ExitStack() as ctx:
+        keep = ctx.enter_context(tc.tile_pool(name="keep", bufs=1))
+        psum = ctx.enter_context(tc.psum_pool(name="psum", bufs=1))
+
+        def held(name, shape, dtype, tag=""):
+            return keep.tile(shape, dtype, name=name, tag=tag or name, align_bytes=64)
+
+        offsets = keep.tile([P, J // 16], U16, name="offsets")
+        table = held("table", [P, T], I32)
+        table_planes = held("table_planes", [P, T], U8)
+        picked_planes = held("picked_planes", [P, J], U8)
+        picked_plane1 = held("picked_plane1", [P, J], U8)
+        wu_planes_raw = held("wu_planes_raw", [P, 2, R], U8, "late_pairs")
+        wu_planes = held("wu_planes", [P, 2, R], U8)
+        wd4_planes = held("wd4_planes", [P, 2, N], U8)
+        wd8_planes = held("wd8_planes", [P, 2, N], U8)
+        wd4 = held("wd4", [P, 2, 2 * N], U8)
+        wd8 = held("wd8", [P, 2, N], I32)
+        resid = [held(f"resid{n}", [P, T], F32) for n in range(2)]
+        wu_raw = {(b, a): held(f"wu_raw{b}{a}", [P, PASS], I32) for b in range(2) for a in range(2)}
+        wu = {(b, a): held(f"wu{b}{a}", [P, PASS], U32) for b in range(2) for a in range(2)}
+        wg_raw = {(b, a): held(f"wg_raw{b}{a}", [P, PACK, PASS], F32) for b in range(2) for a in range(2)}
+        warm = held("warm", [P, 2], F32)
+        banks = [psum.tile([P, PACK * CH], F32, name=f"bank{i}") for i in range(8)]
+
+        plane_words = table_planes[:].bitcast(I32)
+        nc.vector.memset(plane_words[:, 0:640], 0)
+        nc.gpsimd.memset(plane_words[:, 640:1024], 0)
+        nc.vector.memset(warm[:, 0:1], 0.0)
+        nc.scalar.activation(warm[:, 1:2], warm[:, 0:1], SILU)
+        nc.gpsimd.memset(wu_planes_raw[:].rearrange("p a r -> p (a r)").bitcast(I32), 0)
+        nc.gpsimd.memset(picked_plane1[:].bitcast(I32), 0)
+        nc.gpsimd.memset(wd4_planes[:].rearrange("p a n -> p (a n)").bitcast(I32), 0)
+        nc.gpsimd.memset(wd8_planes[:].rearrange("p a n -> p (a n)").bitcast(I32), 0)
+
+        def load_wu(b, a):
+            src = wu_words[a].rearrange("p r i -> p (r i)")[:, 4 * PASS * b : 4 * PASS * (b + 1)]
+            nc.sync.dma_start(wu_raw[b, a][:], src.bitcast(I32))
+
+        def load_wg(b, a):
+            src = wg[PASS * a : PASS * (a + 1), PASS * b : PASS * (b + 1)]
+            nc.sync.dma_start(wg_raw[b, a][:], src.rearrange("(p i) c -> p i c", i=PACK))
+
+        def load_planes(queue, planes, scales, q):
+            queue.dma_start(
+                planes[32 * q : 32 * q + 4, :, :].bitcast(I32),
+                scales[:, 4 * q : 4 * q + 4, :].rearrange("a q n -> q a n").bitcast(I32),
+            )
+
+        nc.sync.dma_start(offsets[:], offs)
+        load_wu(0, 0)
+        for q in range(4):
+            nc.sync.dma_start(plane_words[32 * q : 32 * q + 8, :], tab_scales[:, 4 * q : 4 * q + 4, :].bitcast(I32))
+        nc.sync.dma_start(table[:], tab_words[0].rearrange("p t e -> p (t e)").bitcast(I32))
+        for q in range(4):
+            load_planes(nc.sync, wu_planes_raw, wu_scales, q)
+        load_wu(0, 1)
+        nc.vector.tensor_copy(picked_planes[:], table_planes[:].indirect(offsets[:]))
+        nc.sync.dma_start(picked_plane1[0:100, :].bitcast(I32), picked_planes[4:104, :].bitcast(I32))
+        load_wg(0, 0)
+        load_wg(0, 1)
+        load_wg(1, 0)
+        load_wu(1, 0)
+        load_wu(1, 1)
+        load_wg(1, 1)
+        nc.sync.dma_start(resid[0][:], rT[0:P, :])
+        nc.sync.dma_start(wd4[:].bitcast(I32), wd4_words.rearrange("a p w -> p a w").bitcast(I32))
+        nc.sync.dma_start(wd8[:], wd8_words.rearrange("a p n i -> p a (n i)").bitcast(I32))
+        nc.sync.dma_start(resid[1][:], rT[P : 2 * P, :])
+        for q in range(4):
+            load_planes(nc.gpsimd, wd4_planes, wd4_scales, q)
+            load_planes(nc.gpsimd, wd8_planes, wd8_scales, q)
+
+        picked_plane = [picked_planes, picked_plane1]
+
+        def order_wu_planes(a, b0, b1):
+            cols = slice(PASS * b0, PASS * b1)
+            nc.vector.tensor_copy(
+                wu_planes[:, a, cols].rearrange("p (b t m) -> p b m t", t=PACK, m=P),
+                wu_planes_raw[:, a, cols].rearrange("p (b m t) -> p b m t", t=PACK, m=P),
+            )
+
+        def order_wu(b, a):
+            nc.vector.tensor_copy(
+                wu[b, a][:].rearrange("p (t m) -> p m t", t=PACK),
+                wu_raw[b, a][:].bitcast(U32).rearrange("p (m t) -> p m t", t=PACK),
+            )
+
+        pairs, picked = {}, {}
+
+        def pick_words(half):
+            pairs[half] = held(f"pairs{half}", [P, HALF], U32, "late_pairs" if half else "")
+            cols = slice(half * HALF // 16, (half + 1) * HALF // 16)
+            nc.vector.tensor_copy(pairs[half][:], table[:].bitcast(U32).indirect(offsets[:, cols]))
+
+        def part_words(half, a):
+            picked[half, a] = held(f"picked{half}{a}", [P, HALF], U16)
+            both = pairs[half][:].bitcast(U16).rearrange("p (j a) -> p a j", a=2)
+            nc.vector.tensor_copy(picked[half, a][:], both[:, a, :])
+
+        wg_codes, wg_planes, wg_bf = {}, {}, {}
+
+        def round_wg(b, a, tp, on_vector):
+            rounded = held(f"wg_bf{b}{a}{tp}", [P, 2 * P * PACK], BF16)
+            dst = rounded[:].rearrange("p (t m i) -> p m i t", t=2, i=PACK)
+            src = wg_raw[b, a][:].rearrange("p i (m t) -> p m i t", t=PACK)[:, :, :, 2 * tp : 2 * tp + 2]
+            if on_vector:
+                nc.vector.tensor_copy(dst, src)
+            else:
+                nc.scalar.copy(dst, src)
+            wg_bf[b, a, tp] = rounded
+
+        def quantize_wg(b, a, tp):
+            codes = held(f"wg_codes{b}{a}{tp}", [P, 2 * P], U32)
+            plane = held(f"wg_plane{b}{a}{tp}", [P, 2 * P], U8)
+            nc.vector.quantize_mx(out=codes[:].bitcast(FP8X4), scales=plane[:], in_=wg_bf[b, a, tp][:])
+            wg_codes[b, a, tp], wg_planes[b, a, tp] = codes, plane
+
+        PER = HALF // CH
+
+        def up(b, c, a):
+            cols = slice(c % PER * CH, (c % PER + 1) * CH)
+            for t in range(PACK):
+                nc.tensor.matmul_mx(
+                    banks[c % PER][:, t * CH : (t + 1) * CH],
+                    lhsT=wu[b, a][:, t * P : (t + 1) * P].bitcast(FP8X4),
+                    lhsT_scale=wu_planes[:, a, PASS * b + t * P : PASS * b + (t + 1) * P],
+                    rhs=picked[c // PER, a][:, cols].bitcast(FP4X4),
+                    rhs_scale=picked_plane[a][:, c * CH : (c + 1) * CH],
+                    start=(a == 0 and t == 0),
+                    stop=(a == 1 and t == PACK - 1),
+                )
+
+        def gate(b, half, t, a):
+            cols = slice((t % 2) * P, (t % 2 + 1) * P)
+            nc.tensor.matmul_mx(
+                banks[PER + t][:],
+                lhsT=wg_codes[b, a, t // 2][:, cols].bitcast(FP8X4),
+                lhsT_scale=wg_planes[b, a, t // 2][:, cols],
+                rhs=picked[half, a][:].bitcast(FP4X4),
+                rhs_scale=picked_plane[a][:, half * HALF : (half + 1) * HALF],
+                start=(a == 0),
+                stop=(a == 1),
+            )
+
+        acts = {(b, half): held(f"act{b}{half}", [P, PACK, HALF], F32) for b in range(2) for half in range(2)}
+        h_bf, h_codes, h_planes = {}, {}, {}
+
+        def silu(b, half, t):
+            nc.scalar.activation(acts[b, half][:, t, :], banks[PER + t][:], SILU)
+
+        def product(b, c, dst):
+            cols = slice(c % PER * CH, (c % PER + 1) * CH)
+            nc.vector.tensor_tensor(
+                dst.rearrange("p (j e t) -> p j t e", e=2, t=PACK),
+                banks[c % PER][:].rearrange("p (t j e) -> p j t e", t=PACK, e=2),
+                acts[b, c // PER][:, :, cols].rearrange("p t (j e) -> p j t e", e=2),
+                MULT,
+            )
+
+        def quantize_h(b, c0, c1, src):
+            codes = held(f"h_codes{b}{c0}", [P, (c1 - c0) * CH], U32)
+            plane = held(f"h_plane{b}{c0}", [P, (c1 - c0) * CH], U8)
+            nc.vector.quantize_mx(out=codes[:].bitcast(FP8X4), scales=plane[:], in_=src)
+            h_codes[b, c0, c1], h_planes[b, c0, c1] = codes[:], plane[:]
+            for c in range(c0, c1):
+                cols = slice((c - c0) * CH, (c - c0 + 1) * CH)
+                h_codes[b, c, c + 1], h_planes[b, c, c + 1] = codes[:, cols], plane[:, cols]
+
+        def down(dst, n, b, c0, c1, start, stop):
+            cols = slice(n * P, (n + 1) * P)
+            tiers = (
+                (wd4[:, b, 2 * n * P : 2 * (n + 1) * P].bitcast(FP4X4), wd4_planes[:, b, cols]),
+                (wd8[:, b, cols].bitcast(FP8X4), wd8_planes[:, b, cols]),
+            )
+            for tier, (lhsT, lhsT_scale) in enumerate(tiers):
+                nc.tensor.matmul_mx(
+                    dst,
+                    lhsT=lhsT,
+                    lhsT_scale=lhsT_scale,
+                    rhs=h_codes[b, c0, c1].bitcast(FP8X4),
+                    rhs_scale=h_planes[b, c0, c1],
+                    start=(start and tier == 0),
+                    stop=(stop and tier == 1),
+                )
+
+        picked_resid = held("picked_resid", [P, 2, J], F32)
+        result = held("result", [P, 2, J], F32)
+        out_view = out.rearrange("(n p) j -> p n j", p=P)
+
+        def pick_resid(n):
+            nc.vector.tensor_copy(picked_resid[:, n, :], resid[n][:].indirect(offsets[:]))
+
+        def store(c0, c1):
+            nc.sync.dma_start(out_view[:, :, c0 * CH : c1 * CH], result[:, :, c0 * CH : c1 * CH])
+
+        def finish_first_half():
+            for n in range(2):
+                bank = banks[7 - n]
+                for b in range(2):
+                    down(bank[:], n, b, 0, PER, b == 0, b == 1)
+                nc.vector.tensor_tensor(result[:, n, 0:HALF], bank[:], picked_resid[:, n, 0:HALF], ADD)
+            store(0, PER)
+
+        def finish_chunk(c):
+            bank = banks[PER + (c + 1) % PER]
+            for b in range(2):
+                for n in range(2):
+                    down(bank[:, n * CH : (n + 1) * CH], n, b, c, c + 1, b == 0 and n == 0, b == 1 and n == 1)
+            cols = slice(c * CH, (c + 1) * CH)
+            sums = bank[:, 0 : 2 * CH].rearrange("p (n j) -> p n j", n=2)
+            nc.vector.tensor_tensor(result[:, :, cols], sums, picked_resid[:, :, cols], ADD)
+
+        def prepare_wg(b, a, on_vector):
+            round_wg(b, a, 1, on_vector)
+            round_wg(b, a, 0, False)
+            quantize_wg(b, a, 1)
+            quantize_wg(b, a, 0)
+
+        order_wu(0, 0)
+        pick_words(0)
+        for a in range(2):
+            part_words(0, a)
+            order_wu_planes(a, 0, 1)
+        order_wu(0, 1)
+        for a in range(2):
+            order_wu_planes(a, 1, 2)
+        slots = range(PACK - 1, -1, -1)
+        W = PACK * CH
+        for b in range(2):
+            for a in range(2):
+                for c in range(PER):
+                    up(b, c, a)
+            if b == 0:
+                pick_words(1)
+                part_words(1, 0)
+                part_words(1, 1)
+                prepare_wg(0, 0, False)
+                prepare_wg(0, 1, True)
+            for t in slots:
+                gate(b, 0, t, 0)
+            for t in slots:
+                gate(b, 0, t, 1)
+                silu(b, 0, t)
+            if b == 0:
+                prepare_wg(1, 0, False)
+            else:
+                quantize_h(0, 0, PER, h_bf[0, 0][:])
+                quantize_h(0, PER, CHUNKS, h_bf[0, 1][:])
+                pick_resid(0)
+            h_bf[b, 0] = held(f"h_bf{b}0", [P, PER * W], BF16, "resid0" if b else "")
+            for c in range(PER):
+                product(b, c, h_bf[b, 0][:, c * W : (c + 1) * W])
+                gate(b, 1, slots[c], 0)
+                gate(b, 1, slots[c], 1)
+                silu(b, 1, slots[c])
+            if b == 0:
+                order_wu(1, 0)
+                order_wu(1, 1)
+                prepare_wg(1, 1, False)
+            else:
+                quantize_h(1, 0, PER, h_bf[1, 0][:])
+                pick_resid(1)
+            h_bf[b, 1] = held(f"h_bf{b}1", [P, PER * W], BF16, "resid1" if b else "")
+            for c in range(PER, CHUNKS):
+                up(b, c, 0)
+                up(b, c, 1)
+                dst = h_bf[b, 1][:, (c - PER) * W : (c - PER + 1) * W]
+                product(b, c, dst)
+                if b == 1:
+                    if c == PER:
+                        finish_first_half()
+                    else:
+                        finish_chunk(c - 1)
+                    if c == CHUNKS - 1:
+                        store(PER, c)
+                    quantize_h(1, c, c + 1, dst)
+        finish_chunk(CHUNKS - 1)
+        store(CHUNKS - 1, CHUNKS)

@@ -31,6 +31,7 @@ def tile_list_gmlpt_silu_res_resL_kernel(
     nc = tc.nc
     with ExitStack() as ctx:
         keep = ctx.enter_context(tc.tile_pool(name="keep", bufs=1))
+        ring = ctx.enter_context(tc.tile_pool(name="ring", bufs=CHUNKS))
         psum = ctx.enter_context(tc.psum_pool(name="psum", bufs=1))
 
         def held(name, shape, dtype, tag=""):
@@ -72,49 +73,50 @@ def tile_list_gmlpt_silu_res_resL_kernel(
             src = wg[PASS * a : PASS * (a + 1), PASS * b : PASS * (b + 1)]
             nc.sync.dma_start(wg_raw[b, a][:], src.rearrange("(p i) c -> p i c", i=PACK))
 
-        def load_planes(queue, planes, scales, q):
-            queue.dma_start(
-                planes[32 * q : 32 * q + 4, :, :].bitcast(I32),
-                scales[:, 4 * q : 4 * q + 4, :].rearrange("a q n -> q a n").bitcast(I32),
+        def load_planes(planes, scales, r):
+            nc.sync.dma_start(
+                planes[r:P:32, :, :].bitcast(I32), scales[:, r:16:4, :].rearrange("a q n -> q a n").bitcast(I32)
             )
 
         nc.sync.dma_start(offsets[:], offs)
         load_wu(0, 0)
-        for q in range(4):
-            nc.sync.dma_start(plane_words[32 * q : 32 * q + 8, :], tab_scales[:, 4 * q : 4 * q + 4, :].bitcast(I32))
+        for r in range(4):
+            rows = tab_scales[:, r:16:4, :].rearrange("a q t -> q a t")
+            nc.sync.dma_start(plane_words[r:P:16, :], rows.bitcast(I32))
         nc.sync.dma_start(table[:], tab_words[0].rearrange("p t e -> p (t e)").bitcast(I32))
         for q in range(4):
-            load_planes(nc.sync, wu_planes_raw, wu_scales, q)
+            load_planes(wu_planes_raw, wu_scales, q)
         load_wu(0, 1)
         nc.vector.tensor_copy(picked_planes[:], table_planes[:].indirect(offsets[:]))
-        nc.sync.dma_start(picked_plane1[0:100, :].bitcast(I32), picked_planes[4:104, :].bitcast(I32))
         load_wg(0, 0)
+        nc.sync.dma_start(picked_plane1[0:100, :].bitcast(I32), picked_planes[16:116, :].bitcast(I32))
         load_wg(0, 1)
-        load_wg(1, 0)
         load_wu(1, 0)
         load_wu(1, 1)
+        load_wg(1, 0)
         load_wg(1, 1)
         nc.sync.dma_start(resid[0][:], rT[0:P, :])
+        for q in range(4):
+            load_planes(wd4_planes, wd4_scales, q)
+        nc.sync.dma_start(resid[1][:], rT[P : 2 * P, :])
         nc.sync.dma_start(wd4[:].bitcast(I32), wd4_words.rearrange("a p w -> p a w").bitcast(I32))
         nc.sync.dma_start(wd8[:], wd8_words.rearrange("a p n i -> p a (n i)").bitcast(I32))
-        nc.sync.dma_start(resid[1][:], rT[P : 2 * P, :])
         for q in range(4):
-            load_planes(nc.gpsimd, wd4_planes, wd4_scales, q)
-            load_planes(nc.gpsimd, wd8_planes, wd8_scales, q)
+            load_planes(wd8_planes, wd8_scales, q)
 
         picked_plane = [picked_planes, picked_plane1]
 
-        def order_wu_planes(a, b0, b1):
-            cols = slice(PASS * b0, PASS * b1)
+        def order_wu_planes(b, a):
+            cols = slice(PASS * b, PASS * (b + 1))
             nc.vector.tensor_copy(
-                wu_planes[:, a, cols].rearrange("p (b t m) -> p b m t", t=PACK, m=P),
-                wu_planes_raw[:, a, cols].rearrange("p (b m t) -> p b m t", t=PACK, m=P),
+                wu_planes[:, a, cols].rearrange("p (t g m) -> p g t m", t=PACK, m=16),
+                wu_planes_raw[:, a, cols].rearrange("p (g m t) -> p g t m", t=PACK, m=16),
             )
 
         def order_wu(b, a):
             nc.vector.tensor_copy(
-                wu[b, a][:].rearrange("p (t m) -> p m t", t=PACK),
-                wu_raw[b, a][:].bitcast(U32).rearrange("p (m t) -> p m t", t=PACK),
+                wu[b, a][:].rearrange("p (t g m) -> p g t m", t=PACK, m=4),
+                wu_raw[b, a][:].bitcast(U32).rearrange("p (g m t) -> p g t m", t=PACK, m=4),
             )
 
         pairs, picked = {}, {}
@@ -129,23 +131,20 @@ def tile_list_gmlpt_silu_res_resL_kernel(
             both = pairs[half][:].bitcast(U16).rearrange("p (j a) -> p a j", a=2)
             nc.vector.tensor_copy(picked[half, a][:], both[:, a, :])
 
-        wg_codes, wg_planes, wg_bf = {}, {}, {}
+        wg_codes, wg_planes = {}, {}
 
-        def round_wg(b, a, tp, on_vector):
-            rounded = held(f"wg_bf{b}{a}{tp}", [P, 2 * P * PACK], BF16)
-            dst = rounded[:].rearrange("p (t m i) -> p m i t", t=2, i=PACK)
-            src = wg_raw[b, a][:].rearrange("p i (m t) -> p m i t", t=PACK)[:, :, :, 2 * tp : 2 * tp + 2]
+        def prepare_wg(b, a, on_vector):
+            rounded = held(f"wg_bf{b}{a}", [P, PACK * PASS], BF16)
+            dst = rounded[:].rearrange("p (t m i) -> p m t i", t=PACK, i=PACK)
+            src = wg_raw[b, a][:].rearrange("p i (m t) -> p m t i", t=PACK)
             if on_vector:
                 nc.vector.tensor_copy(dst, src)
             else:
-                nc.scalar.copy(dst, src)
-            wg_bf[b, a, tp] = rounded
-
-        def quantize_wg(b, a, tp):
-            codes = held(f"wg_codes{b}{a}{tp}", [P, 2 * P], U32)
-            plane = held(f"wg_plane{b}{a}{tp}", [P, 2 * P], U8)
-            nc.vector.quantize_mx(out=codes[:].bitcast(FP8X4), scales=plane[:], in_=wg_bf[b, a, tp][:])
-            wg_codes[b, a, tp], wg_planes[b, a, tp] = codes, plane
+                for m0 in range(0, P, P // 4):
+                    nc.scalar.copy(dst[:, m0 : m0 + P // 4], src[:, m0 : m0 + P // 4])
+            wg_codes[b, a] = held(f"wg_codes{b}{a}", [P, PASS], U32)
+            wg_planes[b, a] = held(f"wg_plane{b}{a}", [P, PASS], U8)
+            nc.vector.quantize_mx(out=wg_codes[b, a][:].bitcast(FP8X4), scales=wg_planes[b, a][:], in_=rounded[:])
 
         PER = HALF // CH
 
@@ -162,43 +161,37 @@ def tile_list_gmlpt_silu_res_resL_kernel(
                     stop=(a == 1 and t == PACK - 1),
                 )
 
-        def gate(b, half, t, a):
-            cols = slice((t % 2) * P, (t % 2 + 1) * P)
-            nc.tensor.matmul_mx(
-                banks[PER + t][:],
-                lhsT=wg_codes[b, a, t // 2][:, cols].bitcast(FP8X4),
-                lhsT_scale=wg_planes[b, a, t // 2][:, cols],
-                rhs=picked[half, a][:].bitcast(FP4X4),
-                rhs_scale=picked_plane[a][:, half * HALF : (half + 1) * HALF],
-                start=(a == 0),
-                stop=(a == 1),
-            )
+        def gate(b, c, a):
+            cols = slice(c % PER * CH, (c % PER + 1) * CH)
+            for t in range(PACK):
+                nc.tensor.matmul_mx(
+                    banks[PER + c % PER][:, t * CH : (t + 1) * CH],
+                    lhsT=wg_codes[b, a][:, t * P : (t + 1) * P].bitcast(FP8X4),
+                    lhsT_scale=wg_planes[b, a][:, t * P : (t + 1) * P],
+                    rhs=picked[c // PER, a][:, cols].bitcast(FP4X4),
+                    rhs_scale=picked_plane[a][:, c * CH : (c + 1) * CH],
+                    start=(a == 0 and t == 0),
+                    stop=(a == 1 and t == PACK - 1),
+                )
 
-        acts = {(b, half): held(f"act{b}{half}", [P, PACK, HALF], F32) for b in range(2) for half in range(2)}
         h_bf, h_codes, h_planes = {}, {}, {}
 
-        def silu(b, half, t):
-            nc.scalar.activation(acts[b, half][:, t, :], banks[PER + t][:], SILU)
+        def gated_product(b, c):
+            act = ring.tile([P, CH, PACK], F32, name="act")
+            nc.scalar.activation(act[:], banks[PER + c % PER][:].rearrange("p (t j) -> p j t", t=PACK), SILU)
+            dst = h_bf[b, c // PER][:, c % PER * CH : (c % PER + 1) * CH, :]
+            nc.vector.tensor_tensor(dst, banks[c % PER][:].rearrange("p (t j) -> p j t", t=PACK), act[:], MULT)
 
-        def product(b, c, dst):
-            cols = slice(c % PER * CH, (c % PER + 1) * CH)
-            nc.vector.tensor_tensor(
-                dst.rearrange("p (j e t) -> p j t e", e=2, t=PACK),
-                banks[c % PER][:].rearrange("p (t j e) -> p j t e", t=PACK, e=2),
-                acts[b, c // PER][:, :, cols].rearrange("p t (j e) -> p j t e", e=2),
-                MULT,
+        def quantize_h(b, half):
+            h_codes[b, half] = held(f"h_codes{b}{half}", [P, HALF], U32)
+            h_planes[b, half] = held(f"h_plane{b}{half}", [P, HALF], U8)
+            nc.vector.quantize_mx(
+                out=h_codes[b, half][:].bitcast(FP8X4),
+                scales=h_planes[b, half][:],
+                in_=h_bf[b, half][:].rearrange("p j t -> p (j t)"),
             )
 
-        def quantize_h(b, c0, c1, src):
-            codes = held(f"h_codes{b}{c0}", [P, (c1 - c0) * CH], U32)
-            plane = held(f"h_plane{b}{c0}", [P, (c1 - c0) * CH], U8)
-            nc.vector.quantize_mx(out=codes[:].bitcast(FP8X4), scales=plane[:], in_=src)
-            h_codes[b, c0, c1], h_planes[b, c0, c1] = codes[:], plane[:]
-            for c in range(c0, c1):
-                cols = slice((c - c0) * CH, (c - c0 + 1) * CH)
-                h_codes[b, c, c + 1], h_planes[b, c, c + 1] = codes[:, cols], plane[:, cols]
-
-        def down(dst, n, b, c0, c1, start, stop):
+        def down(n, b, half):
             cols = slice(n * P, (n + 1) * P)
             tiers = (
                 (wd4[:, b, 2 * n * P : 2 * (n + 1) * P].bitcast(FP4X4), wd4_planes[:, b, cols]),
@@ -206,58 +199,35 @@ def tile_list_gmlpt_silu_res_resL_kernel(
             )
             for tier, (lhsT, lhsT_scale) in enumerate(tiers):
                 nc.tensor.matmul_mx(
-                    dst,
+                    banks[PER + 2 * half + n][:],
                     lhsT=lhsT,
                     lhsT_scale=lhsT_scale,
-                    rhs=h_codes[b, c0, c1].bitcast(FP8X4),
-                    rhs_scale=h_planes[b, c0, c1],
-                    start=(start and tier == 0),
-                    stop=(stop and tier == 1),
+                    rhs=h_codes[b, half][:].bitcast(FP8X4),
+                    rhs_scale=h_planes[b, half][:],
+                    start=(b == 0 and tier == 0),
+                    stop=(b == 1 and tier == 1),
                 )
 
-        picked_resid = held("picked_resid", [P, 2, J], F32)
-        result = held("result", [P, 2, J], F32)
-        out_view = out.rearrange("(n p) j -> p n j", p=P)
+        picked_resid = {}
 
-        def pick_resid(n):
-            nc.vector.tensor_copy(picked_resid[:, n, :], resid[n][:].indirect(offsets[:]))
+        def pick_resid(n, half):
+            picked_resid[n, half] = held(f"picked_resid{n}{half}", [P, HALF], F32)
+            cols = slice(half * HALF // 16, (half + 1) * HALF // 16)
+            nc.vector.tensor_copy(picked_resid[n, half][:], resid[n][:].indirect(offsets[:, cols]))
 
-        def store(c0, c1):
-            nc.sync.dma_start(out_view[:, :, c0 * CH : c1 * CH], result[:, :, c0 * CH : c1 * CH])
-
-        def finish_first_half():
-            for n in range(2):
-                bank = banks[7 - n]
-                for b in range(2):
-                    down(bank[:], n, b, 0, PER, b == 0, b == 1)
-                nc.vector.tensor_tensor(result[:, n, 0:HALF], bank[:], picked_resid[:, n, 0:HALF], ADD)
-            store(0, PER)
-
-        def finish_chunk(c):
-            bank = banks[PER + (c + 1) % PER]
-            for b in range(2):
-                for n in range(2):
-                    down(bank[:, n * CH : (n + 1) * CH], n, b, c, c + 1, b == 0 and n == 0, b == 1 and n == 1)
-            cols = slice(c * CH, (c + 1) * CH)
-            sums = bank[:, 0 : 2 * CH].rearrange("p (n j) -> p n j", n=2)
-            nc.vector.tensor_tensor(result[:, :, cols], sums, picked_resid[:, :, cols], ADD)
-
-        def prepare_wg(b, a, on_vector):
-            round_wg(b, a, 1, on_vector)
-            round_wg(b, a, 0, False)
-            quantize_wg(b, a, 1)
-            quantize_wg(b, a, 0)
+        def finish(n, half):
+            result = held(f"result{n}{half}", [P, HALF], F32)
+            nc.vector.tensor_tensor(result[:], banks[PER + 2 * half + n][:], picked_resid[n, half][:], ADD)
+            nc.sync.dma_start(out[P * n : P * (n + 1), half * HALF : (half + 1) * HALF], result[:])
 
         order_wu(0, 0)
         pick_words(0)
         for a in range(2):
             part_words(0, a)
-            order_wu_planes(a, 0, 1)
+            order_wu_planes(0, a)
         order_wu(0, 1)
         for a in range(2):
-            order_wu_planes(a, 1, 2)
-        slots = range(PACK - 1, -1, -1)
-        W = PACK * CH
+            order_wu_planes(1, a)
         for b in range(2):
             for a in range(2):
                 for c in range(PER):
@@ -268,43 +238,37 @@ def tile_list_gmlpt_silu_res_resL_kernel(
                 part_words(1, 1)
                 prepare_wg(0, 0, False)
                 prepare_wg(0, 1, True)
-            for t in slots:
-                gate(b, 0, t, 0)
-            for t in slots:
-                gate(b, 0, t, 1)
-                silu(b, 0, t)
-            if b == 0:
-                prepare_wg(1, 0, False)
-            else:
-                quantize_h(0, 0, PER, h_bf[0, 0][:])
-                quantize_h(0, PER, CHUNKS, h_bf[0, 1][:])
-                pick_resid(0)
-            h_bf[b, 0] = held(f"h_bf{b}0", [P, PER * W], BF16, "resid0" if b else "")
-            for c in range(PER):
-                product(b, c, h_bf[b, 0][:, c * W : (c + 1) * W])
-                gate(b, 1, slots[c], 0)
-                gate(b, 1, slots[c], 1)
-                silu(b, 1, slots[c])
-            if b == 0:
                 order_wu(1, 0)
                 order_wu(1, 1)
+            for c in range(PER):
+                gate(b, c, 0)
+            if b == 1:
+                quantize_h(0, 0)
+                quantize_h(0, 1)
+                pick_resid(0, 0)
+                pick_resid(0, 1)
+            for half in range(2):
+                tag = "resid0" if (b, half) == (1, 0) else ""
+                h_bf[b, half] = held(f"h_bf{b}{half}", [P, HALF, PACK], BF16, tag)
+            for c in range(CHUNKS):
+                if c >= PER:
+                    gate(b, c, 0)
+                gate(b, c, 1)
+                if c >= PER:
+                    up(b, c, 0)
+                    up(b, c, 1)
+                gated_product(b, c)
+                if b == 1 and c == PER - 1:
+                    quantize_h(1, 0)
+            if b == 0:
+                prepare_wg(1, 0, False)
                 prepare_wg(1, 1, False)
-            else:
-                quantize_h(1, 0, PER, h_bf[1, 0][:])
-                pick_resid(1)
-            h_bf[b, 1] = held(f"h_bf{b}1", [P, PER * W], BF16, "resid1" if b else "")
-            for c in range(PER, CHUNKS):
-                up(b, c, 0)
-                up(b, c, 1)
-                dst = h_bf[b, 1][:, (c - PER) * W : (c - PER + 1) * W]
-                product(b, c, dst)
-                if b == 1:
-                    if c == PER:
-                        finish_first_half()
-                    else:
-                        finish_chunk(c - 1)
-                    if c == CHUNKS - 1:
-                        store(PER, c)
-                    quantize_h(1, c, c + 1, dst)
-        finish_chunk(CHUNKS - 1)
-        store(CHUNKS - 1, CHUNKS)
+        quantize_h(1, 1)
+        for half in range(2):
+            for b in range(2):
+                for n in range(2):
+                    down(n, b, half)
+        for half in range(2):
+            finish(0, half)
+            pick_resid(1, half)
+            finish(1, half)

@@ -49,8 +49,7 @@ def tile_list_gmlpt_silu_res_resL_kernel(
         wd4 = held("wd4", [P, 2, 2 * N], U8)
         wd8 = held("wd8", [P, 2, N], I32)
         resid = [held(f"resid{n}", [P, T], F32) for n in range(2)]
-        wu_raw = {(b, a): held(f"wu_raw{b}{a}", [P, PASS], I32) for b in range(2) for a in range(2)}
-        wu = {(b, a): held(f"wu{b}{a}", [P, PASS], U32) for b in range(2) for a in range(2)}
+        wu_raw, wu = {}, {}
         wg_raw = {(b, a): held(f"wg_raw{b}{a}", [P, PACK, PASS], F32) for b in range(2) for a in range(2)}
         warm = held("warm", [P, 2], F32)
         banks = [psum.tile([P, PACK * CH], F32, name=f"bank{i}") for i in range(8)]
@@ -65,9 +64,10 @@ def tile_list_gmlpt_silu_res_resL_kernel(
         nc.gpsimd.memset(wd4_planes[:].rearrange("p a n -> p (a n)").bitcast(I32), 0)
         nc.gpsimd.memset(wd8_planes[:].rearrange("p a n -> p (a n)").bitcast(I32), 0)
 
-        def load_wu(b, a):
-            src = wu_words[a].rearrange("p r i -> p (r i)")[:, 4 * PASS * b : 4 * PASS * (b + 1)]
-            nc.sync.dma_start(wu_raw[b, a][:], src.bitcast(I32))
+        def load_wu(b, a0, a1):
+            wu_raw[b, a0] = held(f"wu_raw{b}{a0}", [P, a1 - a0, PASS], I32)
+            src = wu_words[a0:a1].rearrange("a p r i -> p a (r i)")[:, :, 4 * PASS * b : 4 * PASS * (b + 1)]
+            nc.sync.dma_start(wu_raw[b, a0][:], src.bitcast(I32))
 
         def load_wg(b, a):
             src = wg[PASS * a : PASS * (a + 1), PASS * b : PASS * (b + 1)]
@@ -79,20 +79,19 @@ def tile_list_gmlpt_silu_res_resL_kernel(
             )
 
         nc.sync.dma_start(offsets[:], offs)
-        load_wu(0, 0)
+        load_wu(0, 0, 1)
         for r in range(4):
             rows = tab_scales[:, r:16:4, :].rearrange("a q t -> q a t")
             nc.sync.dma_start(plane_words[r:P:16, :], rows.bitcast(I32))
         nc.sync.dma_start(table[:], tab_words[0].rearrange("p t e -> p (t e)").bitcast(I32))
         for q in range(4):
             load_planes(wu_planes_raw, wu_scales, q)
-        load_wu(0, 1)
+        load_wu(0, 1, 2)
         nc.vector.tensor_copy(picked_planes[:], table_planes[:].indirect(offsets[:]))
         load_wg(0, 0)
         nc.sync.dma_start(picked_plane1[0:100, :].bitcast(I32), picked_planes[16:116, :].bitcast(I32))
         load_wg(0, 1)
-        load_wu(1, 0)
-        load_wu(1, 1)
+        load_wu(1, 0, 2)
         load_wg(1, 0)
         load_wg(1, 1)
         nc.sync.dma_start(resid[0][:], rT[0:P, :])
@@ -106,18 +105,21 @@ def tile_list_gmlpt_silu_res_resL_kernel(
 
         picked_plane = [picked_planes, picked_plane1]
 
-        def order_wu_planes(b, a):
+        def order_wu_planes(b, a0, a1):
             cols = slice(PASS * b, PASS * (b + 1))
             nc.vector.tensor_copy(
-                wu_planes[:, a, cols].rearrange("p (t g m) -> p g t m", t=PACK, m=16),
-                wu_planes_raw[:, a, cols].rearrange("p (g m t) -> p g t m", t=PACK, m=16),
+                wu_planes[:, a0:a1, cols].rearrange("p a (t g m) -> p a g t m", t=PACK, m=16),
+                wu_planes_raw[:, a0:a1, cols].rearrange("p a (g m t) -> p a g t m", t=PACK, m=16),
             )
 
-        def order_wu(b, a):
+        def order_wu(b, a0, a1):
+            ordered = held(f"wu{b}{a0}", [P, a1 - a0, PASS], U32)
             nc.vector.tensor_copy(
-                wu[b, a][:].rearrange("p (t g m) -> p g t m", t=PACK, m=4),
-                wu_raw[b, a][:].bitcast(U32).rearrange("p (g m t) -> p g t m", t=PACK, m=4),
+                ordered[:].rearrange("p a (t g m) -> p a g t m", t=PACK, m=4),
+                wu_raw[b, a0][:].bitcast(U32).rearrange("p a (g m t) -> p a g t m", t=PACK, m=4),
             )
+            for a in range(a0, a1):
+                wu[b, a] = ordered[:, a - a0, :]
 
         pairs, picked = {}, {}
 
@@ -126,22 +128,23 @@ def tile_list_gmlpt_silu_res_resL_kernel(
             cols = slice(half * HALF // 16, (half + 1) * HALF // 16)
             nc.vector.tensor_copy(pairs[half][:], table[:].bitcast(U32).indirect(offsets[:, cols]))
 
-        def part_words(half, a):
-            picked[half, a] = held(f"picked{half}{a}", [P, HALF], U16)
+        def part_words(half, a0, a1):
+            parted = held(f"picked{half}{a0}", [P, a1 - a0, HALF], U16)
             both = pairs[half][:].bitcast(U16).rearrange("p (j a) -> p a j", a=2)
-            nc.vector.tensor_copy(picked[half, a][:], both[:, a, :])
+            nc.vector.tensor_copy(parted[:], both[:, a0:a1, :])
+            for a in range(a0, a1):
+                picked[half, a] = parted[:, a - a0, :]
 
         wg_codes, wg_planes = {}, {}
 
-        def prepare_wg(b, a, on_vector):
+        def prepare_wg(b, a, scalar_quarters):
             rounded = held(f"wg_bf{b}{a}", [P, PACK * PASS], BF16)
             dst = rounded[:].rearrange("p (t m i) -> p m t i", t=PACK, i=PACK)
             src = wg_raw[b, a][:].rearrange("p i (m t) -> p m t i", t=PACK)
-            if on_vector:
-                nc.vector.tensor_copy(dst, src)
-            else:
-                for m0 in range(0, P, P // 4):
-                    nc.scalar.copy(dst[:, m0 : m0 + P // 4], src[:, m0 : m0 + P // 4])
+            for m0 in range(0, scalar_quarters * P // 4, P // 4):
+                nc.scalar.copy(dst[:, m0 : m0 + P // 4], src[:, m0 : m0 + P // 4])
+            if scalar_quarters < 4:
+                nc.vector.tensor_copy(dst[:, scalar_quarters * P // 4 :], src[:, scalar_quarters * P // 4 :])
             wg_codes[b, a] = held(f"wg_codes{b}{a}", [P, PASS], U32)
             wg_planes[b, a] = held(f"wg_plane{b}{a}", [P, PASS], U8)
             nc.vector.quantize_mx(out=wg_codes[b, a][:].bitcast(FP8X4), scales=wg_planes[b, a][:], in_=rounded[:])
@@ -210,45 +213,41 @@ def tile_list_gmlpt_silu_res_resL_kernel(
 
         picked_resid = {}
 
-        def pick_resid(n, half):
-            picked_resid[n, half] = held(f"picked_resid{n}{half}", [P, HALF], F32)
-            cols = slice(half * HALF // 16, (half + 1) * HALF // 16)
-            nc.vector.tensor_copy(picked_resid[n, half][:], resid[n][:].indirect(offsets[:, cols]))
+        def pick_resid(n):
+            picked_resid[n] = held(f"picked_resid{n}", [P, J], F32)
+            nc.vector.tensor_copy(picked_resid[n][:], resid[n][:].indirect(offsets[:]))
 
         def finish(n, half):
             result = held(f"result{n}{half}", [P, HALF], F32)
-            nc.vector.tensor_tensor(result[:], banks[PER + 2 * half + n][:], picked_resid[n, half][:], ADD)
+            nc.vector.tensor_tensor(result[:], banks[PER + 2 * half + n][:], picked_resid[n][:, half * HALF : (half + 1) * HALF], ADD)
             nc.sync.dma_start(out[P * n : P * (n + 1), half * HALF : (half + 1) * HALF], result[:])
 
-        order_wu(0, 0)
+        order_wu(0, 0, 1)
         pick_words(0)
         for a in range(2):
-            part_words(0, a)
-            order_wu_planes(0, a)
-        order_wu(0, 1)
-        for a in range(2):
-            order_wu_planes(1, a)
+            part_words(0, a, a + 1)
+            order_wu_planes(0, a, a + 1)
+        order_wu(0, 1, 2)
+        order_wu_planes(1, 0, 2)
         for b in range(2):
             for a in range(2):
                 for c in range(PER):
                     up(b, c, a)
             if b == 0:
                 pick_words(1)
-                part_words(1, 0)
-                part_words(1, 1)
-                prepare_wg(0, 0, False)
-                prepare_wg(0, 1, True)
-                order_wu(1, 0)
-                order_wu(1, 1)
+                part_words(1, 0, 2)
+                prepare_wg(0, 0, 4)
+                prepare_wg(0, 1, 2)
+                order_wu(1, 0, 2)
             for c in range(PER):
                 gate(b, c, 0)
             if b == 1:
                 quantize_h(0, 0)
                 quantize_h(0, 1)
-                pick_resid(0, 0)
-                pick_resid(0, 1)
+                pick_resid(0)
+                pick_resid(1)
             for half in range(2):
-                tag = "resid0" if (b, half) == (1, 0) else ""
+                tag = "resid1" if (b, half) == (1, 1) else ""
                 h_bf[b, half] = held(f"h_bf{b}{half}", [P, HALF, PACK], BF16, tag)
             for c in range(CHUNKS):
                 if c >= PER:
@@ -261,8 +260,8 @@ def tile_list_gmlpt_silu_res_resL_kernel(
                 if b == 1 and c == PER - 1:
                     quantize_h(1, 0)
             if b == 0:
-                prepare_wg(1, 0, False)
-                prepare_wg(1, 1, False)
+                prepare_wg(1, 0, 4)
+                prepare_wg(1, 1, 2)
         quantize_h(1, 1)
         for half in range(2):
             for b in range(2):
@@ -270,5 +269,4 @@ def tile_list_gmlpt_silu_res_resL_kernel(
                     down(n, b, half)
         for half in range(2):
             finish(0, half)
-            pick_resid(1, half)
             finish(1, half)

@@ -40,9 +40,9 @@ def tile_list_gmlpt_silu_res_resL_kernel(
         offsets = keep.tile([P, J // 16], U16, name="offsets")
         table = held("table", [P, T], I32)
         table_planes = held("table_planes", [P, T], U8)
-        picked_planes = held("picked_planes", [P, J], U8)
-        picked_plane1 = held("picked_plane1", [P, J], U8)
-        wu_planes_raw = held("wu_planes_raw", [P, 2, R], U8, "late_pairs")
+        picked_rows = held("picked_rows", [P, J], U8)
+        picked_planes = held("picked_planes", [P, 2, J], U8)
+        wu_planes_raw = held("wu_planes_raw", [P, 2, R], U8)
         wu_planes = held("wu_planes", [P, 2, R], U8)
         wd4_planes = held("wd4_planes", [P, 2, N], U8)
         wd8_planes = held("wd8_planes", [P, 2, N], U8)
@@ -51,18 +51,15 @@ def tile_list_gmlpt_silu_res_resL_kernel(
         resid = [held(f"resid{n}", [P, T], F32) for n in range(2)]
         wu_raw, wu = {}, {}
         wg_raw = {(b, a): held(f"wg_raw{b}{a}", [P, PACK, PASS], F32) for b in range(2) for a in range(2)}
-        warm = held("warm", [P, 2], F32)
         banks = [psum.tile([P, PACK * CH], F32, name=f"bank{i}") for i in range(8)]
 
         plane_words = table_planes[:].bitcast(I32)
-        nc.vector.memset(plane_words[:, 0:640], 0)
-        nc.gpsimd.memset(plane_words[:, 640:1024], 0)
-        nc.vector.memset(warm[:, 0:1], 0.0)
-        nc.scalar.activation(warm[:, 1:2], warm[:, 0:1], SILU)
+        nc.gpsimd.memset(plane_words[:, 0:640], 0)
+        nc.vector.memset(plane_words[:, 640:1024], 0)
         nc.gpsimd.memset(wu_planes_raw[:].rearrange("p a r -> p (a r)").bitcast(I32), 0)
-        nc.gpsimd.memset(picked_plane1[:].bitcast(I32), 0)
-        nc.gpsimd.memset(wd4_planes[:].rearrange("p a n -> p (a n)").bitcast(I32), 0)
-        nc.gpsimd.memset(wd8_planes[:].rearrange("p a n -> p (a n)").bitcast(I32), 0)
+        nc.vector.memset(picked_planes[:].rearrange("p a j -> p (a j)").bitcast(I32), 0)
+        nc.vector.memset(wd4_planes[:].rearrange("p a n -> p (a n)").bitcast(I32), 0)
+        nc.vector.memset(wd8_planes[:].rearrange("p a n -> p (a n)").bitcast(I32), 0)
 
         def load_wu(b, a0, a1):
             wu_raw[b, a0] = held(f"wu_raw{b}{a0}", [P, a1 - a0, PASS], I32)
@@ -79,18 +76,21 @@ def tile_list_gmlpt_silu_res_resL_kernel(
             )
 
         nc.sync.dma_start(offsets[:], offs)
-        load_wu(0, 0, 1)
+        load_wu(0, 0, 2)
+        nc.sync.dma_start(plane_words[0:P:4, :], tab_scales.rearrange("a q t -> (a q) t").bitcast(I32))
         for r in range(4):
-            rows = tab_scales[:, r:16:4, :].rearrange("a q t -> q a t")
-            nc.sync.dma_start(plane_words[r:P:16, :], rows.bitcast(I32))
+            load_planes(wu_planes_raw, wu_scales, r)
         nc.sync.dma_start(table[:], tab_words[0].rearrange("p t e -> p (t e)").bitcast(I32))
-        for q in range(4):
-            load_planes(wu_planes_raw, wu_scales, q)
-        load_wu(0, 1, 2)
-        nc.vector.tensor_copy(picked_planes[:], table_planes[:].indirect(offsets[:]))
-        load_wg(0, 0)
-        nc.sync.dma_start(picked_plane1[0:100, :].bitcast(I32), picked_planes[16:116, :].bitcast(I32))
-        load_wg(0, 1)
+        nc.vector.tensor_copy(picked_rows[:], table_planes[:].indirect(offsets[:]))
+
+        def place_rows(a):
+            for r in range(4):
+                rows = picked_rows[64 * a + 4 * r : 64 * (a + 1) : 16, :]
+                nc.sync.dma_start(picked_planes[r:P:32, a, :].bitcast(I32), rows.bitcast(I32))
+
+        for a in range(2):
+            place_rows(a)
+            load_wg(0, a)
         load_wu(1, 0, 2)
         load_wg(1, 0)
         load_wg(1, 1)
@@ -103,13 +103,12 @@ def tile_list_gmlpt_silu_res_resL_kernel(
         for q in range(4):
             load_planes(wd8_planes, wd8_scales, q)
 
-        picked_plane = [picked_planes, picked_plane1]
 
-        def order_wu_planes(b, a0, a1):
+        def order_wu_planes(b):
             cols = slice(PASS * b, PASS * (b + 1))
             nc.vector.tensor_copy(
-                wu_planes[:, a0:a1, cols].rearrange("p a (t g m) -> p a g t m", t=PACK, m=16),
-                wu_planes_raw[:, a0:a1, cols].rearrange("p a (g m t) -> p a g t m", t=PACK, m=16),
+                wu_planes[:, :, cols].rearrange("p a (t g m) -> p a g t m", t=PACK, m=16),
+                wu_planes_raw[:, :, cols].rearrange("p a (g m t) -> p a g t m", t=PACK, m=16),
             )
 
         def order_wu(b, a0, a1):
@@ -124,7 +123,7 @@ def tile_list_gmlpt_silu_res_resL_kernel(
         pairs, picked = {}, {}
 
         def pick_words(half):
-            pairs[half] = held(f"pairs{half}", [P, HALF], U32, "late_pairs" if half else "")
+            pairs[half] = held(f"pairs{half}", [P, HALF], U32, "pairs")
             cols = slice(half * HALF // 16, (half + 1) * HALF // 16)
             nc.vector.tensor_copy(pairs[half][:], table[:].bitcast(U32).indirect(offsets[:, cols]))
 
@@ -159,7 +158,7 @@ def tile_list_gmlpt_silu_res_resL_kernel(
                     lhsT=wu[b, a][:, t * P : (t + 1) * P].bitcast(FP8X4),
                     lhsT_scale=wu_planes[:, a, PASS * b + t * P : PASS * b + (t + 1) * P],
                     rhs=picked[c // PER, a][:, cols].bitcast(FP4X4),
-                    rhs_scale=picked_plane[a][:, c * CH : (c + 1) * CH],
+                    rhs_scale=picked_planes[:, a, c * CH : (c + 1) * CH],
                     start=(a == 0 and t == 0),
                     stop=(a == 1 and t == PACK - 1),
                 )
@@ -172,7 +171,7 @@ def tile_list_gmlpt_silu_res_resL_kernel(
                     lhsT=wg_codes[b, a][:, t * P : (t + 1) * P].bitcast(FP8X4),
                     lhsT_scale=wg_planes[b, a][:, t * P : (t + 1) * P],
                     rhs=picked[c // PER, a][:, cols].bitcast(FP4X4),
-                    rhs_scale=picked_plane[a][:, c * CH : (c + 1) * CH],
+                    rhs_scale=picked_planes[:, a, c * CH : (c + 1) * CH],
                     start=(a == 0 and t == 0),
                     stop=(a == 1 and t == PACK - 1),
                 )
@@ -222,13 +221,12 @@ def tile_list_gmlpt_silu_res_resL_kernel(
             nc.vector.tensor_tensor(result[:], banks[PER + 2 * half + n][:], picked_resid[n][:, half * HALF : (half + 1) * HALF], ADD)
             nc.sync.dma_start(out[P * n : P * (n + 1), half * HALF : (half + 1) * HALF], result[:])
 
-        order_wu(0, 0, 1)
+        order_wu(0, 0, 2)
+        order_wu_planes(0)
+        order_wu_planes(1)
         pick_words(0)
         for a in range(2):
             part_words(0, a, a + 1)
-            order_wu_planes(0, a, a + 1)
-        order_wu(0, 1, 2)
-        order_wu_planes(1, 0, 2)
         for b in range(2):
             for a in range(2):
                 for c in range(PER):
@@ -237,7 +235,7 @@ def tile_list_gmlpt_silu_res_resL_kernel(
                 pick_words(1)
                 part_words(1, 0, 2)
                 prepare_wg(0, 0, 4)
-                prepare_wg(0, 1, 2)
+                prepare_wg(0, 1, 1)
                 order_wu(1, 0, 2)
             for c in range(PER):
                 gate(b, c, 0)

@@ -23,6 +23,9 @@ PASS = P * PACK
 CH = 128
 CHUNKS = J // CH
 HALF = J // 2
+PER = HALF // CH
+LIVE = 96
+WU_AT, WD4_AT, WD8_AT, ROW = J, J + R, J + R + N, J + R + 2 * N
 
 
 def tile_list_gmlpt_silu_res_resL_kernel(
@@ -41,81 +44,74 @@ def tile_list_gmlpt_silu_res_resL_kernel(
         table = held("table", [P, T], I32)
         table_planes = held("table_planes", [P, T], U8)
         picked_rows = held("picked_rows", [P, J], U8)
-        picked_planes = held("picked_planes", [P, 2, J], U8)
-        wu_planes_raw = held("wu_planes_raw", [P, 2, R], U8)
-        wu_planes = held("wu_planes", [P, 2, R], U8)
-        wd4_planes = held("wd4_planes", [P, 2, N], U8)
-        wd8_planes = held("wd8_planes", [P, 2, N], U8)
+        wu_rows = held("wu_rows", [P, R], U8)
+        rows = held("rows", [P, ROW], U8)
+        planes = [held(f"planes{a}", [P, ROW], U8) for a in range(2)]
         wd4 = held("wd4", [P, 2, 2 * N], U8)
         wd8 = held("wd8", [P, 2, N], I32)
         resid = [held(f"resid{n}", [P, T], F32) for n in range(2)]
-        wu_raw, wu = {}, {}
-        wg_raw = {(b, a): held(f"wg_raw{b}{a}", [P, PACK, PASS], F32) for b in range(2) for a in range(2)}
+        wu_raw, wu, wg_raw = {}, {}, {}
         banks = [psum.tile([P, PACK * CH], F32, name=f"bank{i}") for i in range(8)]
 
         plane_words = table_planes[:].bitcast(I32)
-        nc.gpsimd.memset(plane_words[:, 0:640], 0)
-        nc.vector.memset(plane_words[:, 640:1024], 0)
-        nc.gpsimd.memset(wu_planes_raw[:].rearrange("p a r -> p (a r)").bitcast(I32), 0)
-        nc.vector.memset(picked_planes[:].rearrange("p a j -> p (a j)").bitcast(I32), 0)
-        nc.vector.memset(wd4_planes[:].rearrange("p a n -> p (a n)").bitcast(I32), 0)
-        nc.vector.memset(wd8_planes[:].rearrange("p a n -> p (a n)").bitcast(I32), 0)
+        nc.gpsimd.memset(plane_words[0:LIVE, :], 0)
+        nc.vector.memset(wu_rows[0:LIVE, :].bitcast(I32), 0)
+        for a in range(2):
+            nc.vector.memset(planes[a][:].bitcast(I32), 0)
 
         def load_wu(b, a0, a1):
             wu_raw[b, a0] = held(f"wu_raw{b}{a0}", [P, a1 - a0, PASS], I32)
             src = wu_words[a0:a1].rearrange("a p r i -> p a (r i)")[:, :, 4 * PASS * b : 4 * PASS * (b + 1)]
             nc.sync.dma_start(wu_raw[b, a0][:], src.bitcast(I32))
 
-        def load_wg(b, a):
-            src = wg[PASS * a : PASS * (a + 1), PASS * b : PASS * (b + 1)]
-            nc.sync.dma_start(wg_raw[b, a][:], src.rearrange("(p i) c -> p i c", i=PACK))
+        def load_wg(b, a, m0, m1):
+            wg_raw[b, a, m0] = held(f"wg_raw{b}{a}{m0}", [P, PACK, PACK * (m1 - m0)], F32)
+            src = wg[PASS * a : PASS * (a + 1), PASS * b + PACK * m0 : PASS * b + PACK * m1]
+            nc.sync.dma_start(wg_raw[b, a, m0][:], src.rearrange("(p i) c -> p i c", i=PACK))
 
-        def load_planes(planes, scales, r):
-            nc.sync.dma_start(
-                planes[r:P:32, :, :].bitcast(I32), scales[:, r:16:4, :].rearrange("a q n -> q a n").bitcast(I32)
-            )
-
-        nc.sync.dma_start(offsets[:], offs)
-        load_wu(0, 0, 2)
-        nc.sync.dma_start(plane_words[0:P:4, :], tab_scales.rearrange("a q t -> (a q) t").bitcast(I32))
-        for r in range(4):
-            load_planes(wu_planes_raw, wu_scales, r)
-        nc.sync.dma_start(table[:], tab_words[0].rearrange("p t e -> p (t e)").bitcast(I32))
-        nc.vector.tensor_copy(picked_rows[:], table_planes[:].indirect(offsets[:]))
+        def load_rows(queue, dst, scales):
+            queue.dma_start(dst.bitcast(I32), scales.rearrange("a q n -> (a q) n").bitcast(I32))
 
         def place_rows(a):
             for r in range(4):
-                rows = picked_rows[64 * a + 4 * r : 64 * (a + 1) : 16, :]
-                nc.sync.dma_start(picked_planes[r:P:32, a, :].bitcast(I32), rows.bitcast(I32))
+                nc.sync.dma_start(planes[a][r:P:32, :].bitcast(I32), rows[LIVE + 16 * a + r : LIVE + 16 * (a + 1) : 4, :].bitcast(I32))
 
-        for a in range(2):
-            place_rows(a)
-            load_wg(0, a)
+        load_rows(nc.sync, table_planes[LIVE:P, :], tab_scales)
+        nc.sync.dma_start(offsets[:], offs)
+        load_rows(nc.scalar, wu_rows[LIVE:P, :], wu_scales)
+        load_rows(nc.scalar, rows[LIVE:P, WD4_AT:WD8_AT], wd4_scales)
+        load_rows(nc.sync, rows[LIVE:P, WD8_AT:ROW], wd8_scales)
+        nc.sync.dma_start(table[:], tab_words[0].rearrange("p t e -> p (t e)").bitcast(I32))
+        load_wu(0, 0, 2)
+
+        warm = held("warm", [P, 2], F32)
+        nc.gpsimd.memset(warm[:, 0:1], 0.0)
+        nc.scalar.activation(warm[:, 1:2], warm[:, 0:1], SILU)
+        nc.vector.tensor_copy(
+            rows[:, WU_AT:WD4_AT].rearrange("p (b t g m) -> p b g t m", b=2, t=PACK, m=16),
+            wu_rows[:].rearrange("p (b g m t) -> p b g t m", b=2, t=PACK, m=16),
+        )
+        nc.vector.tensor_copy(picked_rows[:], table_planes[:].indirect(offsets[:]))
+        nc.vector.tensor_copy(rows[LIVE:P, 0:J].bitcast(I32), picked_rows[LIVE:P, :].bitcast(I32))
+        load_wg(0, 0, 0, P // 2)
+        place_rows(0)
+        load_wg(0, 0, P // 2, P)
+        load_wg(0, 1, 0, P // 2)
+        load_wg(0, 1, P // 2, P)
+        place_rows(1)
+        load_wg(1, 0, 0, P)
+        load_wg(1, 1, 0, P)
         load_wu(1, 0, 2)
-        load_wg(1, 0)
-        load_wg(1, 1)
-        nc.sync.dma_start(resid[0][:], rT[0:P, :])
-        for q in range(4):
-            load_planes(wd4_planes, wd4_scales, q)
-        nc.sync.dma_start(resid[1][:], rT[P : 2 * P, :])
         nc.sync.dma_start(wd4[:].bitcast(I32), wd4_words.rearrange("a p w -> p a w").bitcast(I32))
         nc.sync.dma_start(wd8[:], wd8_words.rearrange("a p n i -> p a (n i)").bitcast(I32))
-        for q in range(4):
-            load_planes(wd8_planes, wd8_scales, q)
-
-
-        def order_wu_planes(b):
-            cols = slice(PASS * b, PASS * (b + 1))
-            nc.vector.tensor_copy(
-                wu_planes[:, :, cols].rearrange("p a (t g m) -> p a g t m", t=PACK, m=16),
-                wu_planes_raw[:, :, cols].rearrange("p a (g m t) -> p a g t m", t=PACK, m=16),
-            )
+        nc.sync.dma_start(resid[0][:], rT[0:P, :])
+        nc.sync.dma_start(resid[1][:], rT[P : 2 * P, :])
 
         def order_wu(b, a0, a1):
             ordered = held(f"wu{b}{a0}", [P, a1 - a0, PASS], U32)
             nc.vector.tensor_copy(
                 ordered[:].rearrange("p a (t g m) -> p a g t m", t=PACK, m=4),
-                wu_raw[b, a0][:].bitcast(U32).rearrange("p a (g m t) -> p a g t m", t=PACK, m=4),
+                wu_raw[b, 0][:, a0:a1, :].bitcast(U32).rearrange("p a (g m t) -> p a g t m", t=PACK, m=4),
             )
             for a in range(a0, a1):
                 wu[b, a] = ordered[:, a - a0, :]
@@ -134,137 +130,183 @@ def tile_list_gmlpt_silu_res_resL_kernel(
             for a in range(a0, a1):
                 picked[half, a] = parted[:, a - a0, :]
 
-        wg_codes, wg_planes = {}, {}
+        wg_bf, wg_codes, wg_planes = {}, {}, {}
+        for b in range(2):
+            for a in range(2):
+                wg_bf[b, a] = held(f"wg_bf{b}{a}", [P, PACK * PASS], BF16)
 
-        def prepare_wg(b, a, scalar_quarters):
-            rounded = held(f"wg_bf{b}{a}", [P, PACK * PASS], BF16)
-            dst = rounded[:].rearrange("p (t m i) -> p m t i", t=PACK, i=PACK)
-            src = wg_raw[b, a][:].rearrange("p i (m t) -> p m t i", t=PACK)
-            for m0 in range(0, scalar_quarters * P // 4, P // 4):
-                nc.scalar.copy(dst[:, m0 : m0 + P // 4], src[:, m0 : m0 + P // 4])
-            if scalar_quarters < 4:
-                nc.vector.tensor_copy(dst[:, scalar_quarters * P // 4 :], src[:, scalar_quarters * P // 4 :])
+        def round_wg(b, a, piece, m0, m1, engine):
+            walk = "m t i" if engine is nc.scalar else "m t i"
+            dst = wg_bf[b, a][:].rearrange("p (t m i) -> p " + walk, t=PACK, i=PACK)[:, m0:m1]
+            src = wg_raw[b, a, piece][:].rearrange("p i (m t) -> p " + walk, t=PACK)[:, m0 - piece : m1 - piece]
+            if engine is nc.scalar:
+                nc.scalar.copy(dst, src)
+            else:
+                engine.tensor_copy(dst, src)
+
+        def round_piece(b, a, piece, scalar_m, vector_m, gpsimd_m=0):
+            for m0 in range(piece, piece + gpsimd_m, 16):
+                round_wg(b, a, piece, m0, m0 + 16, nc.gpsimd)
+            start = piece + gpsimd_m
+            for m0 in range(start, start + scalar_m, 32):
+                round_wg(b, a, piece, m0, min(m0 + 32, start + scalar_m), nc.scalar)
+            if vector_m:
+                round_wg(b, a, piece, start + scalar_m, start + scalar_m + vector_m, nc.vector)
+
+        def quantize_wg(b, a):
             wg_codes[b, a] = held(f"wg_codes{b}{a}", [P, PASS], U32)
             wg_planes[b, a] = held(f"wg_plane{b}{a}", [P, PASS], U8)
-            nc.vector.quantize_mx(out=wg_codes[b, a][:].bitcast(FP8X4), scales=wg_planes[b, a][:], in_=rounded[:])
+            nc.vector.quantize_mx(out=wg_codes[b, a][:].bitcast(FP8X4), scales=wg_planes[b, a][:], in_=wg_bf[b, a][:])
 
-        PER = HALF // CH
+        def up_bank(g):
+            return banks[g % PER]
 
-        def up(b, c, a):
+        def gate_bank(g):
+            return banks[PER + (g % PER if g < 12 else g % 2)]
+
+        def first_stage(bank, codes, scales, c, a):
             cols = slice(c % PER * CH, (c % PER + 1) * CH)
             for t in range(PACK):
                 nc.tensor.matmul_mx(
-                    banks[c % PER][:, t * CH : (t + 1) * CH],
-                    lhsT=wu[b, a][:, t * P : (t + 1) * P].bitcast(FP8X4),
-                    lhsT_scale=wu_planes[:, a, PASS * b + t * P : PASS * b + (t + 1) * P],
+                    bank[:, t * CH : (t + 1) * CH],
+                    lhsT=codes[:, t * P : (t + 1) * P].bitcast(FP8X4),
+                    lhsT_scale=scales[:, t * P : (t + 1) * P],
                     rhs=picked[c // PER, a][:, cols].bitcast(FP4X4),
-                    rhs_scale=picked_planes[:, a, c * CH : (c + 1) * CH],
+                    rhs_scale=planes[a][:, c * CH : (c + 1) * CH],
                     start=(a == 0 and t == 0),
                     stop=(a == 1 and t == PACK - 1),
                 )
 
-        def gate(b, c, a):
-            cols = slice(c % PER * CH, (c % PER + 1) * CH)
-            for t in range(PACK):
-                nc.tensor.matmul_mx(
-                    banks[PER + c % PER][:, t * CH : (t + 1) * CH],
-                    lhsT=wg_codes[b, a][:, t * P : (t + 1) * P].bitcast(FP8X4),
-                    lhsT_scale=wg_planes[b, a][:, t * P : (t + 1) * P],
-                    rhs=picked[c // PER, a][:, cols].bitcast(FP4X4),
-                    rhs_scale=picked_planes[:, a, c * CH : (c + 1) * CH],
-                    start=(a == 0 and t == 0),
-                    stop=(a == 1 and t == PACK - 1),
-                )
+        def up(g, a):
+            b, c = divmod(g, CHUNKS)
+            first_stage(up_bank(g), wu[b, a], planes[a][:, WU_AT + PASS * b : WU_AT + PASS * (b + 1)], c, a)
 
+        def gate(g, a):
+            b, c = divmod(g, CHUNKS)
+            first_stage(gate_bank(g), wg_codes[b, a][:], wg_planes[b, a][:], c, a)
+
+        pieces = ((0, 4), (4, 4), (8, 2), (10, 2), (12, 2), (14, 1), (15, 1))
         h_bf, h_codes, h_planes = {}, {}, {}
+        for g0 in range(0, 2 * CHUNKS, PER):
+            codes = held(f"h_codes{g0}", [P, HALF], U32, {0: "wg_bf10", 4: "wg_bf11"}.get(g0, ""))
+            scales = held(f"h_plane{g0}", [P, HALF], U8)
+            for g in range(g0, g0 + PER):
+                for count in range(1, g0 + PER - g + 1):
+                    cols = slice((g - g0) * CH, (g - g0 + count) * CH)
+                    h_codes[g, count], h_planes[g, count] = codes[:, cols], scales[:, cols]
+        for g0, count in pieces:
+            whole = held(f"h_bf{g0}", [P, count * CH, PACK], BF16, {10: "resid0", 14: "resid1"}.get(g0, ""))
+            for g in range(g0, g0 + count):
+                h_bf[g] = whole[:, (g - g0) * CH : (g - g0 + 1) * CH, :]
+            h_bf[g0, count] = whole[:]
 
-        def gated_product(b, c):
+        def gated_product(g):
             act = ring.tile([P, CH, PACK], F32, name="act")
-            nc.scalar.activation(act[:], banks[PER + c % PER][:].rearrange("p (t j) -> p j t", t=PACK), SILU)
-            dst = h_bf[b, c // PER][:, c % PER * CH : (c % PER + 1) * CH, :]
-            nc.vector.tensor_tensor(dst, banks[c % PER][:].rearrange("p (t j) -> p j t", t=PACK), act[:], MULT)
+            nc.scalar.activation(act[:], gate_bank(g)[:].rearrange("p (t j) -> p j t", t=PACK), SILU)
+            nc.vector.tensor_tensor(h_bf[g], up_bank(g)[:].rearrange("p (t j) -> p j t", t=PACK), act[:], MULT)
 
-        def quantize_h(b, half):
-            h_codes[b, half] = held(f"h_codes{b}{half}", [P, HALF], U32)
-            h_planes[b, half] = held(f"h_plane{b}{half}", [P, HALF], U8)
+        def quantize_h(piece):
             nc.vector.quantize_mx(
-                out=h_codes[b, half][:].bitcast(FP8X4),
-                scales=h_planes[b, half][:],
-                in_=h_bf[b, half][:].rearrange("p j t -> p (j t)"),
+                out=h_codes[piece].bitcast(FP8X4), scales=h_planes[piece], in_=h_bf[piece].rearrange("p j t -> p (j t)")
             )
 
-        def down(n, b, half):
-            cols = slice(n * P, (n + 1) * P)
+        def down(acc, n, b, key, first, last):
             tiers = (
-                (wd4[:, b, 2 * n * P : 2 * (n + 1) * P].bitcast(FP4X4), wd4_planes[:, b, cols]),
-                (wd8[:, b, cols].bitcast(FP8X4), wd8_planes[:, b, cols]),
+                (wd4[:, b, 2 * n * P : 2 * (n + 1) * P].bitcast(FP4X4), planes[b][:, WD4_AT + n * P : WD4_AT + (n + 1) * P]),
+                (wd8[:, b, n * P : (n + 1) * P].bitcast(FP8X4), planes[b][:, WD8_AT + n * P : WD8_AT + (n + 1) * P]),
             )
             for tier, (lhsT, lhsT_scale) in enumerate(tiers):
                 nc.tensor.matmul_mx(
-                    banks[PER + 2 * half + n][:],
+                    acc,
                     lhsT=lhsT,
                     lhsT_scale=lhsT_scale,
-                    rhs=h_codes[b, half][:].bitcast(FP8X4),
-                    rhs_scale=h_planes[b, half][:],
-                    start=(b == 0 and tier == 0),
-                    stop=(b == 1 and tier == 1),
+                    rhs=h_codes[key].bitcast(FP8X4),
+                    rhs_scale=h_planes[key],
+                    start=(first and tier == 0),
+                    stop=(last and tier == 1),
                 )
 
-        picked_resid = {}
+        picked_resid = [held(f"picked_resid{half}", [P, 2, HALF], F32) for half in range(2)]
 
-        def pick_resid(n):
-            picked_resid[n] = held(f"picked_resid{n}", [P, J], F32)
-            nc.vector.tensor_copy(picked_resid[n][:], resid[n][:].indirect(offsets[:]))
+        def pick_resid(n, half):
+            cols = slice(half * HALF // 16, (half + 1) * HALF // 16)
+            nc.vector.tensor_copy(picked_resid[half][:, n, :], resid[n][:].indirect(offsets[:, cols]))
 
-        def finish(n, half):
-            result = held(f"result{n}{half}", [P, HALF], F32)
-            nc.vector.tensor_tensor(result[:], banks[PER + 2 * half + n][:], picked_resid[n][:, half * HALF : (half + 1) * HALF], ADD)
-            nc.sync.dma_start(out[P * n : P * (n + 1), half * HALF : (half + 1) * HALF], result[:])
+        def finish(n, half, j0, j1, acc):
+            result = held(f"result{n}{half}{j0}", [P, j1 - j0], F32)
+            nc.vector.tensor_tensor(result[:], acc, picked_resid[half][:, n, j0:j1], ADD)
+            nc.sync.dma_start(out[P * n : P * (n + 1), half * HALF + j0 : half * HALF + j1], result[:])
 
-        order_wu(0, 0, 2)
-        order_wu_planes(0)
-        order_wu_planes(1)
         pick_words(0)
-        for a in range(2):
-            part_words(0, a, a + 1)
-        for b in range(2):
-            for a in range(2):
-                for c in range(PER):
-                    up(b, c, a)
-            if b == 0:
-                pick_words(1)
-                part_words(1, 0, 2)
-                prepare_wg(0, 0, 4)
-                prepare_wg(0, 1, 1)
-                order_wu(1, 0, 2)
-            for c in range(PER):
-                gate(b, c, 0)
-            if b == 1:
-                quantize_h(0, 0)
-                quantize_h(0, 1)
-                pick_resid(0)
-                pick_resid(1)
-            for half in range(2):
-                tag = "resid1" if (b, half) == (1, 1) else ""
-                h_bf[b, half] = held(f"h_bf{b}{half}", [P, HALF, PACK], BF16, tag)
-            for c in range(CHUNKS):
-                if c >= PER:
-                    gate(b, c, 0)
-                gate(b, c, 1)
-                if c >= PER:
-                    up(b, c, 0)
-                    up(b, c, 1)
-                gated_product(b, c)
-                if b == 1 and c == PER - 1:
-                    quantize_h(1, 0)
-            if b == 0:
-                prepare_wg(1, 0, 4)
-                prepare_wg(1, 1, 2)
-        quantize_h(1, 1)
-        for half in range(2):
+        part_words(0, 0, 1)
+        order_wu(0, 0, 1)
+        part_words(0, 1, 2)
+        order_wu(0, 1, 2)
+        for g in range(PER):
+            up(g, 0)
+        pick_words(1)
+        part_words(1, 0, 2)
+        round_piece(0, 0, 0, 64, 0)
+        round_piece(0, 0, P // 2, 64, 0)
+        quantize_wg(0, 0)
+        for g in range(PER):
+            gate(g, 0)
+        round_piece(0, 1, 0, 64, 0)
+        round_piece(0, 1, P // 2, 16, 48)
+        quantize_wg(0, 1)
+
+        def chunk(g):
+            if g >= PER:
+                gate(g, 0)
+            gate(g, 1)
+            if g >= PER:
+                up(g, 0)
+            up(g, 1)
+            gated_product(g)
+
+        for g in range(4):
+            chunk(g)
+        round_piece(1, 0, 0, 128, 0, 0)
+        round_piece(1, 1, 0, 32, 96, 0)
+        quantize_wg(1, 0)
+        quantize_wg(1, 1)
+        order_wu(1, 0, 2)
+        for g in range(4, CHUNKS):
+            chunk(g)
+
+        chunk(8)
+        quantize_h((0, 4))
+        chunk(9)
+        quantize_h((4, 4))
+        pick_resid(0, 0)
+        pick_resid(0, 1)
+        chunk(10)
+        quantize_h((8, 2))
+        chunk(11)
+        quantize_h((10, 2))
+        pick_resid(1, 0)
+        pick_resid(1, 1)
+        chunk(12)
+        chunk(13)
+        quantize_h((12, 2))
+        chunk(14)
+        quantize_h((14, 1))
+        chunk(15)
+        quantize_h((15, 1))
+        for n in range(2):
+            down(banks[6 + n][:], n, 0, (0, 4), True, False)
+            down(banks[6 + n][:], n, 1, (8, 4), False, True)
+            finish(n, 0, 0, HALF, banks[6 + n][:])
+        for n in range(2):
             for b in range(2):
-                for n in range(2):
-                    down(n, b, half)
-        for half in range(2):
-            finish(0, half)
-            finish(1, half)
+                for c in range(4, 7):
+                    down(banks[n][:, (c - 4) * CH : (c - 3) * CH], n, b, (8 * b + c, 1), (b, c) == (0, 4), (b, c) == (1, 6))
+            finish(n, 1, 0, 3 * CH, banks[n][:, 0 : 3 * CH])
+        for n in range(2):
+            for b in range(2):
+                down(banks[4][:, n * CH : (n + 1) * CH], n, b, (7 + 8 * b, 1), b == 0, b == 1)
+        last = held("last", [P, 2, CH], F32)
+        nc.vector.tensor_tensor(
+            last[:], banks[4][:, 0 : 2 * CH].rearrange("p (n j) -> p n j", n=2), picked_resid[1][:, :, 3 * CH : HALF], ADD
+        )
+        nc.sync.dma_start(out[:, J - CH : J].rearrange("(n p) j -> p n j", n=2), last[:])

@@ -25,6 +25,7 @@ CHUNKS = J // CH
 HALF = J // 2
 PER = HALF // CH
 LIVE = 96
+EARLY = J + PASS
 WU_AT, WD4_AT, WD8_AT, ROW = J, J + R, J + R + N, J + R + 2 * N
 
 
@@ -34,7 +35,6 @@ def tile_list_gmlpt_silu_res_resL_kernel(
     nc = tc.nc
     with ExitStack() as ctx:
         keep = ctx.enter_context(tc.tile_pool(name="keep", bufs=1))
-        ring = ctx.enter_context(tc.tile_pool(name="ring", bufs=CHUNKS))
         psum = ctx.enter_context(tc.psum_pool(name="psum", bufs=1))
 
         def held(name, shape, dtype, tag=""):
@@ -72,38 +72,39 @@ def tile_list_gmlpt_silu_res_resL_kernel(
         def load_rows(queue, dst, scales):
             queue.dma_start(dst.bitcast(I32), scales.rearrange("a q n -> (a q) n").bitcast(I32))
 
-        def place_rows(a):
+        def place_rows(a, c0, c1):
             for r in range(4):
-                nc.sync.dma_start(planes[a][r:P:32, :].bitcast(I32), rows[LIVE + 16 * a + r : LIVE + 16 * (a + 1) : 4, :].bitcast(I32))
+                nc.sync.dma_start(planes[a][r:P:32, c0:c1].bitcast(I32), rows[LIVE + 16 * a + r : LIVE + 16 * (a + 1) : 4, c0:c1].bitcast(I32))
 
         load_rows(nc.sync, table_planes[LIVE:P, :], tab_scales)
         nc.sync.dma_start(offsets[:], offs)
         load_rows(nc.scalar, wu_rows[LIVE:P, :], wu_scales)
         load_rows(nc.scalar, rows[LIVE:P, WD4_AT:WD8_AT], wd4_scales)
-        load_rows(nc.sync, rows[LIVE:P, WD8_AT:ROW], wd8_scales)
+        load_rows(nc.scalar, rows[LIVE:P, WD8_AT:ROW], wd8_scales)
         nc.sync.dma_start(table[:], tab_words[0].rearrange("p t e -> p (t e)").bitcast(I32))
         load_wu(0, 0, 2)
 
         warm = held("warm", [P, 2], F32)
         nc.gpsimd.memset(warm[:, 0:1], 0.0)
         nc.scalar.activation(warm[:, 1:2], warm[:, 0:1], SILU)
+
         nc.vector.tensor_copy(
             rows[:, WU_AT:WD4_AT].rearrange("p (b t g m) -> p b g t m", b=2, t=PACK, m=16),
             wu_rows[:].rearrange("p (b g m t) -> p b g t m", b=2, t=PACK, m=16),
         )
         nc.vector.tensor_copy(picked_rows[:], table_planes[:].indirect(offsets[:]))
         nc.vector.tensor_copy(rows[LIVE:P, 0:J].bitcast(I32), picked_rows[LIVE:P, :].bitcast(I32))
-        load_wg(0, 0, 0, P // 2)
-        place_rows(0)
-        load_wg(0, 0, P // 2, P)
-        load_wg(0, 1, 0, P // 2)
-        load_wg(0, 1, P // 2, P)
-        place_rows(1)
+        load_wg(0, 0, 0, P)
+        place_rows(0, 0, EARLY)
+        load_wg(0, 1, 0, P)
         load_wg(1, 0, 0, P)
+        place_rows(1, 0, EARLY)
         load_wg(1, 1, 0, P)
+        place_rows(0, EARLY, ROW)
         load_wu(1, 0, 2)
         nc.sync.dma_start(wd4[:].bitcast(I32), wd4_words.rearrange("a p w -> p a w").bitcast(I32))
         nc.sync.dma_start(wd8[:], wd8_words.rearrange("a p n i -> p a (n i)").bitcast(I32))
+        place_rows(1, EARLY, ROW)
         nc.sync.dma_start(resid[0][:], rT[0:P, :])
         nc.sync.dma_start(resid[1][:], rT[P : 2 * P, :])
 
@@ -136,9 +137,8 @@ def tile_list_gmlpt_silu_res_resL_kernel(
                 wg_bf[b, a] = held(f"wg_bf{b}{a}", [P, PACK * PASS], BF16)
 
         def round_wg(b, a, piece, m0, m1, engine):
-            walk = "m t i" if engine is nc.scalar else "m t i"
-            dst = wg_bf[b, a][:].rearrange("p (t m i) -> p " + walk, t=PACK, i=PACK)[:, m0:m1]
-            src = wg_raw[b, a, piece][:].rearrange("p i (m t) -> p " + walk, t=PACK)[:, m0 - piece : m1 - piece]
+            dst = wg_bf[b, a][:].rearrange("p (t m h i) -> p m h t i", t=PACK, h=2, i=2)[:, m0:m1]
+            src = wg_raw[b, a, piece][:].rearrange("p (h i) (m t) -> p m h t i", h=2, t=PACK)[:, m0 - piece : m1 - piece]
             if engine is nc.scalar:
                 nc.scalar.copy(dst, src)
             else:
@@ -185,7 +185,6 @@ def tile_list_gmlpt_silu_res_resL_kernel(
             b, c = divmod(g, CHUNKS)
             first_stage(gate_bank(g), wg_codes[b, a][:], wg_planes[b, a][:], c, a)
 
-        pieces = ((0, 4), (4, 4), (8, 2), (10, 2), (12, 2), (14, 1), (15, 1))
         h_bf, h_codes, h_planes = {}, {}, {}
         for g0 in range(0, 2 * CHUNKS, PER):
             codes = held(f"h_codes{g0}", [P, HALF], U32, {0: "wg_bf10", 4: "wg_bf11"}.get(g0, ""))
@@ -194,16 +193,27 @@ def tile_list_gmlpt_silu_res_resL_kernel(
                 for count in range(1, g0 + PER - g + 1):
                     cols = slice((g - g0) * CH, (g - g0 + count) * CH)
                     h_codes[g, count], h_planes[g, count] = codes[:, cols], scales[:, cols]
-        for g0, count in pieces:
-            whole = held(f"h_bf{g0}", [P, count * CH, PACK], BF16, {10: "resid0", 14: "resid1"}.get(g0, ""))
+        for g0, count in ((0, 4), (4, 4), (8, 2), (10, 2), (12, 4)):
+            whole = held(f"h_bf{g0}", [P, count * CH, PACK], BF16, {0: "wg_raw100", 10: "resid0", 99: "resid1"}.get(g0, ""))
             for g in range(g0, g0 + count):
                 h_bf[g] = whole[:, (g - g0) * CH : (g - g0 + 1) * CH, :]
-            h_bf[g0, count] = whole[:]
+                for part in range(1, g0 + count - g + 1):
+                    h_bf[g, part] = whole[:, (g - g0) * CH : (g - g0 + part) * CH, :]
+
+        acts = {}
 
         def gated_product(g):
-            act = ring.tile([P, CH, PACK], F32, name="act")
-            nc.scalar.activation(act[:], gate_bank(g)[:].rearrange("p (t j) -> p j t", t=PACK), SILU)
-            nc.vector.tensor_tensor(h_bf[g], up_bank(g)[:].rearrange("p (t j) -> p j t", t=PACK), act[:], MULT)
+            if g % PER == 0:
+                acts[g // PER] = held(f"act{g}", [P, PER, CH, PACK], F32, "wg_raw110" if g == PER else f"act{g // PER % 2}")
+            act = acts[g // PER][:, g % PER]
+            nc.scalar.activation(act, gate_bank(g)[:].rearrange("p (t j) -> p j t", t=PACK), SILU)
+            ups = up_bank(g)[:].rearrange("p (t j) -> p j t", t=PACK)
+            if g in (4, 12,):
+                moved = held(f"ups{g}", [P, CH, PACK], F32)
+                nc.scalar.copy(moved[:], ups)
+                nc.gpsimd.tensor_tensor(h_bf[g], moved[:], act, MULT)
+            else:
+                nc.vector.tensor_tensor(h_bf[g], ups, act, MULT)
 
         def quantize_h(piece):
             nc.vector.quantize_mx(
@@ -226,16 +236,19 @@ def tile_list_gmlpt_silu_res_resL_kernel(
                     stop=(last and tier == 1),
                 )
 
-        picked_resid = [held(f"picked_resid{half}", [P, 2, HALF], F32) for half in range(2)]
+        picked_resid = held("picked_resid", [P, J], F32)
 
-        def pick_resid(n, half):
-            cols = slice(half * HALF // 16, (half + 1) * HALF // 16)
-            nc.vector.tensor_copy(picked_resid[half][:, n, :], resid[n][:].indirect(offsets[:, cols]))
-
-        def finish(n, half, j0, j1, acc):
-            result = held(f"result{n}{half}{j0}", [P, j1 - j0], F32)
-            nc.vector.tensor_tensor(result[:], acc, picked_resid[half][:, n, j0:j1], ADD)
-            nc.sync.dma_start(out[P * n : P * (n + 1), half * HALF + j0 : half * HALF + j1], result[:])
+        def finish(n, half, acc):
+            cols = slice(half * HALF, (half + 1) * HALF)
+            result = held(f"result{n}{half}", [P, HALF], F32, "sums0" if (n, half) == (0, 1) else "")
+            if n == 0:
+                nc.vector.tensor_tensor(result[:], acc, picked_resid[:, cols], ADD)
+            else:
+                sums = held(f"sums{half}", [P, HALF], F32)
+                nc.scalar.copy(sums[:], acc)
+                listed = offsets[:, half * HALF // 16 : (half + 1) * HALF // 16]
+                nc.vector.tensor_tensor(result[:], resid[1][:].indirect(listed), sums[:], ADD)
+            nc.sync.dma_start(out[P * n : P * (n + 1), cols], result[:])
 
         pick_words(0)
         part_words(0, 0, 1)
@@ -246,13 +259,11 @@ def tile_list_gmlpt_silu_res_resL_kernel(
             up(g, 0)
         pick_words(1)
         part_words(1, 0, 2)
-        round_piece(0, 0, 0, 64, 0)
-        round_piece(0, 0, P // 2, 64, 0)
+        round_piece(0, 0, 0, 96, 32)
         quantize_wg(0, 0)
         for g in range(PER):
             gate(g, 0)
-        round_piece(0, 1, 0, 64, 0)
-        round_piece(0, 1, P // 2, 16, 48)
+        round_piece(0, 1, 0, 48, 80)
         quantize_wg(0, 1)
 
         def chunk(g):
@@ -266,8 +277,8 @@ def tile_list_gmlpt_silu_res_resL_kernel(
 
         for g in range(4):
             chunk(g)
-        round_piece(1, 0, 0, 128, 0, 0)
-        round_piece(1, 1, 0, 32, 96, 0)
+        round_piece(1, 0, 0, 32, 96, 0)
+        round_piece(1, 1, 0, 128, 0, 0)
         quantize_wg(1, 0)
         quantize_wg(1, 1)
         order_wu(1, 0, 2)
@@ -278,35 +289,18 @@ def tile_list_gmlpt_silu_res_resL_kernel(
         quantize_h((0, 4))
         chunk(9)
         quantize_h((4, 4))
-        pick_resid(0, 0)
-        pick_resid(0, 1)
+        nc.vector.tensor_copy(picked_resid[:], resid[0][:].indirect(offsets[:]))
         chunk(10)
         quantize_h((8, 2))
         chunk(11)
         quantize_h((10, 2))
-        pick_resid(1, 0)
-        pick_resid(1, 1)
-        chunk(12)
-        chunk(13)
-        quantize_h((12, 2))
-        chunk(14)
-        quantize_h((14, 1))
-        chunk(15)
-        quantize_h((15, 1))
-        for n in range(2):
-            down(banks[6 + n][:], n, 0, (0, 4), True, False)
-            down(banks[6 + n][:], n, 1, (8, 4), False, True)
-            finish(n, 0, 0, HALF, banks[6 + n][:])
-        for n in range(2):
+        sum_banks = ((banks[6], banks[7]), (banks[3], banks[2]))
+        for g in range(12, 16):
+            chunk(g)
+        quantize_h((12, 4))
+        for half in range(2):
             for b in range(2):
-                for c in range(4, 7):
-                    down(banks[n][:, (c - 4) * CH : (c - 3) * CH], n, b, (8 * b + c, 1), (b, c) == (0, 4), (b, c) == (1, 6))
-            finish(n, 1, 0, 3 * CH, banks[n][:, 0 : 3 * CH])
-        for n in range(2):
-            for b in range(2):
-                down(banks[4][:, n * CH : (n + 1) * CH], n, b, (7 + 8 * b, 1), b == 0, b == 1)
-        last = held("last", [P, 2, CH], F32)
-        nc.vector.tensor_tensor(
-            last[:], banks[4][:, 0 : 2 * CH].rearrange("p (n j) -> p n j", n=2), picked_resid[1][:, :, 3 * CH : HALF], ADD
-        )
-        nc.sync.dma_start(out[:, J - CH : J].rearrange("(n p) j -> p n j", n=2), last[:])
+                for n in (1, 0):
+                    down(sum_banks[half][n][:], n, b, (8 * b + 4 * half, 4), b == 0, b == 1)
+            for n in (1, 0):
+                finish(n, half, sum_banks[half][n][:])

@@ -25,7 +25,6 @@ CHUNKS = J // CH
 HALF = J // 2
 PER = HALF // CH
 LIVE = 96
-EARLY = J + PASS
 WU_AT, WD4_AT, WD8_AT, ROW = J, J + R, J + R + N, J + R + 2 * N
 
 
@@ -72,9 +71,9 @@ def tile_list_gmlpt_silu_res_resL_kernel(
         def load_rows(queue, dst, scales):
             queue.dma_start(dst.bitcast(I32), scales.rearrange("a q n -> (a q) n").bitcast(I32))
 
-        def place_rows(a, c0, c1):
+        def place_rows(a):
             for r in range(4):
-                nc.sync.dma_start(planes[a][r:P:32, c0:c1].bitcast(I32), rows[LIVE + 16 * a + r : LIVE + 16 * (a + 1) : 4, c0:c1].bitcast(I32))
+                nc.sync.dma_start(planes[a][r:P:32, :].bitcast(I32), rows[LIVE + 16 * a + r : LIVE + 16 * (a + 1) : 4, :].bitcast(I32))
 
         load_rows(nc.sync, table_planes[LIVE:P, :], tab_scales)
         nc.sync.dma_start(offsets[:], offs)
@@ -95,16 +94,14 @@ def tile_list_gmlpt_silu_res_resL_kernel(
         nc.vector.tensor_copy(picked_rows[:], table_planes[:].indirect(offsets[:]))
         nc.vector.tensor_copy(rows[LIVE:P, 0:J].bitcast(I32), picked_rows[LIVE:P, :].bitcast(I32))
         load_wg(0, 0, 0, P)
-        place_rows(0, 0, EARLY)
+        place_rows(0)
         load_wg(0, 1, 0, P)
+        place_rows(1)
         load_wg(1, 0, 0, P)
-        place_rows(1, 0, EARLY)
         load_wg(1, 1, 0, P)
-        place_rows(0, EARLY, ROW)
         load_wu(1, 0, 2)
         nc.sync.dma_start(wd4[:].bitcast(I32), wd4_words.rearrange("a p w -> p a w").bitcast(I32))
         nc.sync.dma_start(wd8[:], wd8_words.rearrange("a p n i -> p a (n i)").bitcast(I32))
-        place_rows(1, EARLY, ROW)
         nc.sync.dma_start(resid[0][:], rT[0:P, :])
         nc.sync.dma_start(resid[1][:], rT[P : 2 * P, :])
 
@@ -154,7 +151,7 @@ def tile_list_gmlpt_silu_res_resL_kernel(
                 round_wg(b, a, piece, start + scalar_m, start + scalar_m + vector_m, nc.vector)
 
         def quantize_wg(b, a):
-            wg_codes[b, a] = held(f"wg_codes{b}{a}", [P, PASS], U32)
+            wg_codes[b, a] = held(f"wg_codes{b}{a}", [P, PASS], U32, "act0" if (b, a) == (1, 0) else "")
             wg_planes[b, a] = held(f"wg_plane{b}{a}", [P, PASS], U8)
             nc.vector.quantize_mx(out=wg_codes[b, a][:].bitcast(FP8X4), scales=wg_planes[b, a][:], in_=wg_bf[b, a][:])
 
@@ -204,11 +201,11 @@ def tile_list_gmlpt_silu_res_resL_kernel(
 
         def gated_product(g):
             if g % PER == 0:
-                acts[g // PER] = held(f"act{g}", [P, PER, CH, PACK], F32, "wg_raw110" if g == PER else f"act{g // PER % 2}")
+                acts[g // PER] = held(f"act{g}", [P, PER, CH, PACK], F32, "wg_raw110" if g == PER else "")
             act = acts[g // PER][:, g % PER]
             nc.scalar.activation(act, gate_bank(g)[:].rearrange("p (t j) -> p j t", t=PACK), SILU)
             ups = up_bank(g)[:].rearrange("p (t j) -> p j t", t=PACK)
-            if g in (4, 12,):
+            if g in (4, 8, 12,):
                 moved = held(f"ups{g}", [P, CH, PACK], F32)
                 nc.scalar.copy(moved[:], ups)
                 nc.gpsimd.tensor_tensor(h_bf[g], moved[:], act, MULT)
@@ -275,10 +272,10 @@ def tile_list_gmlpt_silu_res_resL_kernel(
             up(g, 1)
             gated_product(g)
 
+        round_piece(1, 0, 0, 0, 128, 0)
         for g in range(4):
             chunk(g)
-        round_piece(1, 0, 0, 32, 96, 0)
-        round_piece(1, 1, 0, 128, 0, 0)
+        round_piece(1, 1, 0, 96, 32, 0)
         quantize_wg(1, 0)
         quantize_wg(1, 1)
         order_wu(1, 0, 2)

@@ -114,19 +114,8 @@ def tile_list_gmlpt_silu_res_resL_kernel(
             for a in range(a0, a1):
                 wu[b, a] = ordered[:, a - a0, :]
 
-        pairs, picked = {}, {}
-
-        def pick_words(half):
-            pairs[half] = held(f"pairs{half}", [P, HALF], U32, "pairs")
-            cols = slice(half * HALF // 16, (half + 1) * HALF // 16)
-            nc.vector.tensor_copy(pairs[half][:], table[:].bitcast(U32).indirect(offsets[:, cols]))
-
-        def part_words(half, a0, a1):
-            parted = held(f"picked{half}{a0}", [P, a1 - a0, HALF], U16)
-            both = pairs[half][:].bitcast(U16).rearrange("p (j a) -> p a j", a=2)
-            nc.vector.tensor_copy(parted[:], both[:, a0:a1, :])
-            for a in range(a0, a1):
-                picked[half, a] = parted[:, a - a0, :]
+        pairs = held("pairs", [P, J], U32)
+        picked = [held(f"picked{a}", [P, J], U16) for a in range(2)]
 
         wg_bf, wg_codes, wg_planes = {}, {}, {}
         for b in range(2):
@@ -162,14 +151,14 @@ def tile_list_gmlpt_silu_res_resL_kernel(
             return banks[PER + (g % PER if g < 12 else g % 2)]
 
         def first_stage(bank, codes, scales, c, a):
-            cols = slice(c % PER * CH, (c % PER + 1) * CH)
+            cols = slice(c * CH, (c + 1) * CH)
             for t in range(PACK):
                 nc.tensor.matmul_mx(
                     bank[:, t * CH : (t + 1) * CH],
                     lhsT=codes[:, t * P : (t + 1) * P].bitcast(FP8X4),
                     lhsT_scale=scales[:, t * P : (t + 1) * P],
-                    rhs=picked[c // PER, a][:, cols].bitcast(FP4X4),
-                    rhs_scale=planes[a][:, c * CH : (c + 1) * CH],
+                    rhs=picked[a][:, cols].bitcast(FP4X4),
+                    rhs_scale=planes[a][:, cols],
                     start=(a == 0 and t == 0),
                     stop=(a == 1 and t == PACK - 1),
                 )
@@ -190,8 +179,8 @@ def tile_list_gmlpt_silu_res_resL_kernel(
                 for count in range(1, g0 + PER - g + 1):
                     cols = slice((g - g0) * CH, (g - g0 + count) * CH)
                     h_codes[g, count], h_planes[g, count] = codes[:, cols], scales[:, cols]
-        for g0, count in ((0, 4), (4, 4), (8, 2), (10, 2), (12, 4)):
-            whole = held(f"h_bf{g0}", [P, count * CH, PACK], BF16, {0: "wg_raw100", 10: "resid0", 99: "resid1"}.get(g0, ""))
+        for g0, count in ((0, 4), (4, 4), (8, 4), (12, 4)):
+            whole = held(f"h_bf{g0}", [P, count * CH, PACK], BF16, {0: "wg_raw100", 8: "resid0"}.get(g0, ""))
             for g in range(g0, g0 + count):
                 h_bf[g] = whole[:, (g - g0) * CH : (g - g0 + 1) * CH, :]
                 for part in range(1, g0 + count - g + 1):
@@ -247,16 +236,13 @@ def tile_list_gmlpt_silu_res_resL_kernel(
                 nc.vector.tensor_tensor(result[:], resid[1][:].indirect(listed), sums[:], ADD)
             nc.sync.dma_start(out[P * n : P * (n + 1), cols], result[:])
 
-        pick_words(0)
-        part_words(0, 0, 1)
-        order_wu(0, 0, 1)
-        part_words(0, 1, 2)
-        order_wu(0, 1, 2)
+        nc.vector.tensor_copy(pairs[:], table[:].bitcast(U32).indirect(offsets[:]))
+        order_wu(0, 0, 2)
+        for a in range(2):
+            nc.vector.tensor_copy(picked[a][:], pairs[:].bitcast(U16).rearrange("p (j a) -> p a j", a=2)[:, a, :])
         for g in range(PER):
             up(g, 0)
-        pick_words(1)
-        part_words(1, 0, 2)
-        round_piece(0, 0, 0, 96, 32)
+        round_piece(0, 0, 0, 128, 0)
         quantize_wg(0, 0)
         for g in range(PER):
             gate(g, 0)
@@ -275,22 +261,19 @@ def tile_list_gmlpt_silu_res_resL_kernel(
         round_piece(1, 0, 0, 0, 128, 0)
         for g in range(4):
             chunk(g)
-        round_piece(1, 1, 0, 96, 32, 0)
+        round_piece(1, 1, 0, 96, 0, 32)
         quantize_wg(1, 0)
         quantize_wg(1, 1)
         order_wu(1, 0, 2)
         for g in range(4, CHUNKS):
             chunk(g)
 
-        chunk(8)
         quantize_h((0, 4))
-        chunk(9)
         quantize_h((4, 4))
         nc.vector.tensor_copy(picked_resid[:], resid[0][:].indirect(offsets[:]))
-        chunk(10)
-        quantize_h((8, 2))
-        chunk(11)
-        quantize_h((10, 2))
+        for g in range(8, 12):
+            chunk(g)
+        quantize_h((8, 4))
         sum_banks = ((banks[6], banks[7]), (banks[3], banks[2]))
         for g in range(12, 16):
             chunk(g)

@@ -249,7 +249,44 @@ def tile_list_gmlpt_silu_res_resL_kernel(
         round_piece(0, 1, 0, 48, 80)
         quantize_wg(0, 1)
 
+        def wide_gate(g0):
+            b, half = divmod(g0 // PER, 2)
+            acts[g0 // PER] = held(f"act{g0}", [P, PACK, HALF], F32, "wg_raw110" if g0 == PER else "")
+            for t in range(PACK):
+                for a in range(2):
+                    nc.tensor.matmul_mx(
+                        banks[PER + t][:],
+                        lhsT=wg_codes[b, a][:, t * P : (t + 1) * P].bitcast(FP8X4),
+                        lhsT_scale=wg_planes[b, a][:, t * P : (t + 1) * P],
+                        rhs=picked[a][:, half * HALF : (half + 1) * HALF].bitcast(FP4X4),
+                        rhs_scale=planes[a][:, half * HALF : (half + 1) * HALF],
+                        start=(a == 0),
+                        stop=(a == 1),
+                    )
+                nc.scalar.activation(acts[g0 // PER][:, t, :], banks[PER + t][:], SILU)
+
+        def wide_product(g):
+            act = acts[g // PER][:, :, g % PER * CH : (g % PER + 1) * CH]
+            if g % PER == 0:
+                moved = held(f"ups{g}", [P, CH, PACK], F32)
+                nc.scalar.copy(moved[:], up_bank(g)[:].rearrange("p (t j) -> p j t", t=PACK))
+                nc.gpsimd.tensor_tensor(h_bf[g], moved[:], act.rearrange("p t j -> p j t"), MULT)
+            else:
+                nc.vector.tensor_tensor(
+                    h_bf[g].rearrange("p (j e) t -> p j t e", e=2),
+                    up_bank(g)[:].rearrange("p (t j e) -> p j t e", t=PACK, e=2),
+                    act.rearrange("p t (j e) -> p j t e", e=2),
+                    MULT,
+                )
+
         def chunk(g):
+            if g // PER in (2, 3,):
+                if g % PER == 0:
+                    wide_gate(g)
+                up(g, 0)
+                up(g, 1)
+                wide_product(g)
+                return
             if g >= PER:
                 gate(g, 0)
             gate(g, 1)

@@ -118,12 +118,13 @@ def tile_list_gmlpt_silu_res_resL_kernel(
         picked = [held(f"picked{a}", [P, J], U16) for a in range(2)]
 
         wg_bf, wg_codes, wg_planes = {}, {}, {}
-        for b in range(2):
-            for a in range(2):
-                wg_bf[b, a] = held(f"wg_bf{b}{a}", [P, PACK * PASS], BF16)
+        span_bf = held("wg_bf1", [P, 2, PACK * PASS], BF16)
+        for a in range(2):
+            wg_bf[0, a] = held(f"wg_bf0{a}", [P, PACK * PASS], BF16)[:]
+            wg_bf[1, a] = span_bf[:, a, :]
 
         def round_wg(b, a, piece, m0, m1, engine):
-            dst = wg_bf[b, a][:].rearrange("p (t m h i) -> p m h t i", t=PACK, h=2, i=2)[:, m0:m1]
+            dst = wg_bf[b, a].rearrange("p (t m h i) -> p m h t i", t=PACK, h=2, i=2)[:, m0:m1]
             src = wg_raw[b, a, piece][:].rearrange("p (h i) (m t) -> p m h t i", h=2, t=PACK)[:, m0 - piece : m1 - piece]
             if engine is nc.scalar:
                 nc.scalar.copy(dst, src)
@@ -139,10 +140,13 @@ def tile_list_gmlpt_silu_res_resL_kernel(
             if vector_m:
                 round_wg(b, a, piece, start + scalar_m, start + scalar_m + vector_m, nc.vector)
 
-        def quantize_wg(b, a):
-            wg_codes[b, a] = held(f"wg_codes{b}{a}", [P, PASS], U32, "act0" if (b, a) == (1, 0) else "")
-            wg_planes[b, a] = held(f"wg_plane{b}{a}", [P, PASS], U8)
-            nc.vector.quantize_mx(out=wg_codes[b, a][:].bitcast(FP8X4), scales=wg_planes[b, a][:], in_=wg_bf[b, a][:])
+        def quantize_wg(b, a0, a1, src):
+            codes = held(f"wg_codes{b}{a0}", [P, (a1 - a0) * PASS], U32)
+            scales = held(f"wg_plane{b}{a0}", [P, (a1 - a0) * PASS], U8)
+            nc.vector.quantize_mx(out=codes[:].bitcast(FP8X4), scales=scales[:], in_=src)
+            for a in range(a0, a1):
+                cols = slice((a - a0) * PASS, (a - a0 + 1) * PASS)
+                wg_codes[b, a], wg_planes[b, a] = codes[:, cols], scales[:, cols]
 
         def up_bank(g):
             return banks[g % PER]
@@ -169,24 +173,26 @@ def tile_list_gmlpt_silu_res_resL_kernel(
 
         def gate(g, a):
             b, c = divmod(g, CHUNKS)
-            first_stage(gate_bank(g), wg_codes[b, a][:], wg_planes[b, a][:], c, a)
+            first_stage(gate_bank(g), wg_codes[b, a], wg_planes[b, a], c, a)
 
         h_bf, h_codes, h_planes = {}, {}, {}
-        for g0 in range(0, 2 * CHUNKS, PER):
-            codes = held(f"h_codes{g0}", [P, HALF], U32, {0: "wg_bf10", 4: "wg_bf11"}.get(g0, ""))
-            scales = held(f"h_plane{g0}", [P, HALF], U8)
-            for g in range(g0, g0 + PER):
-                for count in range(1, g0 + PER - g + 1):
-                    cols = slice((g - g0) * CH, (g - g0 + count) * CH)
-                    h_codes[g, count], h_planes[g, count] = codes[:, cols], scales[:, cols]
-        for g0, count in ((0, 4), (4, 4), (8, 4), (12, 4)):
-            whole = held(f"h_bf{g0}", [P, count * CH, PACK], BF16, {0: "wg_raw100", 8: "resid0"}.get(g0, ""))
+        for g0, count in ((0, 8), (8, 4), (12, 4)):
+            codes = held(f"h_codes{g0}", [P, count * CH], U32, "wg_bf1" if g0 == 0 else "")
+            scales = held(f"h_plane{g0}", [P, count * CH], U8)
+            whole = held(f"h_bf{g0}", [P, count * CH, PACK], BF16, "wg_raw100" if g0 == 0 else "")
             for g in range(g0, g0 + count):
                 h_bf[g] = whole[:, (g - g0) * CH : (g - g0 + 1) * CH, :]
                 for part in range(1, g0 + count - g + 1):
-                    h_bf[g, part] = whole[:, (g - g0) * CH : (g - g0 + part) * CH, :]
+                    cols = slice((g - g0) * CH, (g - g0 + part) * CH)
+                    h_codes[g, part], h_planes[g, part], h_bf[g, part] = codes[:, cols], scales[:, cols], whole[:, cols, :]
 
         acts = {}
+
+        emptied = {}
+
+        def empty_bank(g):
+            emptied[g] = held(f"ups{g}", [P, CH, PACK], F32)
+            nc.scalar.copy(emptied[g][:], up_bank(g)[:].rearrange("p (t j) -> p j t", t=PACK))
 
         def gated_product(g):
             if g % PER == 0:
@@ -194,10 +200,10 @@ def tile_list_gmlpt_silu_res_resL_kernel(
             act = acts[g // PER][:, g % PER]
             nc.scalar.activation(act, gate_bank(g)[:].rearrange("p (t j) -> p j t", t=PACK), SILU)
             ups = up_bank(g)[:].rearrange("p (t j) -> p j t", t=PACK)
-            if g in (4, 8, 12,):
-                moved = held(f"ups{g}", [P, CH, PACK], F32)
-                nc.scalar.copy(moved[:], ups)
-                nc.gpsimd.tensor_tensor(h_bf[g], moved[:], act, MULT)
+            if g % PER == 0:
+                if g:
+                    empty_bank(g)
+                nc.gpsimd.tensor_tensor(h_bf[g], emptied[g][:], act, MULT)
             else:
                 nc.vector.tensor_tensor(h_bf[g], ups, act, MULT)
 
@@ -222,18 +228,20 @@ def tile_list_gmlpt_silu_res_resL_kernel(
                     stop=(last and tier == 1),
                 )
 
-        picked_resid = held("picked_resid", [P, J], F32)
+        picked_resid = held("picked_resid", [P, HALF], F32)
+
+        def listed(half):
+            return offsets[:, half * HALF // 16 : (half + 1) * HALF // 16]
 
         def finish(n, half, acc):
             cols = slice(half * HALF, (half + 1) * HALF)
-            result = held(f"result{n}{half}", [P, HALF], F32, "sums0" if (n, half) == (0, 1) else "")
-            if n == 0:
-                nc.vector.tensor_tensor(result[:], acc, picked_resid[:, cols], ADD)
+            result = held(f"result{n}{half}", [P, HALF], F32, {(0, 0): "h_bf12", (0, 1): "sums11"}.get((n, half), ""))
+            if (n, half) == (0, 1):
+                nc.vector.tensor_tensor(result[:], acc, picked_resid[:], ADD)
             else:
-                sums = held(f"sums{half}", [P, HALF], F32)
+                sums = held(f"sums{n}{half}", [P, HALF], F32)
                 nc.scalar.copy(sums[:], acc)
-                listed = offsets[:, half * HALF // 16 : (half + 1) * HALF // 16]
-                nc.vector.tensor_tensor(result[:], resid[1][:].indirect(listed), sums[:], ADD)
+                nc.vector.tensor_tensor(result[:], resid[n][:].indirect(listed(half)), sums[:], ADD)
             nc.sync.dma_start(out[P * n : P * (n + 1), cols], result[:])
 
         nc.vector.tensor_copy(pairs[:], table[:].bitcast(U32).indirect(offsets[:]))
@@ -243,11 +251,14 @@ def tile_list_gmlpt_silu_res_resL_kernel(
         for g in range(PER):
             up(g, 0)
         round_piece(0, 0, 0, 128, 0)
-        quantize_wg(0, 0)
+        quantize_wg(0, 0, 1, wg_bf[0, 0])
         for g in range(PER):
             gate(g, 0)
-        round_piece(0, 1, 0, 48, 80)
-        quantize_wg(0, 1)
+        round_piece(0, 1, 0, 80, 48)
+        quantize_wg(0, 1, 2, wg_bf[0, 1])
+        for g in range(PER):
+            up(g, 1)
+        empty_bank(0)
 
         def wide_gate(g0):
             b, half = divmod(g0 // PER, 2)
@@ -292,32 +303,29 @@ def tile_list_gmlpt_silu_res_resL_kernel(
             gate(g, 1)
             if g >= PER:
                 up(g, 0)
-            up(g, 1)
+                up(g, 1)
             gated_product(g)
 
         round_piece(1, 0, 0, 0, 128, 0)
         for g in range(4):
             chunk(g)
         round_piece(1, 1, 0, 96, 0, 32)
-        quantize_wg(1, 0)
-        quantize_wg(1, 1)
+        quantize_wg(1, 0, 2, span_bf[:].rearrange("p a c -> p (a c)"))
         order_wu(1, 0, 2)
         for g in range(4, CHUNKS):
             chunk(g)
 
-        quantize_h((0, 4))
-        quantize_h((4, 4))
-        nc.vector.tensor_copy(picked_resid[:], resid[0][:].indirect(offsets[:]))
+        quantize_h((0, 8))
         for g in range(8, 12):
             chunk(g)
         quantize_h((8, 4))
-        sum_banks = ((banks[6], banks[7]), (banks[3], banks[2]))
+        nc.vector.tensor_copy(picked_resid[:], resid[0][:].indirect(listed(1)))
         for g in range(12, 16):
             chunk(g)
         quantize_h((12, 4))
         for half in range(2):
-            for b in range(2):
-                for n in (1, 0):
-                    down(sum_banks[half][n][:], n, b, (8 * b + 4 * half, 4), b == 0, b == 1)
-            for n in (1, 0):
-                finish(n, half, sum_banks[half][n][:])
+            for turn, n in enumerate((half, 1 - half)):
+                acc = banks[PER + 2 * half + turn][:]
+                for step, b in enumerate((turn, 1 - turn)):
+                    down(acc, n, b, (8 * b + 4 * half, 4), step == 0, step == 1)
+                finish(n, half, acc)

@@ -24,8 +24,14 @@ CH = 128
 CHUNKS = J // CH
 HALF = J // 2
 PER = HALF // CH
-LIVE = 96
-WU_AT, WD4_AT, WD8_AT, ROW = J, J + R, J + R + N, J + R + 2 * N
+ROWS = 16
+LISTED = 16
+STAGE = P - 2 * ROWS
+WU_AT, ROW = J, J + R
+
+ROUNDING = {(0, 0): (0, 96), (0, 1): (0, 80), (1, 0): (0, 0), (1, 1): (32, 64)}
+SCALAR_STEP = 32
+GPSIMD_STEP = 16
 
 
 def tile_list_gmlpt_silu_res_resL_kernel(
@@ -36,296 +42,292 @@ def tile_list_gmlpt_silu_res_resL_kernel(
         keep = ctx.enter_context(tc.tile_pool(name="keep", bufs=1))
         psum = ctx.enter_context(tc.psum_pool(name="psum", bufs=1))
 
-        def held(name, shape, dtype, tag=""):
-            return keep.tile(shape, dtype, name=name, tag=tag or name, align_bytes=64)
+        def held(name, shape, dtype, after=""):
+            return keep.tile(shape, dtype, name=name, tag=after or name, align_bytes=64)
 
-        offsets = keep.tile([P, J // 16], U16, name="offsets")
+        offsets = keep.tile([P, J // LISTED], U16, name="offsets")
         table = held("table", [P, T], I32)
-        table_planes = held("table_planes", [P, T], U8)
+        table_rows = held("table_rows", [P, T], U8)
         picked_rows = held("picked_rows", [P, J], U8)
         wu_rows = held("wu_rows", [P, R], U8)
         rows = held("rows", [P, ROW], U8)
         planes = [held(f"planes{a}", [P, ROW], U8) for a in range(2)]
+        wd_rows = held("wd_rows", [P, 2, 2, N], U8)
+        wd_planes = held("wd_planes", [P, 2, 2, N], U8)
         wd4 = held("wd4", [P, 2, 2 * N], U8)
         wd8 = held("wd8", [P, 2, N], I32)
         resid = [held(f"resid{n}", [P, T], F32) for n in range(2)]
-        wu_raw, wu, wg_raw = {}, {}, {}
-        banks = [psum.tile([P, PACK * CH], F32, name=f"bank{i}") for i in range(8)]
+        banks = [psum.tile([P, PACK * CH], F32, name=f"bank{i}") for i in range(2 * PER)]
+        up_banks, gate_banks = banks[:PER], banks[PER:]
 
-        plane_words = table_planes[:].bitcast(I32)
-        nc.gpsimd.memset(plane_words[0:LIVE, :], 0)
-        nc.vector.memset(wu_rows[0:LIVE, :].bitcast(I32), 0)
+        nc.gpsimd.memset(table_rows[:].bitcast(I32)[0:STAGE, :], 0)
+        nc.gpsimd.memset(wd_planes[:].bitcast(I32), 0)
+        nc.vector.memset(wu_rows[0:STAGE, :].bitcast(I32), 0)
         for a in range(2):
             nc.vector.memset(planes[a][:].bitcast(I32), 0)
 
-        def load_wu(b, a0, a1):
-            wu_raw[b, a0] = held(f"wu_raw{b}{a0}", [P, a1 - a0, PASS], I32)
-            src = wu_words[a0:a1].rearrange("a p r i -> p a (r i)")[:, :, 4 * PASS * b : 4 * PASS * (b + 1)]
-            nc.sync.dma_start(wu_raw[b, a0][:], src.bitcast(I32))
+        wu_raw, wg_raw = {}, {}
 
-        def load_wg(b, a, m0, m1):
-            wg_raw[b, a, m0] = held(f"wg_raw{b}{a}{m0}", [P, PACK, PACK * (m1 - m0)], F32)
-            src = wg[PASS * a : PASS * (a + 1), PASS * b + PACK * m0 : PASS * b + PACK * m1]
-            nc.sync.dma_start(wg_raw[b, a, m0][:], src.rearrange("(p i) c -> p i c", i=PACK))
+        def load_wu(b):
+            wu_raw[b] = held(f"wu_raw{b}", [P, 2, PASS], I32)
+            src = wu_words.rearrange("a p r i -> p a (r i)")[:, :, 4 * PASS * b : 4 * PASS * (b + 1)]
+            nc.sync.dma_start(wu_raw[b][:], src.bitcast(I32))
+
+        def load_wg(b, a):
+            wg_raw[b, a] = held(f"wg_raw{b}{a}", [P, PACK, PASS], F32)
+            src = wg[PASS * a : PASS * (a + 1), PASS * b : PASS * (b + 1)]
+            nc.sync.dma_start(wg_raw[b, a][:], src.rearrange("(p i) c -> p i c", i=PACK))
 
         def load_rows(queue, dst, scales):
-            queue.dma_start(dst.bitcast(I32), scales.rearrange("a q n -> (a q) n").bitcast(I32))
+            queue.dma_start(dst[STAGE:P, :].bitcast(I32), scales.rearrange("a q n -> (a q) n").bitcast(I32))
 
         def place_rows(a):
-            for r in range(4):
-                nc.sync.dma_start(planes[a][r:P:32, :].bitcast(I32), rows[LIVE + 16 * a + r : LIVE + 16 * (a + 1) : 4, :].bitcast(I32))
+            first = STAGE + ROWS * a
+            for s in range(4):
+                nc.sync.dma_start(planes[a][s:P:32, :].bitcast(I32), rows[first + s : first + ROWS : 4, :].bitcast(I32))
 
-        load_rows(nc.sync, table_planes[LIVE:P, :], tab_scales)
+        load_rows(nc.sync, table_rows, tab_scales)
         nc.sync.dma_start(offsets[:], offs)
-        load_rows(nc.scalar, wu_rows[LIVE:P, :], wu_scales)
-        load_rows(nc.scalar, rows[LIVE:P, WD4_AT:WD8_AT], wd4_scales)
-        load_rows(nc.scalar, rows[LIVE:P, WD8_AT:ROW], wd8_scales)
+        load_rows(nc.scalar, wu_rows, wu_scales)
         nc.sync.dma_start(table[:], tab_words[0].rearrange("p t e -> p (t e)").bitcast(I32))
-        load_wu(0, 0, 2)
+        load_wu(0)
 
         warm = held("warm", [P, 2], F32)
-        nc.gpsimd.memset(warm[:, 0:1], 0.0)
+        nc.vector.memset(warm[:, 0:1], 0.0)
         nc.scalar.activation(warm[:, 1:2], warm[:, 0:1], SILU)
 
         nc.vector.tensor_copy(
-            rows[:, WU_AT:WD4_AT].rearrange("p (b t g m) -> p b g t m", b=2, t=PACK, m=16),
+            rows[:, WU_AT:ROW].rearrange("p (b t g m) -> p b g t m", b=2, t=PACK, m=16),
             wu_rows[:].rearrange("p (b g m t) -> p b g t m", b=2, t=PACK, m=16),
         )
-        nc.vector.tensor_copy(picked_rows[:], table_planes[:].indirect(offsets[:]))
-        nc.vector.tensor_copy(rows[LIVE:P, 0:J].bitcast(I32), picked_rows[LIVE:P, :].bitcast(I32))
-        load_wg(0, 0, 0, P)
+        nc.vector.tensor_copy(picked_rows[:], table_rows[:].indirect(offsets[:]))
+        nc.vector.tensor_copy(rows[STAGE:P, 0:J].bitcast(I32), picked_rows[STAGE:P, :].bitcast(I32))
+
+        load_wg(0, 0)
         place_rows(0)
-        load_wg(0, 1, 0, P)
+        load_wg(0, 1)
         place_rows(1)
-        load_wg(1, 0, 0, P)
-        load_wg(1, 1, 0, P)
-        load_wu(1, 0, 2)
+        load_wg(1, 0)
+        load_wg(1, 1)
+        load_wu(1)
         nc.sync.dma_start(wd4[:].bitcast(I32), wd4_words.rearrange("a p w -> p a w").bitcast(I32))
         nc.sync.dma_start(wd8[:], wd8_words.rearrange("a p n i -> p a (n i)").bitcast(I32))
+        for tier, scales in enumerate((wd4_scales, wd8_scales)):
+            nc.sync.dma_start(wd_rows[P - ROWS : P, tier].bitcast(I32), scales.rearrange("a q n -> q a n").bitcast(I32))
         nc.sync.dma_start(resid[0][:], rT[0:P, :])
+        for s in range(4):
+            nc.sync.dma_start(wd_planes[s:P:32].bitcast(I32), wd_rows[P - ROWS + s : P : 4].bitcast(I32))
         nc.sync.dma_start(resid[1][:], rT[P : 2 * P, :])
 
-        def order_wu(b, a0, a1):
-            ordered = held(f"wu{b}{a0}", [P, a1 - a0, PASS], U32)
+        wu = {}
+
+        def order_wu(b):
+            wu[b] = held(f"wu{b}", [P, 2, PASS], U32)
             nc.vector.tensor_copy(
-                ordered[:].rearrange("p a (t g m) -> p a g t m", t=PACK, m=4),
-                wu_raw[b, 0][:, a0:a1, :].bitcast(U32).rearrange("p a (g m t) -> p a g t m", t=PACK, m=4),
+                wu[b][:].rearrange("p a (t g m) -> p a g t m", t=PACK, m=4),
+                wu_raw[b][:].bitcast(U32).rearrange("p a (g m t) -> p a g t m", t=PACK, m=4),
             )
-            for a in range(a0, a1):
-                wu[b, a] = ordered[:, a - a0, :]
 
         pairs = held("pairs", [P, J], U32)
         picked = [held(f"picked{a}", [P, J], U16) for a in range(2)]
+        wg_bf = {(b, a): held(f"wg_bf{b}{a}", [P, PACK * PASS], BF16) for b in range(2) for a in range(2)}
+        wg_codes, wg_planes = {}, {}
 
-        wg_bf, wg_codes, wg_planes = {}, {}, {}
-        span_bf = held("wg_bf1", [P, 2, PACK * PASS], BF16)
-        for a in range(2):
-            wg_bf[0, a] = held(f"wg_bf0{a}", [P, PACK * PASS], BF16)[:]
-            wg_bf[1, a] = span_bf[:, a, :]
+        def round_wg(b, a):
+            dst = wg_bf[b, a][:].rearrange("p (t m h i) -> p m h t i", t=PACK, h=2, i=2)
+            src = wg_raw[b, a][:].rearrange("p (h i) (m t) -> p m h t i", h=2, t=PACK)
+            on_gpsimd, on_scalar = ROUNDING[b, a]
+            vector_from = on_gpsimd + on_scalar
+            for m in range(0, on_gpsimd, GPSIMD_STEP):
+                nc.gpsimd.tensor_copy(dst[:, m : m + GPSIMD_STEP], src[:, m : m + GPSIMD_STEP])
+            for m in range(on_gpsimd, vector_from, SCALAR_STEP):
+                end = min(m + SCALAR_STEP, vector_from)
+                nc.scalar.copy(dst[:, m:end], src[:, m:end])
+            nc.vector.tensor_copy(dst[:, vector_from:P], src[:, vector_from:P])
 
-        def round_wg(b, a, piece, m0, m1, engine):
-            dst = wg_bf[b, a].rearrange("p (t m h i) -> p m h t i", t=PACK, h=2, i=2)[:, m0:m1]
-            src = wg_raw[b, a, piece][:].rearrange("p (h i) (m t) -> p m h t i", h=2, t=PACK)[:, m0 - piece : m1 - piece]
-            if engine is nc.scalar:
-                nc.scalar.copy(dst, src)
-            else:
-                engine.tensor_copy(dst, src)
+        def quantize_wg(b, a, after=""):
+            wg_codes[b, a] = held(f"wg_codes{b}{a}", [P, PASS], U32, after)
+            wg_planes[b, a] = held(f"wg_plane{b}{a}", [P, PASS], U8)
+            nc.vector.quantize_mx(out=wg_codes[b, a][:].bitcast(FP8X4), scales=wg_planes[b, a][:], in_=wg_bf[b, a][:])
 
-        def round_piece(b, a, piece, scalar_m, vector_m, gpsimd_m=0):
-            for m0 in range(piece, piece + gpsimd_m, 16):
-                round_wg(b, a, piece, m0, m0 + 16, nc.gpsimd)
-            start = piece + gpsimd_m
-            for m0 in range(start, start + scalar_m, 32):
-                round_wg(b, a, piece, m0, min(m0 + 32, start + scalar_m), nc.scalar)
-            if vector_m:
-                round_wg(b, a, piece, start + scalar_m, start + scalar_m + vector_m, nc.vector)
+        def first_stage(acc, codes, scales, t, cols, a, start, stop):
+            nc.tensor.matmul_mx(
+                acc,
+                lhsT=codes[:, t * P : (t + 1) * P].bitcast(FP8X4),
+                lhsT_scale=scales[:, t * P : (t + 1) * P],
+                rhs=picked[a][:, cols].bitcast(FP4X4),
+                rhs_scale=planes[a][:, cols],
+                start=start,
+                stop=stop,
+            )
 
-        def quantize_wg(b, a0, a1, src):
-            codes = held(f"wg_codes{b}{a0}", [P, (a1 - a0) * PASS], U32)
-            scales = held(f"wg_plane{b}{a0}", [P, (a1 - a0) * PASS], U8)
-            nc.vector.quantize_mx(out=codes[:].bitcast(FP8X4), scales=scales[:], in_=src)
-            for a in range(a0, a1):
-                cols = slice((a - a0) * PASS, (a - a0 + 1) * PASS)
-                wg_codes[b, a], wg_planes[b, a] = codes[:, cols], scales[:, cols]
-
-        def up_bank(g):
-            return banks[g % PER]
-
-        def gate_bank(g):
-            return banks[PER + (g % PER if g < 12 else g % 2)]
-
-        def first_stage(bank, codes, scales, c, a):
-            cols = slice(c * CH, (c + 1) * CH)
+        def chunk_pass(bank, codes, scales, g, a):
+            cols = slice(g % CHUNKS * CH, (g % CHUNKS + 1) * CH)
             for t in range(PACK):
-                nc.tensor.matmul_mx(
-                    bank[:, t * CH : (t + 1) * CH],
-                    lhsT=codes[:, t * P : (t + 1) * P].bitcast(FP8X4),
-                    lhsT_scale=scales[:, t * P : (t + 1) * P],
-                    rhs=picked[a][:, cols].bitcast(FP4X4),
-                    rhs_scale=planes[a][:, cols],
-                    start=(a == 0 and t == 0),
-                    stop=(a == 1 and t == PACK - 1),
-                )
+                acc = bank[:, t * CH : (t + 1) * CH]
+                first_stage(acc, codes, scales, t, cols, a, a == 0 and t == 0, a == 1 and t == PACK - 1)
 
         def up(g, a):
-            b, c = divmod(g, CHUNKS)
-            first_stage(up_bank(g), wu[b, a], planes[a][:, WU_AT + PASS * b : WU_AT + PASS * (b + 1)], c, a)
+            b = g // CHUNKS
+            chunk_pass(up_banks[g % PER], wu[b][:, a, :], planes[a][:, WU_AT + PASS * b : WU_AT + PASS * (b + 1)], g, a)
 
         def gate(g, a):
-            b, c = divmod(g, CHUNKS)
-            first_stage(gate_bank(g), wg_codes[b, a], wg_planes[b, a], c, a)
+            b = g // CHUNKS
+            chunk_pass(gate_banks[g % PER], wg_codes[b, a][:], wg_planes[b, a][:], g, a)
 
         h_bf, h_codes, h_planes = {}, {}, {}
-        for g0, count in ((0, 8), (8, 4), (12, 4)):
-            codes = held(f"h_codes{g0}", [P, count * CH], U32, "wg_bf1" if g0 == 0 else "")
-            scales = held(f"h_plane{g0}", [P, count * CH], U8)
-            whole = held(f"h_bf{g0}", [P, count * CH, PACK], BF16, "wg_raw100" if g0 == 0 else "")
-            for g in range(g0, g0 + count):
-                h_bf[g] = whole[:, (g - g0) * CH : (g - g0 + 1) * CH, :]
-                for part in range(1, g0 + count - g + 1):
-                    cols = slice((g - g0) * CH, (g - g0 + part) * CH)
-                    h_codes[g, part], h_planes[g, part], h_bf[g, part] = codes[:, cols], scales[:, cols], whole[:, cols, :]
+        for first, count in ((0, CHUNKS), (CHUNKS, PER), (CHUNKS + PER, PER)):
+            h_codes[first] = held(f"h_codes{first}", [P, count * CH], U32, "" if first else "wg_bf11")
+            h_planes[first] = held(f"h_plane{first}", [P, count * CH], U8)
+            h_bf[first] = held(f"h_bf{first}", [P, count * CH, PACK], BF16, "" if first else "wg_raw10")
 
-        acts = {}
+        def part_of(g):
+            return 0 if g < CHUNKS else g - g % PER
 
-        emptied = {}
+        def h_chunk(g):
+            at = (g - part_of(g)) * CH
+            return h_bf[part_of(g)][:, at : at + CH, :]
+
+        def by_entry(bank):
+            return bank[:].rearrange("p (t j) -> p j t", t=PACK)
+
+        acts, emptied = {}, {}
 
         def empty_bank(g):
             emptied[g] = held(f"ups{g}", [P, CH, PACK], F32)
-            nc.scalar.copy(emptied[g][:], up_bank(g)[:].rearrange("p (t j) -> p j t", t=PACK))
+            nc.scalar.copy(emptied[g][:], by_entry(up_banks[g % PER]))
 
-        def gated_product(g):
+        def chunk_silu(g):
             if g % PER == 0:
-                acts[g // PER] = held(f"act{g}", [P, PER, CH, PACK], F32, "wg_raw110" if g == PER else "")
+                acts[g // PER] = held(f"act{g // PER}", [P, PER, CH, PACK], F32, "wg_raw11" if g else "")
+            nc.scalar.activation(acts[g // PER][:, g % PER], by_entry(gate_banks[g % PER]), SILU)
+
+        def chunk_product(g):
             act = acts[g // PER][:, g % PER]
-            nc.scalar.activation(act, gate_bank(g)[:].rearrange("p (t j) -> p j t", t=PACK), SILU)
-            ups = up_bank(g)[:].rearrange("p (t j) -> p j t", t=PACK)
             if g % PER == 0:
-                if g:
-                    empty_bank(g)
-                nc.gpsimd.tensor_tensor(h_bf[g], emptied[g][:], act, MULT)
+                nc.gpsimd.tensor_tensor(h_chunk(g), emptied[g][:], act, MULT)
             else:
-                nc.vector.tensor_tensor(h_bf[g], ups, act, MULT)
+                nc.vector.tensor_tensor(h_chunk(g), by_entry(up_banks[g % PER]), act, MULT)
 
-        def quantize_h(piece):
-            nc.vector.quantize_mx(
-                out=h_codes[piece].bitcast(FP8X4), scales=h_planes[piece], in_=h_bf[piece].rearrange("p j t -> p (j t)")
-            )
-
-        def down(acc, n, b, key, first, last):
-            tiers = (
-                (wd4[:, b, 2 * n * P : 2 * (n + 1) * P].bitcast(FP4X4), planes[b][:, WD4_AT + n * P : WD4_AT + (n + 1) * P]),
-                (wd8[:, b, n * P : (n + 1) * P].bitcast(FP8X4), planes[b][:, WD8_AT + n * P : WD8_AT + (n + 1) * P]),
-            )
-            for tier, (lhsT, lhsT_scale) in enumerate(tiers):
-                nc.tensor.matmul_mx(
-                    acc,
-                    lhsT=lhsT,
-                    lhsT_scale=lhsT_scale,
-                    rhs=h_codes[key].bitcast(FP8X4),
-                    rhs_scale=h_planes[key],
-                    start=(first and tier == 0),
-                    stop=(last and tier == 1),
-                )
-
-        picked_resid = held("picked_resid", [P, HALF], F32)
-
-        def listed(half):
-            return offsets[:, half * HALF // 16 : (half + 1) * HALF // 16]
-
-        def finish(n, half, acc):
-            cols = slice(half * HALF, (half + 1) * HALF)
-            result = held(f"result{n}{half}", [P, HALF], F32, {(0, 0): "h_bf12", (0, 1): "sums11"}.get((n, half), ""))
-            if (n, half) == (0, 1):
-                nc.vector.tensor_tensor(result[:], acc, picked_resid[:], ADD)
-            else:
-                sums = held(f"sums{n}{half}", [P, HALF], F32)
-                nc.scalar.copy(sums[:], acc)
-                nc.vector.tensor_tensor(result[:], resid[n][:].indirect(listed(half)), sums[:], ADD)
-            nc.sync.dma_start(out[P * n : P * (n + 1), cols], result[:])
-
-        nc.vector.tensor_copy(pairs[:], table[:].bitcast(U32).indirect(offsets[:]))
-        order_wu(0, 0, 2)
-        for a in range(2):
-            nc.vector.tensor_copy(picked[a][:], pairs[:].bitcast(U16).rearrange("p (j a) -> p a j", a=2)[:, a, :])
-        for g in range(PER):
-            up(g, 0)
-        round_piece(0, 0, 0, 128, 0)
-        quantize_wg(0, 0, 1, wg_bf[0, 0])
-        for g in range(PER):
-            gate(g, 0)
-        round_piece(0, 1, 0, 80, 48)
-        quantize_wg(0, 1, 2, wg_bf[0, 1])
-        for g in range(PER):
-            up(g, 1)
-        empty_bank(0)
-
-        def wide_gate(g0):
-            b, half = divmod(g0 // PER, 2)
-            acts[g0 // PER] = held(f"act{g0}", [P, PACK, HALF], F32, "wg_raw110" if g0 == PER else "")
+        def wide_gate(u):
+            cols = slice(u % 2 * HALF, (u % 2 + 1) * HALF)
+            acts[u] = held(f"act{u}", [P, PACK, HALF], F32)
             for t in range(PACK):
                 for a in range(2):
-                    nc.tensor.matmul_mx(
-                        banks[PER + t][:],
-                        lhsT=wg_codes[b, a][:, t * P : (t + 1) * P].bitcast(FP8X4),
-                        lhsT_scale=wg_planes[b, a][:, t * P : (t + 1) * P],
-                        rhs=picked[a][:, half * HALF : (half + 1) * HALF].bitcast(FP4X4),
-                        rhs_scale=planes[a][:, half * HALF : (half + 1) * HALF],
-                        start=(a == 0),
-                        stop=(a == 1),
-                    )
-                nc.scalar.activation(acts[g0 // PER][:, t, :], banks[PER + t][:], SILU)
+                    first_stage(gate_banks[t][:], wg_codes[1, a], wg_planes[1, a], t, cols, a, a == 0, a == 1)
+                nc.scalar.activation(acts[u][:, t, :], gate_banks[t][:], SILU)
 
         def wide_product(g):
             act = acts[g // PER][:, :, g % PER * CH : (g % PER + 1) * CH]
             if g % PER == 0:
-                moved = held(f"ups{g}", [P, CH, PACK], F32)
-                nc.scalar.copy(moved[:], up_bank(g)[:].rearrange("p (t j) -> p j t", t=PACK))
-                nc.gpsimd.tensor_tensor(h_bf[g], moved[:], act.rearrange("p t j -> p j t"), MULT)
+                empty_bank(g)
+                nc.gpsimd.tensor_tensor(h_chunk(g), emptied[g][:], act.rearrange("p t j -> p j t"), MULT)
             else:
                 nc.vector.tensor_tensor(
-                    h_bf[g].rearrange("p (j e) t -> p j t e", e=2),
-                    up_bank(g)[:].rearrange("p (t j e) -> p j t e", t=PACK, e=2),
+                    h_chunk(g).rearrange("p (j e) t -> p j t e", e=2),
+                    up_banks[g % PER][:].rearrange("p (t j e) -> p j t e", t=PACK, e=2),
                     act.rearrange("p t (j e) -> p j t e", e=2),
                     MULT,
                 )
 
-        def chunk(g):
-            if g // PER in (2, 3,):
-                if g % PER == 0:
-                    wide_gate(g)
-                up(g, 0)
-                up(g, 1)
-                wide_product(g)
-                return
-            if g >= PER:
-                gate(g, 0)
+        def quantize_h(first):
+            nc.vector.quantize_mx(
+                out=h_codes[first][:].bitcast(FP8X4),
+                scales=h_planes[first][:],
+                in_=h_bf[first][:].rearrange("p j t -> p (j t)"),
+            )
+
+        def down(acc, n, b, half, start, stop):
+            g = CHUNKS * b + PER * half
+            cols = slice((g - part_of(g)) * CH, (g - part_of(g)) * CH + HALF)
+            tiers = (wd4[:, b, 2 * n * P : 2 * (n + 1) * P].bitcast(FP4X4), wd8[:, b, n * P : (n + 1) * P].bitcast(FP8X4))
+            for tier, words in enumerate(tiers):
+                nc.tensor.matmul_mx(
+                    acc,
+                    lhsT=words,
+                    lhsT_scale=wd_planes[:, tier, b, n * P : (n + 1) * P],
+                    rhs=h_codes[part_of(g)][:, cols].bitcast(FP8X4),
+                    rhs_scale=h_planes[part_of(g)][:, cols],
+                    start=(start and tier == 0),
+                    stop=(stop and tier == 1),
+                )
+
+        def listed(half):
+            return offsets[:, half * HALF // LISTED : (half + 1) * HALF // LISTED]
+
+        picked_resid = {}
+
+        def gather_resid(half, after=""):
+            picked_resid[half] = held(f"picked_resid{half}", [P, HALF], F32, after)
+            nc.vector.tensor_copy(picked_resid[half][:], resid[0][:].indirect(listed(half)))
+
+        def finish_gathering(half, acc, after=""):
+            result = held(f"result1{half}", [P, HALF], F32, after)
+            sums = held(f"sums{half}", [P, HALF], F32)
+            nc.scalar.copy(sums[:], acc)
+            nc.vector.tensor_tensor(result[:], resid[1][:].indirect(listed(half)), sums[:], ADD)
+            nc.sync.dma_start(out[P : 2 * P, half * HALF : (half + 1) * HALF], result[:])
+
+        def finish_plain(half, acc, parts, after=""):
+            result = held(f"result0{half}", [P, HALF], F32, after)
+            width = HALF // parts
+            for at in range(0, HALF, width):
+                cols = slice(at, at + width)
+                nc.vector.tensor_tensor(result[:, cols], acc[:, cols], picked_resid[half][:, cols], ADD)
+                nc.sync.dma_start(out[0:P, half * HALF + at : half * HALF + at + width], result[:, cols])
+
+        nc.vector.tensor_copy(pairs[:], table[:].bitcast(U32).indirect(offsets[:]))
+        order_wu(0)
+        for a in range(2):
+            nc.vector.tensor_copy(picked[a][:], pairs[:].bitcast(U16).rearrange("p (j a) -> p a j", a=2)[:, a, :])
+        for g in range(PER):
+            up(g, 0)
+        round_wg(0, 0)
+        quantize_wg(0, 0)
+        for g in range(PER):
+            gate(g, 0)
+        round_wg(0, 1)
+        quantize_wg(0, 1)
+        for g in range(PER):
+            up(g, 1)
+        empty_bank(0)
+        round_wg(1, 0)
+        for g in range(PER):
             gate(g, 1)
-            if g >= PER:
-                up(g, 0)
-                up(g, 1)
-            gated_product(g)
+            chunk_silu(g)
+            chunk_product(g)
 
-        round_piece(1, 0, 0, 0, 128, 0)
-        for g in range(4):
-            chunk(g)
-        round_piece(1, 1, 0, 96, 0, 32)
-        quantize_wg(1, 0, 2, span_bf[:].rearrange("p a c -> p (a c)"))
-        order_wu(1, 0, 2)
-        for g in range(4, CHUNKS):
-            chunk(g)
+        round_wg(1, 1)
+        quantize_wg(1, 0, after="act0")
+        quantize_wg(1, 1)
+        order_wu(1)
 
-        quantize_h((0, 8))
-        for g in range(8, 12):
-            chunk(g)
-        quantize_h((8, 4))
-        nc.vector.tensor_copy(picked_resid[:], resid[0][:].indirect(listed(1)))
-        for g in range(12, 16):
-            chunk(g)
-        quantize_h((12, 4))
+        for g in range(PER, CHUNKS):
+            for a in range(2):
+                gate(g, a)
+            for a in range(2):
+                up(g, a)
+            chunk_silu(g)
+            if g == PER:
+                empty_bank(g)
+            chunk_product(g)
+        quantize_h(0)
+
+        for u in (2, 3):
+            gather_resid(u % 2, after="h_bf8" if u == 3 else "")
+            wide_gate(u)
+            for g in range(PER * u, PER * (u + 1)):
+                for a in range(2):
+                    up(g, a)
+                wide_product(g)
+            quantize_h(PER * u)
+
         for half in range(2):
-            for turn, n in enumerate((half, 1 - half)):
-                acc = banks[PER + 2 * half + turn][:]
-                for step, b in enumerate((turn, 1 - turn)):
-                    down(acc, n, b, (8 * b + 4 * half, 4), step == 0, step == 1)
-                finish(n, half, acc)
+            acc = gate_banks[2 * half][:]
+            for b in (0, 1):
+                down(acc, 1, b, half, b == 0, b == 1)
+            finish_gathering(half, acc, after="" if half else "h_bf12")
+            acc = gate_banks[2 * half + 1][:]
+            for b in (1, 0):
+                down(acc, 0, b, half, b == 1, b == 0)
+            finish_plain(half, acc, parts=1 + half, after="sums1" if half else "")

@@ -29,7 +29,7 @@ LISTED = 16
 STAGE = P - 2 * ROWS
 WU_AT, ROW = J, J + R
 
-ROUNDING = {(0, 0): (0, 96), (0, 1): (0, 80), (1, 0): (0, 0), (1, 1): (32, 64)}
+ROUNDING = {(0, 0): (0, 64), (0, 1): (0, 48), (1, 0): (0, 0), (1, 1): (0, 0)}
 SCALAR_STEP = 32
 GPSIMD_STEP = 16
 
@@ -68,15 +68,17 @@ def tile_list_gmlpt_silu_res_resL_kernel(
 
         wu_raw, wg_raw = {}, {}
 
-        def load_wu(b):
-            wu_raw[b] = held(f"wu_raw{b}", [P, 2, PASS], I32)
-            src = wu_words.rearrange("a p r i -> p a (r i)")[:, :, 4 * PASS * b : 4 * PASS * (b + 1)]
-            nc.sync.dma_start(wu_raw[b][:], src.bitcast(I32))
+        def load_wu(b, passes):
+            tile = held(f"wu_raw{b}{passes.start}", [P, passes.stop - passes.start, PASS], I32)
+            src = wu_words.rearrange("a p r i -> p a (r i)")[:, passes, 4 * PASS * b : 4 * PASS * (b + 1)]
+            nc.sync.dma_start(tile[:], src.bitcast(I32))
+            wu_raw[b, passes.start] = tile
 
-        def load_wg(b, a):
-            wg_raw[b, a] = held(f"wg_raw{b}{a}", [P, PACK, PASS], F32)
-            src = wg[PASS * a : PASS * (a + 1), PASS * b : PASS * (b + 1)]
-            nc.sync.dma_start(wg_raw[b, a][:], src.rearrange("(p i) c -> p i c", i=PACK))
+        def load_wg(b, a, first=0, count=PACK):
+            if first == 0:
+                wg_raw[b, a] = held(f"wg_raw{b}{a}", [P, PACK, PASS], F32)
+            src = wg[PASS * a : PASS * (a + 1), PASS * b : PASS * (b + 1)].rearrange("(p i) c -> p i c", i=PACK)
+            nc.sync.dma_start(wg_raw[b, a][:, first : first + count, :], src[:, first : first + count, :])
 
         def load_rows(queue, dst, scales):
             queue.dma_start(dst[STAGE:P, :].bitcast(I32), scales.rearrange("a q n -> (a q) n").bitcast(I32))
@@ -90,7 +92,8 @@ def tile_list_gmlpt_silu_res_resL_kernel(
         nc.sync.dma_start(offsets[:], offs)
         load_rows(nc.scalar, wu_rows, wu_scales)
         nc.sync.dma_start(table[:], tab_words[0].rearrange("p t e -> p (t e)").bitcast(I32))
-        load_wu(0)
+        load_wu(0, slice(0, 1))
+        load_wu(0, slice(1, 2))
 
         warm = held("warm", [P, 2], F32)
         nc.vector.memset(warm[:, 0:1], 0.0)
@@ -103,13 +106,14 @@ def tile_list_gmlpt_silu_res_resL_kernel(
         nc.vector.tensor_copy(picked_rows[:], table_rows[:].indirect(offsets[:]))
         nc.vector.tensor_copy(rows[STAGE:P, 0:J].bitcast(I32), picked_rows[STAGE:P, :].bitcast(I32))
 
-        load_wg(0, 0)
+        load_wg(0, 0, 0, 2)
         place_rows(0)
+        load_wg(0, 0, 2, 2)
         load_wg(0, 1)
         place_rows(1)
         load_wg(1, 0)
         load_wg(1, 1)
-        load_wu(1)
+        load_wu(1, slice(0, 2))
         nc.sync.dma_start(wd4[:].bitcast(I32), wd4_words.rearrange("a p w -> p a w").bitcast(I32))
         nc.sync.dma_start(wd8[:], wd8_words.rearrange("a p n i -> p a (n i)").bitcast(I32))
         for tier, scales in enumerate((wd4_scales, wd8_scales)):
@@ -121,15 +125,27 @@ def tile_list_gmlpt_silu_res_resL_kernel(
 
         wu = {}
 
-        def order_wu(b):
-            wu[b] = held(f"wu{b}", [P, 2, PASS], U32)
-            nc.vector.tensor_copy(
-                wu[b][:].rearrange("p a (t g m) -> p a g t m", t=PACK, m=4),
-                wu_raw[b][:].bitcast(U32).rearrange("p a (g m t) -> p a g t m", t=PACK, m=4),
+        def order_wu(copy, b, first, count):
+            tile = held(f"wu{b}{first}", [P, count, PASS], U32)
+            copy(
+                tile[:].rearrange("p a (t g m) -> p a g t m", t=PACK, m=4),
+                wu_raw[b, first][:].bitcast(U32).rearrange("p a (g m t) -> p a g t m", t=PACK, m=4),
             )
+            for a in range(count):
+                wu[b, first + a] = tile[:, a, :]
 
-        pairs = held("pairs", [P, J], U32)
-        picked = [held(f"picked{a}", [P, J], U16) for a in range(2)]
+        picked = {}
+
+        def pick_words(half):
+            pairs = held(f"pairs{half}", [P, HALF], U32, "pairs")
+            entries = offsets[:, half * HALF // LISTED : (half + 1) * HALF // LISTED]
+            nc.vector.tensor_copy(pairs[:], table[:].bitcast(U32).indirect(entries))
+            return pairs
+
+        def part_words(pairs, half, a, after=""):
+            picked[half, a] = held(f"picked{half}{a}", [P, HALF], U16, after)
+            nc.vector.tensor_copy(picked[half, a][:], pairs[:].bitcast(U16).rearrange("p (j a) -> p a j", a=2)[:, a, :])
+
         wg_bf = {(b, a): held(f"wg_bf{b}{a}", [P, PACK * PASS], BF16) for b in range(2) for a in range(2)}
         wg_codes, wg_planes = {}, {}
 
@@ -155,7 +171,7 @@ def tile_list_gmlpt_silu_res_resL_kernel(
                 acc,
                 lhsT=codes[:, t * P : (t + 1) * P].bitcast(FP8X4),
                 lhsT_scale=scales[:, t * P : (t + 1) * P],
-                rhs=picked[a][:, cols].bitcast(FP4X4),
+                rhs=picked[cols.start // HALF, a][:, cols.start % HALF : (cols.stop - 1) % HALF + 1].bitcast(FP4X4),
                 rhs_scale=planes[a][:, cols],
                 start=start,
                 stop=stop,
@@ -169,20 +185,20 @@ def tile_list_gmlpt_silu_res_resL_kernel(
 
         def up(g, a):
             b = g // CHUNKS
-            chunk_pass(up_banks[g % PER], wu[b][:, a, :], planes[a][:, WU_AT + PASS * b : WU_AT + PASS * (b + 1)], g, a)
+            chunk_pass(up_banks[g % PER], wu[b, a], planes[a][:, WU_AT + PASS * b : WU_AT + PASS * (b + 1)], g, a)
 
         def gate(g, a):
             b = g // CHUNKS
             chunk_pass(gate_banks[g % PER], wg_codes[b, a][:], wg_planes[b, a][:], g, a)
 
         h_bf, h_codes, h_planes = {}, {}, {}
-        for first, count in ((0, CHUNKS), (CHUNKS, PER), (CHUNKS + PER, PER)):
-            h_codes[first] = held(f"h_codes{first}", [P, count * CH], U32, "" if first else "wg_bf11")
-            h_planes[first] = held(f"h_plane{first}", [P, count * CH], U8)
-            h_bf[first] = held(f"h_bf{first}", [P, count * CH, PACK], BF16, "" if first else "wg_raw10")
+        for first in range(0, 2 * CHUNKS, PER):
+            h_codes[first] = held(f"h_codes{first}", [P, HALF], U32)
+            h_planes[first] = held(f"h_plane{first}", [P, HALF], U8)
+            h_bf[first] = held(f"h_bf{first}", [P, HALF, PACK], BF16, {0: "wg_raw10", PER: "wg_bf11"}.get(first, ""))
 
         def part_of(g):
-            return 0 if g < CHUNKS else g - g % PER
+            return g - g % PER
 
         def h_chunk(g):
             at = (g - part_of(g)) * CH
@@ -199,7 +215,7 @@ def tile_list_gmlpt_silu_res_resL_kernel(
 
         def chunk_silu(g):
             if g % PER == 0:
-                acts[g // PER] = held(f"act{g // PER}", [P, PER, CH, PACK], F32, "wg_raw11" if g else "")
+                acts[g // PER] = held(f"act{g // PER}", [P, PER, CH, PACK], F32, "")
             nc.scalar.activation(acts[g // PER][:, g % PER], by_entry(gate_banks[g % PER]), SILU)
 
         def chunk_product(g):
@@ -214,7 +230,7 @@ def tile_list_gmlpt_silu_res_resL_kernel(
             acts[u] = held(f"act{u}", [P, PACK, HALF], F32)
             for t in range(PACK):
                 for a in range(2):
-                    first_stage(gate_banks[t][:], wg_codes[1, a], wg_planes[1, a], t, cols, a, a == 0, a == 1)
+                    first_stage(gate_banks[t][:], wg_codes[u // 2, a], wg_planes[u // 2, a], t, cols, a, a == 0, a == 1)
                 nc.scalar.activation(acts[u][:, t, :], gate_banks[t][:], SILU)
 
         def wide_product(g):
@@ -276,18 +292,21 @@ def tile_list_gmlpt_silu_res_resL_kernel(
                 nc.vector.tensor_tensor(result[:, cols], acc[:, cols], picked_resid[half][:, cols], ADD)
                 nc.sync.dma_start(out[0:P, half * HALF + at : half * HALF + at + width], result[:, cols])
 
-        nc.vector.tensor_copy(pairs[:], table[:].bitcast(U32).indirect(offsets[:]))
-        order_wu(0)
+        pairs = pick_words(0)
         for a in range(2):
-            nc.vector.tensor_copy(picked[a][:], pairs[:].bitcast(U16).rearrange("p (j a) -> p a j", a=2)[:, a, :])
+            part_words(pairs, 0, a)
+            order_wu(nc.scalar.copy, 0, a, 1)
+        pairs = pick_words(1)
         for g in range(PER):
             up(g, 0)
         round_wg(0, 0)
         quantize_wg(0, 0)
+        part_words(pairs, 1, 0, after="wg_bf00")
         for g in range(PER):
             gate(g, 0)
         round_wg(0, 1)
         quantize_wg(0, 1)
+        part_words(pairs, 1, 1, after="wg_bf01")
         for g in range(PER):
             up(g, 1)
         empty_bank(0)
@@ -300,18 +319,15 @@ def tile_list_gmlpt_silu_res_resL_kernel(
         round_wg(1, 1)
         quantize_wg(1, 0, after="act0")
         quantize_wg(1, 1)
-        order_wu(1)
 
+        wide_gate(1)
         for g in range(PER, CHUNKS):
             for a in range(2):
-                gate(g, a)
-            for a in range(2):
                 up(g, a)
-            chunk_silu(g)
-            if g == PER:
-                empty_bank(g)
-            chunk_product(g)
+            wide_product(g)
+        order_wu(nc.scalar.copy, 1, 0, 2)
         quantize_h(0)
+        quantize_h(PER)
 
         for u in (2, 3):
             gather_resid(u % 2, after="h_bf8" if u == 3 else "")

@@ -29,9 +29,8 @@ LISTED = 16
 STAGE = P - 2 * ROWS
 WU_AT, ROW = J, J + R
 
-ROUNDING = {(0, 0): (0, 64), (0, 1): (0, 48), (1, 0): (0, 0), (1, 1): (0, 0)}
-SCALAR_STEP = 32
-GPSIMD_STEP = 16
+PAIR = 2 * P * PACK
+ON_SCALAR = 80
 
 
 def tile_list_gmlpt_silu_res_resL_kernel(
@@ -74,11 +73,16 @@ def tile_list_gmlpt_silu_res_resL_kernel(
             nc.sync.dma_start(tile[:], src.bitcast(I32))
             wu_raw[b, passes.start] = tile
 
-        def load_wg(b, a, first=0, count=PACK):
+        def load_wg_half(b, a, c):
+            wg_raw[b, a, c] = held(f"wg_raw{b}{a}{c}", [P, PACK, PASS // 2], F32)
+            cols = slice(PASS * b + c * PASS // 2, PASS * b + (c + 1) * PASS // 2)
+            nc.sync.dma_start(wg_raw[b, a, c][:], wg[PASS * a : PASS * (a + 1), cols].rearrange("(p i) c -> p i c", i=PACK))
+
+        def load_wg(b, a, first=0, last=PACK):
             if first == 0:
                 wg_raw[b, a] = held(f"wg_raw{b}{a}", [P, PACK, PASS], F32)
             src = wg[PASS * a : PASS * (a + 1), PASS * b : PASS * (b + 1)].rearrange("(p i) c -> p i c", i=PACK)
-            nc.sync.dma_start(wg_raw[b, a][:, first : first + count, :], src[:, first : first + count, :])
+            nc.sync.dma_start(wg_raw[b, a][:, first:last, :], src[:, first:last, :])
 
         def load_rows(queue, dst, scales):
             queue.dma_start(dst[STAGE:P, :].bitcast(I32), scales.rearrange("a q n -> (a q) n").bitcast(I32))
@@ -93,7 +97,6 @@ def tile_list_gmlpt_silu_res_resL_kernel(
         load_rows(nc.scalar, wu_rows, wu_scales)
         nc.sync.dma_start(table[:], tab_words[0].rearrange("p t e -> p (t e)").bitcast(I32))
         load_wu(0, slice(0, 1))
-        load_wu(0, slice(1, 2))
 
         warm = held("warm", [P, 2], F32)
         nc.vector.memset(warm[:, 0:1], 0.0)
@@ -106,12 +109,14 @@ def tile_list_gmlpt_silu_res_resL_kernel(
         nc.vector.tensor_copy(picked_rows[:], table_rows[:].indirect(offsets[:]))
         nc.vector.tensor_copy(rows[STAGE:P, 0:J].bitcast(I32), picked_rows[STAGE:P, :].bitcast(I32))
 
-        load_wg(0, 0, 0, 2)
         place_rows(0)
-        load_wg(0, 0, 2, 2)
-        load_wg(0, 1)
+        load_wu(0, slice(1, 2))
+        load_wg(0, 0, 0, PACK - 1)
         place_rows(1)
-        load_wg(1, 0)
+        load_wg(0, 0, PACK - 1, PACK)
+        load_wg(0, 1)
+        load_wg_half(1, 0, 0)
+        load_wg_half(1, 0, 1)
         load_wg(1, 1)
         load_wu(1, slice(0, 2))
         nc.sync.dma_start(wd4[:].bitcast(I32), wd4_words.rearrange("a p w -> p a w").bitcast(I32))
@@ -134,114 +139,130 @@ def tile_list_gmlpt_silu_res_resL_kernel(
             for a in range(count):
                 wu[b, first + a] = tile[:, a, :]
 
-        picked = {}
+        picked = [held(f"picked{half}", [P, 2, HALF], U16) for half in range(2)]
 
-        def pick_words(half):
-            pairs = held(f"pairs{half}", [P, HALF], U32, "pairs")
-            entries = offsets[:, half * HALF // LISTED : (half + 1) * HALF // LISTED]
+        def pick_words(first, count):
+            pairs = held(f"pairs{first}", [P, count], U32, "pairs")
+            entries = offsets[:, first // LISTED : (first + count) // LISTED]
             nc.vector.tensor_copy(pairs[:], table[:].bitcast(U32).indirect(entries))
-            return pairs
+            at = first % HALF
+            nc.vector.tensor_copy(
+                picked[first // HALF][:, :, at : at + count], pairs[:].bitcast(U16).rearrange("p (j a) -> p a j", a=2)
+            )
 
-        def part_words(pairs, half, a, after=""):
-            picked[half, a] = held(f"picked{half}{a}", [P, HALF], U16, after)
-            nc.vector.tensor_copy(picked[half, a][:], pairs[:].bitcast(U16).rearrange("p (j a) -> p a j", a=2)[:, a, :])
+        h_bf = {0: held("h_bf0", [P, (PER + 1) * CH * PACK], BF16, "wg_raw101")}
+        wg_bf, wg_codes, wg_planes = {}, {}, {}
 
-        wg_bf = {(b, a): held(f"wg_bf{b}{a}", [P, PACK * PASS], BF16) for b in range(2) for a in range(2)}
-        wg_codes, wg_planes = {}, {}
+        def round_whole(b, a):
+            tile = held(f"wg_bf{b}{a}", [P, 2 * PAIR], BF16)
+            wg_bf[b, a] = tile[:]
+            for c in range(2):
+                nc.vector.tensor_copy(
+                    tile[:].rearrange("p (t m h i) -> p m h t i", t=PACK, h=2, i=2)[:, c * P // 2 : (c + 1) * P // 2],
+                    wg_raw[b, a, c][:].rearrange("p (h i) (m t) -> p m h t i", h=2, t=PACK),
+                )
 
-        def round_wg(b, a):
-            dst = wg_bf[b, a][:].rearrange("p (t m h i) -> p m h t i", t=PACK, h=2, i=2)
-            src = wg_raw[b, a][:].rearrange("p (h i) (m t) -> p m h t i", h=2, t=PACK)
-            on_gpsimd, on_scalar = ROUNDING[b, a]
-            vector_from = on_gpsimd + on_scalar
-            for m in range(0, on_gpsimd, GPSIMD_STEP):
-                nc.gpsimd.tensor_copy(dst[:, m : m + GPSIMD_STEP], src[:, m : m + GPSIMD_STEP])
-            for m in range(on_gpsimd, vector_from, SCALAR_STEP):
-                end = min(m + SCALAR_STEP, vector_from)
-                nc.scalar.copy(dst[:, m:end], src[:, m:end])
-            nc.vector.tensor_copy(dst[:, vector_from:P], src[:, vector_from:P])
+        def round_pair(copy, b, a, c, first=0, last=P):
+            if (b, a, c) not in wg_bf:
+                if (b, a, c) == (1, 1, 1):
+                    wg_bf[b, a, c] = h_bf[0][:, (PER - 1) * CH * PACK :]
+                else:
+                    wg_bf[b, a, c] = held(f"wg_bf{b}{a}{c}", [P, PAIR], BF16)[:]
+            dst = wg_bf[b, a, c].rearrange("p (e m i) -> p m i e", e=2, i=PACK)
+            src = wg_raw[b, a][:].rearrange("p i (m c e) -> p c m i e", c=2, e=2)[:, c]
+            copy(dst[:, first:last], src[:, first:last])
 
-        def quantize_wg(b, a, after=""):
-            wg_codes[b, a] = held(f"wg_codes{b}{a}", [P, PASS], U32, after)
-            wg_planes[b, a] = held(f"wg_plane{b}{a}", [P, PASS], U8)
-            nc.vector.quantize_mx(out=wg_codes[b, a][:].bitcast(FP8X4), scales=wg_planes[b, a][:], in_=wg_bf[b, a][:])
+        def quantize_wg(key, slots, after=""):
+            name = "".join(str(k) for k in key)
+            codes = held(f"wg_codes{name}", [P, len(slots) * P], U32, after)
+            plane = held(f"wg_plane{name}", [P, len(slots) * P], U8)
+            nc.vector.quantize_mx(out=codes[:].bitcast(FP8X4), scales=plane[:], in_=wg_bf[key])
+            for at, t in enumerate(slots):
+                wg_codes[key[0], key[1], t] = codes[:, at * P : (at + 1) * P]
+                wg_planes[key[0], key[1], t] = plane[:, at * P : (at + 1) * P]
 
-        def first_stage(acc, codes, scales, t, cols, a, start, stop):
+        def first_stage(acc, codes, scales, cols, a, start, stop):
             nc.tensor.matmul_mx(
                 acc,
-                lhsT=codes[:, t * P : (t + 1) * P].bitcast(FP8X4),
-                lhsT_scale=scales[:, t * P : (t + 1) * P],
-                rhs=picked[cols.start // HALF, a][:, cols.start % HALF : (cols.stop - 1) % HALF + 1].bitcast(FP4X4),
+                lhsT=codes.bitcast(FP8X4),
+                lhsT_scale=scales,
+                rhs=picked[cols.start // HALF][:, a, cols.start % HALF : (cols.stop - 1) % HALF + 1].bitcast(FP4X4),
                 rhs_scale=planes[a][:, cols],
                 start=start,
                 stop=stop,
             )
 
-        def chunk_pass(bank, codes, scales, g, a):
-            cols = slice(g % CHUNKS * CH, (g % CHUNKS + 1) * CH)
-            for t in range(PACK):
-                acc = bank[:, t * CH : (t + 1) * CH]
-                first_stage(acc, codes, scales, t, cols, a, a == 0 and t == 0, a == 1 and t == PACK - 1)
+        def up_bank(g):
+            return up_banks[(1, 3, 0, 2)[g % PER] if g // PER else g]
 
         def up(g, a):
             b = g // CHUNKS
-            chunk_pass(up_banks[g % PER], wu[b, a], planes[a][:, WU_AT + PASS * b : WU_AT + PASS * (b + 1)], g, a)
+            cols = slice(g % CHUNKS * CH, (g % CHUNKS + 1) * CH)
+            scales = planes[a][:, WU_AT + PASS * b : WU_AT + PASS * (b + 1)]
+            for t in range(PACK):
+                slot = slice(t * P, (t + 1) * P)
+                acc = up_bank(g)[:, t * CH : (t + 1) * CH]
+                first_stage(acc, wu[b, a][:, slot], scales[:, slot], cols, a, a == 0 and t == 0, a == 1 and t == PACK - 1)
 
-        def gate(g, a):
-            b = g // CHUNKS
-            chunk_pass(gate_banks[g % PER], wg_codes[b, a][:], wg_planes[b, a][:], g, a)
-
-        h_bf, h_codes, h_planes = {}, {}, {}
+        h_codes, h_planes = {}, {}
         for first in range(0, 2 * CHUNKS, PER):
             h_codes[first] = held(f"h_codes{first}", [P, HALF], U32)
             h_planes[first] = held(f"h_plane{first}", [P, HALF], U8)
-            h_bf[first] = held(f"h_bf{first}", [P, HALF, PACK], BF16, {0: "wg_raw10", PER: "wg_bf11"}.get(first, ""))
+            if first > PER:
+                h_bf[first] = held(f"h_bf{first}", [P, HALF * PACK], BF16)
 
         def part_of(g):
             return g - g % PER
 
         def h_chunk(g):
-            at = (g - part_of(g)) * CH
-            return h_bf[part_of(g)][:, at : at + CH, :]
+            at = (g - part_of(g)) * CH * PACK
+            return h_bf[part_of(g)][:, at : at + CH * PACK].rearrange("p (j t) -> p j t", t=PACK)
 
         def by_entry(bank):
             return bank[:].rearrange("p (t j) -> p j t", t=PACK)
 
         acts, emptied = {}, {}
 
-        def empty_bank(g):
-            emptied[g] = held(f"ups{g}", [P, CH, PACK], F32)
-            nc.scalar.copy(emptied[g][:], by_entry(up_banks[g % PER]))
+        def empty_bank(g, after=""):
+            emptied[g] = held(f"ups{g}", [P, CH, PACK], F32, after)
+            nc.scalar.copy(emptied[g][:], by_entry(up_bank(g)))
 
-        def chunk_silu(g):
-            if g % PER == 0:
-                acts[g // PER] = held(f"act{g // PER}", [P, PER, CH, PACK], F32, "")
-            nc.scalar.activation(acts[g // PER][:, g % PER], by_entry(gate_banks[g % PER]), SILU)
-
-        def chunk_product(g):
-            act = acts[g // PER][:, g % PER]
-            if g % PER == 0:
-                nc.gpsimd.tensor_tensor(h_chunk(g), emptied[g][:], act, MULT)
-            else:
-                nc.vector.tensor_tensor(h_chunk(g), by_entry(up_banks[g % PER]), act, MULT)
-
-        def wide_gate(u):
+        def gate_pass(u, t, a):
             cols = slice(u % 2 * HALF, (u % 2 + 1) * HALF)
-            acts[u] = held(f"act{u}", [P, PACK, HALF], F32)
-            for t in range(PACK):
-                for a in range(2):
-                    first_stage(gate_banks[t][:], wg_codes[u // 2, a], wg_planes[u // 2, a], t, cols, a, a == 0, a == 1)
+            first_stage(gate_banks[t][:], wg_codes[u // 2, a, t], wg_planes[u // 2, a, t], cols, a, a == 0, a == 1)
+            if a:
+                if t == 0:
+                    acts[u] = held(f"act{u}", [P, PACK, HALF], F32)
                 nc.scalar.activation(acts[u][:, t, :], gate_banks[t][:], SILU)
 
-        def wide_product(g):
-            act = acts[g // PER][:, :, g % PER * CH : (g % PER + 1) * CH]
-            if g % PER == 0:
-                empty_bank(g)
+        def pair_pass(c, quarter, a):
+            bank = gate_banks[2 * quarter + c]
+            cols = slice(quarter * HALF // 2, (quarter + 1) * HALF // 2)
+            for e in range(2):
+                acc = bank[:, e * HALF // 2 : (e + 1) * HALF // 2]
+                t = 2 * c + e
+                first_stage(acc, wg_codes[0, a, t], wg_planes[0, a, t], cols, a, a == 0 and e == 0, a == 1 and e == 1)
+            if a:
+                if c == 0:
+                    acts[0, quarter] = held(f"act0{quarter}", [P, PACK, HALF // 2], F32)
+                nc.scalar.activation(acts[0, quarter][:, 2 * c : 2 * c + 2, :], bank[:].rearrange("p (e j) -> p e j", e=2), SILU)
+
+        def wide_gate(u):
+            for t in range(PACK):
+                for a in range(2):
+                    gate_pass(u, t, a)
+
+        def product(g):
+            if g < PER:
+                act = acts[0, g // 2][:, :, g % 2 * CH : (g % 2 + 1) * CH]
+            else:
+                act = acts[g // PER][:, :, g % PER * CH : (g % PER + 1) * CH]
+            if g in emptied:
                 nc.gpsimd.tensor_tensor(h_chunk(g), emptied[g][:], act.rearrange("p t j -> p j t"), MULT)
             else:
                 nc.vector.tensor_tensor(
                     h_chunk(g).rearrange("p (j e) t -> p j t e", e=2),
-                    up_banks[g % PER][:].rearrange("p (t j e) -> p j t e", t=PACK, e=2),
+                    up_bank(g)[:].rearrange("p (t j e) -> p j t e", t=PACK, e=2),
                     act.rearrange("p t (j e) -> p j t e", e=2),
                     MULT,
                 )
@@ -250,7 +271,7 @@ def tile_list_gmlpt_silu_res_resL_kernel(
             nc.vector.quantize_mx(
                 out=h_codes[first][:].bitcast(FP8X4),
                 scales=h_planes[first][:],
-                in_=h_bf[first][:].rearrange("p j t -> p (j t)"),
+                in_=h_bf[first][:, 0 : HALF * PACK],
             )
 
         def down(acc, n, b, half, start, stop):
@@ -292,39 +313,45 @@ def tile_list_gmlpt_silu_res_resL_kernel(
                 nc.vector.tensor_tensor(result[:, cols], acc[:, cols], picked_resid[half][:, cols], ADD)
                 nc.sync.dma_start(out[0:P, half * HALF + at : half * HALF + at + width], result[:, cols])
 
-        pairs = pick_words(0)
+        pick_words(0, HALF // 2)
+        pick_words(HALF // 2, HALF // 2)
+        pick_words(HALF, HALF)
         for a in range(2):
-            part_words(pairs, 0, a)
             order_wu(nc.scalar.copy, 0, a, 1)
-        pairs = pick_words(1)
-        for g in range(PER):
-            up(g, 0)
-        round_wg(0, 0)
-        quantize_wg(0, 0)
-        part_words(pairs, 1, 0, after="wg_bf00")
-        for g in range(PER):
-            gate(g, 0)
-        round_wg(0, 1)
-        quantize_wg(0, 1)
-        part_words(pairs, 1, 1, after="wg_bf01")
-        for g in range(PER):
-            up(g, 1)
-        empty_bank(0)
-        round_wg(1, 0)
-        for g in range(PER):
-            gate(g, 1)
-            chunk_silu(g)
-            chunk_product(g)
-
-        round_wg(1, 1)
-        quantize_wg(1, 0, after="act0")
-        quantize_wg(1, 1)
+            for g in (1, 3, 0, 2) if a else range(PER):
+                up(g, a)
+        for a in range(2):
+            round_pair(nc.vector.tensor_copy, 0, a, 0)
+            if a:
+                round_pair(nc.vector.tensor_copy, 0, a, 1, ON_SCALAR, P)
+            round_pair(nc.scalar.copy, 0, a, 1, 0, ON_SCALAR if a else P)
+            if a == 0:
+                empty_bank(1, after="wg_raw00")
+                empty_bank(PER - 1)
+            for c in range(2):
+                quantize_wg((0, a, c), (2 * c, 2 * c + 1))
+                if a == 0:
+                    pair_pass(c, 0, a)
+                    pair_pass(c, 1, a)
+        round_whole(1, 0)
+        for quarter in range(2):
+            for c in range(2):
+                pair_pass(c, quarter, 1)
+        quantize_wg((1, 0), range(PACK))
+        for g in range(PER - 1):
+            product(g)
 
         wide_gate(1)
+        round_pair(nc.vector.tensor_copy, 1, 1, 0)
+        round_pair(nc.vector.tensor_copy, 1, 1, 1)
+        for c in range(2):
+            quantize_wg((1, 1, c), (2 * c, 2 * c + 1))
+        product(PER - 1)
+        h_bf[PER] = held("h_bf4", [P, HALF * PACK], BF16, "wg_bf110")
         for g in range(PER, CHUNKS):
             for a in range(2):
                 up(g, a)
-            wide_product(g)
+            product(g)
         order_wu(nc.scalar.copy, 1, 0, 2)
         quantize_h(0)
         quantize_h(PER)
@@ -335,7 +362,9 @@ def tile_list_gmlpt_silu_res_resL_kernel(
             for g in range(PER * u, PER * (u + 1)):
                 for a in range(2):
                     up(g, a)
-                wide_product(g)
+                if g % PER == 0:
+                    empty_bank(g)
+                product(g)
             quantize_h(PER * u)
 
         for half in range(2):

@@ -150,7 +150,7 @@ def tile_list_gmlpt_silu_res_resL_kernel(
                 picked[first // HALF][:, :, at : at + count], pairs[:].bitcast(U16).rearrange("p (j a) -> p a j", a=2)
             )
 
-        h_bf = {0: held("h_bf0", [P, (PER + 1) * CH * PACK], BF16, "wg_raw101")}
+        h_bf = {}
         wg_bf, wg_codes, wg_planes = {}, {}, {}
 
         def round_whole(b, a):
@@ -292,11 +292,7 @@ def tile_list_gmlpt_silu_res_resL_kernel(
         def listed(half):
             return offsets[:, half * HALF // LISTED : (half + 1) * HALF // LISTED]
 
-        picked_resid = {}
-
-        def gather_resid(half, after=""):
-            picked_resid[half] = held(f"picked_resid{half}", [P, HALF], F32, after)
-            nc.vector.tensor_copy(picked_resid[half][:], resid[0][:].indirect(listed(half)))
+        picked_resid = held("picked_resid", [P, J], F32)
 
         def finish_gathering(half, acc, after=""):
             result = held(f"result1{half}", [P, HALF], F32, after)
@@ -310,7 +306,7 @@ def tile_list_gmlpt_silu_res_resL_kernel(
             width = HALF // parts
             for at in range(0, HALF, width):
                 cols = slice(at, at + width)
-                nc.vector.tensor_tensor(result[:, cols], acc[:, cols], picked_resid[half][:, cols], ADD)
+                nc.vector.tensor_tensor(result[:, cols], acc[:, cols], picked_resid[:, half * HALF + at : half * HALF + at + width], ADD)
                 nc.sync.dma_start(out[0:P, half * HALF + at : half * HALF + at + width], result[:, cols])
 
         pick_words(0, HALF // 2)
@@ -338,6 +334,7 @@ def tile_list_gmlpt_silu_res_resL_kernel(
             for c in range(2):
                 pair_pass(c, quarter, 1)
         quantize_wg((1, 0), range(PACK))
+        h_bf[0] = held("h_bf0", [P, (PER + 1) * CH * PACK], BF16, "wg_bf10")
         for g in range(PER - 1):
             product(g)
 
@@ -357,7 +354,8 @@ def tile_list_gmlpt_silu_res_resL_kernel(
         quantize_h(PER)
 
         for u in (2, 3):
-            gather_resid(u % 2, after="h_bf8" if u == 3 else "")
+            if u == 3:
+                nc.vector.tensor_copy(picked_resid[:], resid[0][:].indirect(offsets[:]))
             wide_gate(u)
             for g in range(PER * u, PER * (u + 1)):
                 for a in range(2):

@@ -97,6 +97,7 @@ def tile_list_gmlpt_silu_res_resL_kernel(
         load_rows(nc.scalar, wu_rows, wu_scales)
         nc.sync.dma_start(table[:], tab_words[0].rearrange("p t e -> p (t e)").bitcast(I32))
         load_wu(0, slice(0, 1))
+        load_wu(0, slice(1, 2))
 
         warm = held("warm", [P, 2], F32)
         nc.vector.memset(warm[:, 0:1], 0.0)
@@ -110,7 +111,6 @@ def tile_list_gmlpt_silu_res_resL_kernel(
         nc.vector.tensor_copy(rows[STAGE:P, 0:J].bitcast(I32), picked_rows[STAGE:P, :].bitcast(I32))
 
         place_rows(0)
-        load_wu(0, slice(1, 2))
         load_wg(0, 0, 0, PACK - 1)
         place_rows(1)
         load_wg(0, 0, PACK - 1, PACK)
@@ -168,8 +168,8 @@ def tile_list_gmlpt_silu_res_resL_kernel(
                     wg_bf[b, a, c] = h_bf[0][:, (PER - 1) * CH * PACK :]
                 else:
                     wg_bf[b, a, c] = held(f"wg_bf{b}{a}{c}", [P, PAIR], BF16)[:]
-            dst = wg_bf[b, a, c].rearrange("p (e m i) -> p m i e", e=2, i=PACK)
-            src = wg_raw[b, a][:].rearrange("p i (m c e) -> p c m i e", c=2, e=2)[:, c]
+            dst = wg_bf[b, a, c].rearrange("p (e m h i) -> p m h e i", e=2, h=2, i=2)
+            src = wg_raw[b, a][:].rearrange("p (h i) (m c e) -> p c m h e i", h=2, c=2, e=2)[:, c]
             copy(dst[:, first:last], src[:, first:last])
 
         def quantize_wg(key, slots, after=""):

@@ -289,17 +289,19 @@ def tile_list_gmlpt_silu_res_resL_kernel(
                     stop=(stop and tier == 1),
                 )
 
-        def listed(half):
-            return offsets[:, half * HALF // LISTED : (half + 1) * HALF // LISTED]
-
         picked_resid = held("picked_resid", [P, J], F32)
 
-        def finish_gathering(half, acc, after=""):
+        def finish_gathering(half, acc, parts, after=""):
             result = held(f"result1{half}", [P, HALF], F32, after)
             sums = held(f"sums{half}", [P, HALF], F32)
             nc.scalar.copy(sums[:], acc)
-            nc.vector.tensor_tensor(result[:], resid[1][:].indirect(listed(half)), sums[:], ADD)
-            nc.sync.dma_start(out[P : 2 * P, half * HALF : (half + 1) * HALF], result[:])
+            width = HALF // parts
+            for at in range(0, HALF, width):
+                first = half * HALF + at
+                entries = offsets[:, first // LISTED : (first + width) // LISTED]
+                cols = slice(at, at + width)
+                nc.vector.tensor_tensor(result[:, cols], resid[1][:].indirect(entries), sums[:, cols], ADD)
+                nc.sync.dma_start(out[P : 2 * P, first : first + width], result[:, cols])
 
         def finish_plain(half, acc, parts, after=""):
             result = held(f"result0{half}", [P, HALF], F32, after)
@@ -369,8 +371,8 @@ def tile_list_gmlpt_silu_res_resL_kernel(
             acc = gate_banks[2 * half][:]
             for b in (0, 1):
                 down(acc, 1, b, half, b == 0, b == 1)
-            finish_gathering(half, acc, after="" if half else "h_bf12")
+            finish_gathering(half, acc, parts=1 + half, after="" if half else "act3")
             acc = gate_banks[2 * half + 1][:]
             for b in (1, 0):
                 down(acc, 0, b, half, b == 1, b == 0)
-            finish_plain(half, acc, parts=1 + half, after="sums1" if half else "")
+            finish_plain(half, acc, parts=1 + half, after="sums0" if half else "")

@@ -153,14 +153,13 @@ def tile_list_gmlpt_silu_res_resL_kernel(
         h_bf = {}
         wg_bf, wg_codes, wg_planes = {}, {}, {}
 
-        def round_whole(b, a):
-            tile = held(f"wg_bf{b}{a}", [P, 2 * PAIR], BF16)
-            wg_bf[b, a] = tile[:]
+        def round_half(b, a, half):
             for c in range(2):
-                nc.vector.tensor_copy(
-                    tile[:].rearrange("p (t m h i) -> p m h t i", t=PACK, h=2, i=2)[:, c * P // 2 : (c + 1) * P // 2],
-                    wg_raw[b, a, c][:].rearrange("p (h i) (m t) -> p m h t i", h=2, t=PACK),
-                )
+                if half == 0:
+                    wg_bf[b, a, c] = held(f"wg_bf{b}{a}{c}", [P, PAIR], BF16)[:]
+                dst = wg_bf[b, a, c].rearrange("p (e m h i) -> p m h e i", e=2, h=2, i=2)
+                src = wg_raw[b, a, half][:].rearrange("p (h i) (m c e) -> p c m h e i", h=2, c=2, e=2)[:, c]
+                nc.vector.tensor_copy(dst[:, half * P // 2 : (half + 1) * P // 2], src)
 
         def round_pair(copy, b, a, c, first=0, last=P):
             if (b, a, c) not in wg_bf:
@@ -193,7 +192,7 @@ def tile_list_gmlpt_silu_res_resL_kernel(
             )
 
         def up_bank(g):
-            return up_banks[(1, 3, 0, 2)[g % PER] if g // PER else g]
+            return up_banks[((0, 1, 2, 3), (1, 3, 0, 2), (3, 0, 1, 2), (3, 0, 1, 2))[g // PER][g % PER]]
 
         def up(g, a):
             b = g // CHUNKS
@@ -267,16 +266,18 @@ def tile_list_gmlpt_silu_res_resL_kernel(
                     MULT,
                 )
 
-        def quantize_h(first):
-            nc.vector.quantize_mx(
-                out=h_codes[first][:].bitcast(FP8X4),
-                scales=h_planes[first][:],
-                in_=h_bf[first][:, 0 : HALF * PACK],
-            )
+        def quantize_h(first, parts=1):
+            width = HALF // parts
+            for at in range(0, HALF, width):
+                nc.vector.quantize_mx(
+                    out=h_codes[first][:, at : at + width].bitcast(FP8X4),
+                    scales=h_planes[first][:, at : at + width],
+                    in_=h_bf[first][:, at * PACK : (at + width) * PACK],
+                )
 
-        def down(acc, n, b, half, start, stop):
-            g = CHUNKS * b + PER * half
-            cols = slice((g - part_of(g)) * CH, (g - part_of(g)) * CH + HALF)
+        def down(acc, n, b, first, width, start, stop):
+            g = CHUNKS * b + first // CH
+            cols = slice(first % HALF, first % HALF + width)
             tiers = (wd4[:, b, 2 * n * P : 2 * (n + 1) * P].bitcast(FP4X4), wd8[:, b, n * P : (n + 1) * P].bitcast(FP8X4))
             for tier, words in enumerate(tiers):
                 nc.tensor.matmul_mx(
@@ -291,17 +292,15 @@ def tile_list_gmlpt_silu_res_resL_kernel(
 
         picked_resid = held("picked_resid", [P, J], F32)
 
-        def finish_gathering(half, acc, parts, after=""):
-            result = held(f"result1{half}", [P, HALF], F32, after)
-            sums = held(f"sums{half}", [P, HALF], F32)
-            nc.scalar.copy(sums[:], acc)
-            width = HALF // parts
-            for at in range(0, HALF, width):
-                first = half * HALF + at
-                entries = offsets[:, first // LISTED : (first + width) // LISTED]
-                cols = slice(at, at + width)
-                nc.vector.tensor_tensor(result[:, cols], resid[1][:].indirect(entries), sums[:, cols], ADD)
-                nc.sync.dma_start(out[P : 2 * P, first : first + width], result[:, cols])
+        def gathering_sum(bank, first, width, after=""):
+            for b in (0, 1):
+                down(bank[:, 0:width], 1, b, first, width, b == 0, b == 1)
+            result = held(f"result1{first}", [P, width], F32, after)
+            sums = held(f"sums{first}", [P, width], F32)
+            nc.scalar.copy(sums[:], bank[:, 0:width])
+            entries = offsets[:, first // LISTED : (first + width) // LISTED]
+            nc.vector.tensor_tensor(result[:], resid[1][:].indirect(entries), sums[:], ADD)
+            nc.sync.dma_start(out[P : 2 * P, first : first + width], result[:])
 
         def finish_plain(half, acc, parts, after=""):
             result = held(f"result0{half}", [P, HALF], F32, after)
@@ -331,12 +330,14 @@ def tile_list_gmlpt_silu_res_resL_kernel(
                 if a == 0:
                     pair_pass(c, 0, a)
                     pair_pass(c, 1, a)
-        round_whole(1, 0)
+        round_half(1, 0, 0)
+        round_half(1, 0, 1)
         for quarter in range(2):
             for c in range(2):
                 pair_pass(c, quarter, 1)
-        quantize_wg((1, 0), range(PACK))
-        h_bf[0] = held("h_bf0", [P, (PER + 1) * CH * PACK], BF16, "wg_bf10")
+        for c in range(2):
+            quantize_wg((1, 0, c), (2 * c, 2 * c + 1))
+        h_bf[0] = held("h_bf0", [P, (PER + 1) * CH * PACK], BF16, "wg_bf100")
         for g in range(PER - 1):
             product(g)
 
@@ -359,20 +360,20 @@ def tile_list_gmlpt_silu_res_resL_kernel(
             if u == 3:
                 nc.vector.tensor_copy(picked_resid[:], resid[0][:].indirect(offsets[:]))
             wide_gate(u)
-            for g in range(PER * u, PER * (u + 1)):
+            for g in (PER * u + 2, PER * u, PER * u + 1, PER * u + 3):
                 for a in range(2):
                     up(g, a)
-                if g % PER == 0:
+                if g % PER == 2:
                     empty_bank(g)
                 product(g)
-            quantize_h(PER * u)
+            quantize_h(PER * u, parts=2)
 
-        for half in range(2):
-            acc = gate_banks[2 * half][:]
-            for b in (0, 1):
-                down(acc, 1, b, half, b == 0, b == 1)
-            finish_gathering(half, acc, parts=1 + half, after="" if half else "act3")
-            acc = gate_banks[2 * half + 1][:]
-            for b in (1, 0):
-                down(acc, 0, b, half, b == 1, b == 0)
-            finish_plain(half, acc, parts=1 + half, after="sums0" if half else "")
+        gathering_sum(gate_banks[0], 0, HALF, after="act3")
+        for b in (1, 0):
+            down(gate_banks[1][:], 0, b, 0, HALF, b == 1, b == 0)
+        finish_plain(0, gate_banks[1][:], parts=1)
+        gathering_sum(gate_banks[2], HALF, HALF // 2)
+        gathering_sum(up_bank(3 * PER + 2), HALF + HALF // 2, HALF // 2)
+        for b in (1, 0):
+            down(gate_banks[3][:], 0, b, HALF, HALF, b == 1, b == 0)
+        finish_plain(1, gate_banks[3][:], parts=2, after="sums0")

@@ -31,6 +31,7 @@ WU_AT, ROW = J, J + R
 
 PAIR = 2 * P * PACK
 ON_SCALAR = 80
+ON_GPSIMD = {1: 64, 3: CH, 10: 96, 14: 96}
 
 
 def tile_list_gmlpt_silu_res_resL_kernel(
@@ -223,8 +224,9 @@ def tile_list_gmlpt_silu_res_resL_kernel(
         acts, emptied = {}, {}
 
         def empty_bank(g, after=""):
-            emptied[g] = held(f"ups{g}", [P, CH, PACK], F32, after)
-            nc.scalar.copy(emptied[g][:], by_entry(up_bank(g)))
+            count = CH if g < PER else ON_GPSIMD[g]
+            emptied[g] = held(f"ups{g}", [P, count, PACK], F32, after)
+            nc.scalar.copy(emptied[g][:], by_entry(up_bank(g))[:, 0:count])
 
         def gate_pass(u, t, a):
             cols = slice(u % 2 * HALF, (u % 2 + 1) * HALF)
@@ -256,13 +258,19 @@ def tile_list_gmlpt_silu_res_resL_kernel(
                 act = acts[0, g // 2][:, :, g % 2 * CH : (g % 2 + 1) * CH]
             else:
                 act = acts[g // PER][:, :, g % PER * CH : (g % PER + 1) * CH]
-            if g in emptied:
-                nc.gpsimd.tensor_tensor(h_chunk(g), emptied[g][:], act.rearrange("p t j -> p j t"), MULT)
-            else:
+            count = ON_GPSIMD.get(g, 0)
+            if count:
+                shown = act.rearrange("p t j -> p j t")[:, 0:count]
+                nc.gpsimd.tensor_tensor(h_chunk(g)[:, 0:count], emptied[g][:, 0:count], shown, MULT)
+            if count < CH:
+                if count and g < PER:
+                    ups = emptied[g][:].rearrange("p (j e) t -> p j t e", e=2)
+                else:
+                    ups = up_bank(g)[:].rearrange("p (t j e) -> p j t e", t=PACK, e=2)
                 nc.vector.tensor_tensor(
-                    h_chunk(g).rearrange("p (j e) t -> p j t e", e=2),
-                    up_bank(g)[:].rearrange("p (t j e) -> p j t e", t=PACK, e=2),
-                    act.rearrange("p t (j e) -> p j t e", e=2),
+                    h_chunk(g).rearrange("p (j e) t -> p j t e", e=2)[:, count // 2 :],
+                    ups[:, count // 2 :],
+                    act.rearrange("p t (j e) -> p j t e", e=2)[:, count // 2 :],
                     MULT,
                 )
 

from contextlib import ExitStack

import concourse.mybir as mybir

K, R, N, T, J = 1024, 1024, 256, 4096, 1024
FLOPS = 2 * (2 * K * R * J + 2 * R * N * J)

F32 = mybir.dt.float32
BF16 = mybir.dt.bfloat16
I32 = mybir.dt.int32
U32 = mybir.dt.uint32
U16 = mybir.dt.uint16
U8 = mybir.dt.uint8
FP8X4 = mybir.dt.float8_e4m3fn_x4
FP4X4 = mybir.dt.float4_e2m1fn_x4
SILU = mybir.ActivationFunctionType.Silu
MULT = mybir.AluOpType.mult
ADD = mybir.AluOpType.add

P = 128
PACK = 4
PASS = P * PACK
CH = 128
CHUNKS = J // CH
HALF = J // 2
PER = HALF // CH
ROWS = 16
LISTED = 16
STAGE = P - 2 * ROWS
WU_AT, ROW = J, J + R

PAIR = 2 * P * PACK
ON_SCALAR = 80
ON_GPSIMD = {1: 64, 3: CH, 10: 96, 14: 96}


def tile_list_gmlpt_silu_res_resL_kernel(
    tc, tab_words, tab_scales, wg, wu_words, wu_scales, wd4_words, wd4_scales, wd8_words, wd8_scales, rT, offs, out
):
    nc = tc.nc
    with ExitStack() as ctx:
        keep = ctx.enter_context(tc.tile_pool(name="keep", bufs=1))
        psum = ctx.enter_context(tc.psum_pool(name="psum", bufs=1))

        def held(name, shape, dtype, after=""):
            return keep.tile(shape, dtype, name=name, tag=after or name, align_bytes=64)

        offsets = keep.tile([P, J // LISTED], U16, name="offsets")
        table = held("table", [P, T], I32)
        table_rows = held("table_rows", [P, T], U8)
        picked_rows = held("picked_rows", [P, J], U8)
        wu_rows = held("wu_rows", [P, R], U8)
        rows = held("rows", [P, ROW], U8)
        planes = [held(f"planes{a}", [P, ROW], U8) for a in range(2)]
        wd_rows = held("wd_rows", [P, 2, 2, N], U8)
        wd_planes = held("wd_planes", [P, 2, 2, N], U8)
        wd4 = held("wd4", [P, 2, 2 * N], U8)
        wd8 = held("wd8", [P, 2, N], I32)
        resid = [held(f"resid{n}", [P, T], F32) for n in range(2)]
        banks = [psum.tile([P, PACK * CH], F32, name=f"bank{i}") for i in range(2 * PER)]
        up_banks, gate_banks = banks[:PER], banks[PER:]

        nc.gpsimd.memset(table_rows[:].bitcast(I32)[0:STAGE, :], 0)
        nc.gpsimd.memset(wd_planes[:].bitcast(I32), 0)
        nc.vector.memset(wu_rows[0:STAGE, :].bitcast(I32), 0)
        for a in range(2):
            nc.vector.memset(planes[a][:].bitcast(I32), 0)

        wu_raw, wg_raw = {}, {}

        def load_wu(b, passes):
            tile = held(f"wu_raw{b}{passes.start}", [P, passes.stop - passes.start, PASS], I32)
            src = wu_words.rearrange("a p r i -> p a (r i)")[:, passes, 4 * PASS * b : 4 * PASS * (b + 1)]
            nc.sync.dma_start(tile[:], src.bitcast(I32))
            wu_raw[b, passes.start] = tile

        def load_wg_half(b, a, c):
            wg_raw[b, a, c] = held(f"wg_raw{b}{a}{c}", [P, PACK, PASS // 2], F32)
            cols = slice(PASS * b + c * PASS // 2, PASS * b + (c + 1) * PASS // 2)
            nc.sync.dma_start(wg_raw[b, a, c][:], wg[PASS * a : PASS * (a + 1), cols].rearrange("(p i) c -> p i c", i=PACK))

        def load_wg(b, a, first=0, last=PACK):
            if first == 0:
                wg_raw[b, a] = held(f"wg_raw{b}{a}", [P, PACK, PASS], F32)
            src = wg[PASS * a : PASS * (a + 1), PASS * b : PASS * (b + 1)].rearrange("(p i) c -> p i c", i=PACK)
            nc.sync.dma_start(wg_raw[b, a][:, first:last, :], src[:, first:last, :])

        def load_rows(queue, dst, scales):
            queue.dma_start(dst[STAGE:P, :].bitcast(I32), scales.rearrange("a q n -> (a q) n").bitcast(I32))

        def place_rows(a):
            first = STAGE + ROWS * a
            for s in range(4):
                nc.sync.dma_start(planes[a][s:P:32, :].bitcast(I32), rows[first + s : first + ROWS : 4, :].bitcast(I32))

        load_rows(nc.sync, table_rows, tab_scales)
        nc.sync.dma_start(offsets[:], offs)
        load_rows(nc.scalar, wu_rows, wu_scales)
        nc.sync.dma_start(table[:], tab_words[0].rearrange("p t e -> p (t e)").bitcast(I32))
        load_wu(0, slice(0, 1))
        load_wu(0, slice(1, 2))

        warm = held("warm", [P, 2], F32)
        nc.vector.memset(warm[:, 0:1], 0.0)
        nc.scalar.activation(warm[:, 1:2], warm[:, 0:1], SILU)

        nc.vector.tensor_copy(
            rows[:, WU_AT:ROW].rearrange("p (b t g m) -> p b g t m", b=2, t=PACK, m=16),
            wu_rows[:].rearrange("p (b g m t) -> p b g t m", b=2, t=PACK, m=16),
        )
        nc.vector.tensor_copy(picked_rows[:], table_rows[:].indirect(offsets[:]))
        nc.vector.tensor_copy(rows[STAGE:P, 0:J].bitcast(I32), picked_rows[STAGE:P, :].bitcast(I32))

        place_rows(0)
        load_wg(0, 0, 0, PACK - 1)
        place_rows(1)
        load_wg(0, 0, PACK - 1, PACK)
        load_wg(0, 1)
        load_wg_half(1, 0, 0)
        load_wg_half(1, 0, 1)
        load_wg(1, 1)
        load_wu(1, slice(0, 2))
        nc.sync.dma_start(wd4[:].bitcast(I32), wd4_words.rearrange("a p w -> p a w").bitcast(I32))
        nc.sync.dma_start(wd8[:], wd8_words.rearrange("a p n i -> p a (n i)").bitcast(I32))
        for tier, scales in enumerate((wd4_scales, wd8_scales)):
            nc.sync.dma_start(wd_rows[P - ROWS : P, tier].bitcast(I32), scales.rearrange("a q n -> q a n").bitcast(I32))
        nc.sync.dma_start(resid[0][:], rT[0:P, :])
        for s in range(4):
            nc.sync.dma_start(wd_planes[s:P:32].bitcast(I32), wd_rows[P - ROWS + s : P : 4].bitcast(I32))
        nc.sync.dma_start(resid[1][:], rT[P : 2 * P, :])

        wu = {}

        def order_wu(copy, b, first, count):
            tile = held(f"wu{b}{first}", [P, count, PASS], U32)
            copy(
                tile[:].rearrange("p a (t g m) -> p a g t m", t=PACK, m=4),
                wu_raw[b, first][:].bitcast(U32).rearrange("p a (g m t) -> p a g t m", t=PACK, m=4),
            )
            for a in range(count):
                wu[b, first + a] = tile[:, a, :]

        picked = [held(f"picked{half}", [P, 2, HALF], U16) for half in range(2)]

        def pick_words(first, count):
            pairs = held(f"pairs{first}", [P, count], U32, "pairs")
            entries = offsets[:, first // LISTED : (first + count) // LISTED]
            nc.vector.tensor_copy(pairs[:], table[:].bitcast(U32).indirect(entries))
            at = first % HALF
            nc.vector.tensor_copy(
                picked[first // HALF][:, :, at : at + count], pairs[:].bitcast(U16).rearrange("p (j a) -> p a j", a=2)
            )

        h_bf = {}
        wg_bf, wg_codes, wg_planes = {}, {}, {}

        def round_half(b, a, half):
            for c in range(2):
                if half == 0:
                    wg_bf[b, a, c] = held(f"wg_bf{b}{a}{c}", [P, PAIR], BF16)[:]
                dst = wg_bf[b, a, c].rearrange("p (e m h i) -> p m h e i", e=2, h=2, i=2)
                src = wg_raw[b, a, half][:].rearrange("p (h i) (m c e) -> p c m h e i", h=2, c=2, e=2)[:, c]
                nc.vector.tensor_copy(dst[:, half * P // 2 : (half + 1) * P // 2], src)

        def round_pair(copy, b, a, c, first=0, last=P):
            if (b, a, c) not in wg_bf:
                if (b, a, c) == (1, 1, 1):
                    wg_bf[b, a, c] = h_bf[0][:, (PER - 1) * CH * PACK :]
                else:
                    wg_bf[b, a, c] = held(f"wg_bf{b}{a}{c}", [P, PAIR], BF16)[:]
            dst = wg_bf[b, a, c].rearrange("p (e m h i) -> p m h e i", e=2, h=2, i=2)
            src = wg_raw[b, a][:].rearrange("p (h i) (m c e) -> p c m h e i", h=2, c=2, e=2)[:, c]
            copy(dst[:, first:last], src[:, first:last])

        def quantize_wg(key, slots, after=""):
            name = "".join(str(k) for k in key)
            codes = held(f"wg_codes{name}", [P, len(slots) * P], U32, after)
            plane = held(f"wg_plane{name}", [P, len(slots) * P], U8)
            nc.vector.quantize_mx(out=codes[:].bitcast(FP8X4), scales=plane[:], in_=wg_bf[key])
            for at, t in enumerate(slots):
                wg_codes[key[0], key[1], t] = codes[:, at * P : (at + 1) * P]
                wg_planes[key[0], key[1], t] = plane[:, at * P : (at + 1) * P]

        def first_stage(acc, codes, scales, cols, a, start, stop):
            nc.tensor.matmul_mx(
                acc,
                lhsT=codes.bitcast(FP8X4),
                lhsT_scale=scales,
                rhs=picked[cols.start // HALF][:, a, cols.start % HALF : (cols.stop - 1) % HALF + 1].bitcast(FP4X4),
                rhs_scale=planes[a][:, cols],
                start=start,
                stop=stop,
            )

        def up_bank(g):
            return up_banks[((0, 1, 2, 3), (1, 3, 0, 2), (3, 0, 1, 2), (3, 0, 1, 2))[g // PER][g % PER]]

        def up(g, a):
            b = g // CHUNKS
            cols = slice(g % CHUNKS * CH, (g % CHUNKS + 1) * CH)
            scales = planes[a][:, WU_AT + PASS * b : WU_AT + PASS * (b + 1)]
            for t in range(PACK):
                slot = slice(t * P, (t + 1) * P)
                acc = up_bank(g)[:, t * CH : (t + 1) * CH]
                first_stage(acc, wu[b, a][:, slot], scales[:, slot], cols, a, a == 0 and t == 0, a == 1 and t == PACK - 1)

        h_codes, h_planes = {}, {}
        for first in range(0, 2 * CHUNKS, PER):
            h_codes[first] = held(f"h_codes{first}", [P, HALF], U32)
            h_planes[first] = held(f"h_plane{first}", [P, HALF], U8)
            if first > PER:
                h_bf[first] = held(f"h_bf{first}", [P, HALF * PACK], BF16)

        def part_of(g):
            return g - g % PER

        def h_chunk(g):
            at = (g - part_of(g)) * CH * PACK
            return h_bf[part_of(g)][:, at : at + CH * PACK].rearrange("p (j t) -> p j t", t=PACK)

        def by_entry(bank):
            return bank[:].rearrange("p (t j) -> p j t", t=PACK)

        acts, emptied = {}, {}

        def empty_bank(g, after=""):
            count = CH if g < PER else ON_GPSIMD[g]
            emptied[g] = held(f"ups{g}", [P, count, PACK], F32, after)
            nc.scalar.copy(emptied[g][:], by_entry(up_bank(g))[:, 0:count])

        def gate_pass(u, t, a):
            cols = slice(u % 2 * HALF, (u % 2 + 1) * HALF)
            first_stage(gate_banks[t][:], wg_codes[u // 2, a, t], wg_planes[u // 2, a, t], cols, a, a == 0, a == 1)
            if a:
                if t == 0:
                    acts[u] = held(f"act{u}", [P, PACK, HALF], F32)
                nc.scalar.activation(acts[u][:, t, :], gate_banks[t][:], SILU)

        def pair_pass(c, quarter, a):
            bank = gate_banks[2 * quarter + c]
            cols = slice(quarter * HALF // 2, (quarter + 1) * HALF // 2)
            for e in range(2):
                acc = bank[:, e * HALF // 2 : (e + 1) * HALF // 2]
                t = 2 * c + e
                first_stage(acc, wg_codes[0, a, t], wg_planes[0, a, t], cols, a, a == 0 and e == 0, a == 1 and e == 1)
            if a:
                if c == 0:
                    acts[0, quarter] = held(f"act0{quarter}", [P, PACK, HALF // 2], F32)
                nc.scalar.activation(acts[0, quarter][:, 2 * c : 2 * c + 2, :], bank[:].rearrange("p (e j) -> p e j", e=2), SILU)

        def wide_gate(u):
            for t in range(PACK):
                for a in range(2):
                    gate_pass(u, t, a)

        def product(g):
            if g < PER:
                act = acts[0, g // 2][:, :, g % 2 * CH : (g % 2 + 1) * CH]
            else:
                act = acts[g // PER][:, :, g % PER * CH : (g % PER + 1) * CH]
            count = ON_GPSIMD.get(g, 0)
            if count:
                shown = act.rearrange("p t j -> p j t")[:, 0:count]
                nc.gpsimd.tensor_tensor(h_chunk(g)[:, 0:count], emptied[g][:, 0:count], shown, MULT)
            if count < CH:
                if count and g < PER:
                    ups = emptied[g][:].rearrange("p (j e) t -> p j t e", e=2)
                else:
                    ups = up_bank(g)[:].rearrange("p (t j e) -> p j t e", t=PACK, e=2)
                nc.vector.tensor_tensor(
                    h_chunk(g).rearrange("p (j e) t -> p j t e", e=2)[:, count // 2 :],
                    ups[:, count // 2 :],
                    act.rearrange("p t (j e) -> p j t e", e=2)[:, count // 2 :],
                    MULT,
                )

        def quantize_h(first, parts=1):
            width = HALF // parts
            for at in range(0, HALF, width):
                nc.vector.quantize_mx(
                    out=h_codes[first][:, at : at + width].bitcast(FP8X4),
                    scales=h_planes[first][:, at : at + width],
                    in_=h_bf[first][:, at * PACK : (at + width) * PACK],
                )

        def down(acc, n, b, first, width, start, stop):
            g = CHUNKS * b + first // CH
            cols = slice(first % HALF, first % HALF + width)
            tiers = (wd4[:, b, 2 * n * P : 2 * (n + 1) * P].bitcast(FP4X4), wd8[:, b, n * P : (n + 1) * P].bitcast(FP8X4))
            for tier, words in enumerate(tiers):
                nc.tensor.matmul_mx(
                    acc,
                    lhsT=words,
                    lhsT_scale=wd_planes[:, tier, b, n * P : (n + 1) * P],
                    rhs=h_codes[part_of(g)][:, cols].bitcast(FP8X4),
                    rhs_scale=h_planes[part_of(g)][:, cols],
                    start=(start and tier == 0),
                    stop=(stop and tier == 1),
                )

        picked_resid = held("picked_resid", [P, J], F32)

        def gathering_sum(bank, first, width, after=""):
            for b in (0, 1):
                down(bank[:, 0:width], 1, b, first, width, b == 0, b == 1)
            result = held(f"result1{first}", [P, width], F32, after)
            sums = held(f"sums{first}", [P, width], F32)
            nc.scalar.copy(sums[:], bank[:, 0:width])
            entries = offsets[:, first // LISTED : (first + width) // LISTED]
            nc.vector.tensor_tensor(result[:], resid[1][:].indirect(entries), sums[:], ADD)
            nc.sync.dma_start(out[P : 2 * P, first : first + width], result[:])

        def finish_plain(half, acc, parts, after=""):
            result = held(f"result0{half}", [P, HALF], F32, after)
            width = HALF // parts
            for at in range(0, HALF, width):
                cols = slice(at, at + width)
                nc.vector.tensor_tensor(result[:, cols], acc[:, cols], picked_resid[:, half * HALF + at : half * HALF + at + width], ADD)
                nc.sync.dma_start(out[0:P, half * HALF + at : half * HALF + at + width], result[:, cols])

        pick_words(0, HALF // 2)
        pick_words(HALF // 2, HALF // 2)
        pick_words(HALF, HALF)
        for a in range(2):
            order_wu(nc.scalar.copy, 0, a, 1)
            for g in (1, 3, 0, 2) if a else range(PER):
                up(g, a)
        for a in range(2):
            round_pair(nc.vector.tensor_copy, 0, a, 0)
            if a:
                round_pair(nc.vector.tensor_copy, 0, a, 1, ON_SCALAR, P)
            round_pair(nc.scalar.copy, 0, a, 1, 0, ON_SCALAR if a else P)
            if a == 0:
                empty_bank(1, after="wg_raw00")
                empty_bank(PER - 1)
            for c in range(2):
                quantize_wg((0, a, c), (2 * c, 2 * c + 1))
                if a == 0:
                    pair_pass(c, 0, a)
                    pair_pass(c, 1, a)
        round_half(1, 0, 0)
        round_half(1, 0, 1)
        for quarter in range(2):
            for c in range(2):
                pair_pass(c, quarter, 1)
        for c in range(2):
            quantize_wg((1, 0, c), (2 * c, 2 * c + 1))
        h_bf[0] = held("h_bf0", [P, (PER + 1) * CH * PACK], BF16, "wg_bf100")
        for g in range(PER - 1):
            product(g)

        wide_gate(1)
        round_pair(nc.vector.tensor_copy, 1, 1, 0)
        round_pair(nc.vector.tensor_copy, 1, 1, 1)
        for c in range(2):
            quantize_wg((1, 1, c), (2 * c, 2 * c + 1))
        product(PER - 1)
        h_bf[PER] = held("h_bf4", [P, HALF * PACK], BF16, "wg_bf110")
        for g in range(PER, CHUNKS):
            for a in range(2):
                up(g, a)
            product(g)
        order_wu(nc.scalar.copy, 1, 0, 2)
        quantize_h(0)
        quantize_h(PER)

        for u in (2, 3):
            if u == 3:
                nc.vector.tensor_copy(picked_resid[:], resid[0][:].indirect(offsets[:]))
            wide_gate(u)
            for g in (PER * u + 2, PER * u, PER * u + 1, PER * u + 3):
                for a in range(2):
                    up(g, a)
                if g % PER == 2:
                    empty_bank(g)
                product(g)
            quantize_h(PER * u, parts=2)

        gathering_sum(gate_banks[0], 0, HALF, after="act3")
        for b in (1, 0):
            down(gate_banks[1][:], 0, b, 0, HALF, b == 1, b == 0)
        finish_plain(0, gate_banks[1][:], parts=1)
        gathering_sum(gate_banks[2], HALF, HALF // 2)
        gathering_sum(up_bank(3 * PER + 2), HALF + HALF // 2, HALF // 2)
        for b in (1, 0):
            down(gate_banks[3][:], 0, b, HALF, HALF, b == 1, b == 0)
        finish_plain(1, gate_banks[3][:], parts=2, after="sums0")
